import numpy as np
import ml_dtypes


def mxq(x, axis, fmt="e4m3"):
    dtype, down = {"e4m3": (ml_dtypes.float8_e4m3fn, 7), "e5m2": (ml_dtypes.float8_e5m2, 14)}[fmt]
    v = np.moveaxis(np.asarray(x, np.float32).astype(ml_dtypes.bfloat16).astype(np.float64), axis, -1)
    blocks = v.reshape(v.shape[:-1] + (-1, 32))
    amax = np.abs(blocks).max(-1, keepdims=True)
    byte = np.maximum(np.where(amax > 0, np.frexp(amax)[1] - 1 + 127, 0) - down, 1)
    scale = np.exp2(byte - 127.0)
    codes = (blocks / scale).astype(np.float32).astype(dtype).astype(np.float64)
    return np.moveaxis((codes * scale).reshape(v.shape), -1, axis)


WIDE = False


def mx_kscale(k):
    if not WIDE:
        return np.ones(k)
    levels = np.array([10, -10, 5, -5, 0])
    if k % 512:
        return np.exp2(np.random.permutation(np.resize(levels, k // 32))).repeat(32)
    a = np.empty((k // 512, 16))
    for p in range(k // 512):
        a[p, :8] = np.random.permutation(np.resize(levels, 8))
        for g in range(8):
            far = levels[np.abs(levels - a[p, g]) >= 10]
            a[p, g + 8] = far[np.random.randint(len(far))]
    return np.exp2(a.ravel()).repeat(32)


def f64(x):
    return np.asarray(x).astype(np.float64)


def striped(idx):
    return np.tile(idx.reshape(-1, 16).T, (8, 1)).astype(np.uint16)


def unstriped(offs):
    return offs[:16].T.reshape(-1).astype(np.int64)


E2M1 = np.array([0.0, 0.5, 1.0, 1.5, 2.0, 3.0, 4.0, 6.0, -0.0, -0.5, -1.0, -1.5, -2.0, -3.0, -4.0, -6.0])


def pack_weight(w, fmt):
    k, n = w.shape
    w = f64(np.asarray(w, np.float32).astype(ml_dtypes.bfloat16)).reshape(k // 32, 32, n)
    amax = np.abs(w).max(1)
    if fmt == "e4m3":
        byte = np.frexp(amax)[1] - 1 + 127 - 7
    else:
        mant, ex = np.frexp(amax / 6.0)
        byte = np.where(mant > 0.5, ex, ex - 1) + 127
    byte = np.clip(np.where(amax > 0, byte, 1), 1, 254)
    scaled = (w * np.exp2(127.0 - byte)[:, None, :]).reshape(k, n).astype(np.float32)
    by_word = np.ascontiguousarray(scaled.reshape(k // 512, 128, 4, n).transpose(0, 1, 3, 2))
    if fmt == "e4m3":
        words = by_word.astype(ml_dtypes.float8_e4m3fn).view(np.uint8)
    else:
        c = by_word.astype(ml_dtypes.float4_e2m1fn).view(np.uint8) & 0xF
        words = (c[..., 0::2] | (c[..., 1::2] << 4)).reshape(k // 512, 128, 2 * n)
    return np.ascontiguousarray(words), np.ascontiguousarray(byte.astype(np.uint8).reshape(k // 512, 16, n))


def unpack_weight(words, scales, fmt):
    g, _, n = scales.shape
    words = np.ascontiguousarray(words).reshape(g, 128, n, -1)
    if fmt == "e4m3":
        vals = words.view(ml_dtypes.float8_e4m3fn).astype(np.float64)
    else:
        nib = np.empty((g, 128, n, 4), np.uint8)
        nib[..., 0::2] = words & 0xF
        nib[..., 1::2] = words >> 4
        vals = E2M1[nib]
    vals = vals * np.repeat(np.exp2(scales.astype(np.float64) - 127.0), 8, axis=1)[..., None]
    return vals.transpose(0, 1, 3, 2).reshape(g * 512, n)


def gelu(v):
    return 0.5 * v * (1.0 + np.tanh(np.sqrt(2.0 / np.pi) * (v + 0.044715 * v**3)))


def often(T, S):
    return np.random.permutation(T)[(T * np.random.uniform(0, 1, S) ** 4).astype(np.int64)]


K, K2, T, T2, S, H, N = 1024, 512, 2048, 1024, 512, 1024, 512


def setup_inputs():
    n = np.random.standard_normal
    s = mx_kscale(K)[:, None]
    s2 = mx_kscale(K2)[:, None]
    u = mx_kscale(H)[:, None]
    tab_words, tab_scales = pack_weight(n((K, T)) * s, "e4m3")
    tab2_words, tab2_scales = pack_weight(n((K2, T2)) * s2, "e2m1")
    w1_words, w1_scales = pack_weight(n((K, H)) / np.sqrt(K) / s, "e2m1")
    w4_words, w4_scales = pack_weight(1.5 * n((H, N)) / np.sqrt(H) / u, "e4m3")
    return {
        "tab_words": tab_words, "tab_scales": tab_scales,
        "tab2_words": tab2_words, "tab2_scales": tab2_scales,
        "offs": striped(often(T, S)),
        "offs2": striped(often(T2, S)),
        "w1_words": w1_words, "w1_scales": w1_scales,
        "w2": (1.3 * n((K2, H)) / np.sqrt(K2) / s2).astype(np.float32),
        "gh": (np.exp(0.3 * n(H)) * u[:, 0]).astype(np.float32),
        "gs": (np.exp(0.3 * n(H)) * u[:, 0]).astype(np.float32),
        "w3": (1.5 * n((H, N)) / np.sqrt(H) / u).astype(np.float32),
        "w4_words": w4_words, "w4_scales": w4_scales,
    }


def reference(tab_words, tab_scales, tab2_words, tab2_scales, offs, offs2, w1_words, w1_scales, w2, gh, gs, w3, w4_words, w4_scales):
    v = unpack_weight(tab_words, tab_scales, "e4m3")[:, unstriped(offs)]
    v2 = unpack_weight(tab2_words, tab2_scales, "e2m1")[:, unstriped(offs2)]
    b = unpack_weight(w1_words, w1_scales, "e2m1").T @ v
    d = mxq(f64(w2), 0, "e4m3").T @ v2
    h = 0.5 * b * (1.0 + np.tanh(np.sqrt(2.0 / np.pi) * (b + 0.044715 * b ** 3))) * f64(gh)[:, None]
    h2 = d / (1.0 + np.exp(-d)) * f64(gs)[:, None]
    hq = mxq(h, 0, "e4m3")
    h2q = mxq(h2, 0, "e4m3")
    y = mxq(f64(w3), 0, "e4m3").T @ hq + unpack_weight(w4_words, w4_scales, "e4m3").T @ h2q
    return 1.0 / (1.0 + np.exp(-y))

@@ -1,0 +1,354 @@
+from contextlib import ExitStack
+
+import concourse.mybir as mybir
+from concourse.masks import make_identity
+
+K, K2, T, T2, S, H, N = 1024, 512, 2048, 1024, 512, 1024, 512
+FLOPS = 2 * S * (K * H + K2 * H + 2 * H * N)
+
+F32 = mybir.dt.float32
+BF16 = mybir.dt.bfloat16
+I32 = mybir.dt.int32
+U32 = mybir.dt.uint32
+U16 = mybir.dt.uint16
+U8 = mybir.dt.uint8
+FP8X4 = mybir.dt.float8_e4m3fn_x4
+FP4X4 = mybir.dt.float4_e2m1fn_x4
+ACT = mybir.ActivationFunctionType
+MULT = mybir.AluOpType.mult
+ADD = mybir.AluOpType.add
+
+P = 128
+PACK = 4
+PASS = P * PACK
+QUADS = 4
+SQ = 128
+NQ = S // SQ
+GS_ROW = 64
+
+
+def tile_list_parking_occupancy_kernel(
+    tc, tab_words, tab_scales, tab2_words, tab2_scales, offs, offs2,
+    w1_words, w1_scales, w2, gh, gs, w3, w4_words, w4_scales, out,
+):
+    nc = tc.nc
+    with ExitStack() as ctx:
+        keep = ctx.enter_context(tc.tile_pool(name="keep", bufs=1))
+        reuse = ctx.enter_context(tc.tile_pool(name="reuse", bufs=1))
+        held = ctx.enter_context(tc.psum_pool(name="held", bufs=1))
+
+        def sb(shape, dtype, name, tag=None):
+            return keep.tile(shape, dtype, name=name, tag=tag or name, align_bytes=64)
+
+        def over(shape, dtype, name, offset):
+            return reuse.tile(shape, dtype, name=name, align_bytes=64, offset=offset)
+
+        def load_scales(queue, plane, scales):
+            rows = scales.bitcast(I32)
+            for quad in range(QUADS):
+                queue.dma_start(
+                    out=plane[:].bitcast(I32)[32 * quad : 32 * quad + 4],
+                    in_=rows[:, 4 * quad : 4 * quad + 4, :].rearrange("a r c -> r a c"),
+                )
+
+        def load_packed_scales(queue, plane, scales, row):
+            rows = scales.bitcast(I32)
+            for quad in range(QUADS):
+                queue.dma_start(
+                    out=plane[:].bitcast(I32)[32 * quad + row : 32 * quad + row + 8],
+                    in_=rows[:, 4 * quad : 4 * quad + 4, :],
+                )
+
+        list1 = keep.tile([P, S // 16], U16, name="list1")
+        list2 = keep.tile([P, S // 16], U16, name="list2")
+        t2_words = sb([P, T2], U16, "t2_words")
+        t2_plane = sb([P, 1, T2], U8, "t2_plane")
+        t1_words = [sb([P, T], U32, "t1_words0"), over([P, T], U32, "t1_words1", 16384)]
+        t1_plane = sb([P, 2, T], U8, "t1_plane")
+        w1_raw = sb([P, 2, H // 2], I32, "w1_raw")
+        w1_raw_plane = sb([P, 2, H], U8, "w1_raw_plane")
+        w4_codes = sb([P, 2, N], U32, "w4_codes")
+        w4_plane = sb([P, N], U8, "w4_plane")
+        w2_raw = [[sb([P, PACK, 256], F32, "w2_raw%d%d" % (a, u)) for u in range(2)] for a in range(1)]
+        w2_late = sb([P, PACK, PASS], F32, "w2_late")
+        w2_raw.append([w2_late[:, :, 0:256], w2_late[:, :, 256:512]])
+        w3_raw = [sb([P, PACK, N], F32, "w3_raw%d" % a) for a in range(2)]
+        gain_rows = [sb([P, PASS], F32, "gain_rows%d" % i) for i in range(2)]
+
+        nc.gpsimd.memset(t2_plane[:].bitcast(I32), 0)
+        nc.vector.memset(t1_plane[:].bitcast(I32), 0)
+        warm = sb([P, 8], F32, "warm")
+        nc.gpsimd.memset(warm[:], 0.0)
+        nc.scalar.activation(warm[:, 4:5], warm[:, 0:1], ACT.Silu)
+        gain_slots = [None, sb([P, PACK, P], F32, "gain_slots1")]
+        nc.gpsimd.memset(gain_slots[1][:], 0.0)
+        nc.gpsimd.memset(w1_raw_plane[:].bitcast(I32), 0)
+        nc.gpsimd.memset(w4_plane[:].bitcast(I32), 0)
+        identity = sb([P, P], F32, "identity")
+        make_identity(nc, identity[:])
+
+        w2_rows = w2.rearrange("(p j) c -> p j c", j=PACK)
+
+        def load_w2(a, u):
+            c0 = PASS * a + 256 * u
+            nc.sync.dma_start(out=w2_raw[a][u][:], in_=w2_rows[:, :, c0 : c0 + 256])
+
+        def load_t1(a):
+            nc.sync.dma_start(
+                out=t1_words[a][:].bitcast(I32),
+                in_=tab_words[a].rearrange("p t i -> p (t i)").bitcast(I32),
+            )
+
+        def load_w3(a):
+            rows = w3[PASS * a : PASS * (a + 1), :].rearrange("(g t e) n -> e g t n", t=PACK, e=4)
+            for e in range(4):
+                nc.sync.dma_start(out=w3_raw[a][e:P:4], in_=rows[e])
+
+        nc.sync.dma_start(out=t2_words[:].bitcast(I32), in_=tab2_words[0].bitcast(I32))
+        nc.sync.dma_start(list2[:], offs2)
+        load_scales(nc.sync, t2_plane, tab2_scales)
+        load_w2(0, 0)
+        load_w2(0, 1)
+        nc.sync.dma_start(out=gain_rows[1][0:2], in_=gs.rearrange("(a c) -> a c", a=2))
+        nc.sync.dma_start(out=w2_late[:], in_=w2_rows[:, :, PASS : 2 * PASS])
+        nc.sync.dma_start(list1[:], offs)
+        load_scales(nc.sync, t1_plane, tab_scales)
+        load_t1(0)
+
+        v2_codes = sb([P, S], U16, "v2_codes")
+        v2_plane = sb([P, S], U8, "v2_plane")
+        nc.vector.tensor_copy(v2_codes[:], t2_words[:].indirect(list2[:]))
+        nc.vector.tensor_copy(v2_plane[:], t2_plane[:, 0, :].indirect(list2[:]))
+
+        nc.sync.dma_start(out=w1_raw[:], in_=w1_words.bitcast(I32).rearrange("a p c -> p a c"))
+        load_scales(nc.sync, w1_raw_plane, w1_scales)
+        nc.sync.dma_start(out=gain_rows[0][0:2], in_=gh.rearrange("(a c) -> a c", a=2))
+        load_t1(1)
+        load_w3(0)
+        load_w3(1)
+        nc.sync.dma_start(
+            out=w4_codes[:].bitcast(I32),
+            in_=w4_words.rearrange("a p c i -> p a (c i)").bitcast(I32),
+        )
+        load_packed_scales(nc.sync, w4_plane, w4_scales, 4)
+
+        w2_bf = [over([P, PACK, P, PACK], BF16, "w2_bf%d" % a, 4096 * a) for a in range(2)]
+        w2_codes = [sb([P, PASS], U32, "w2_codes%d" % a) for a in range(2)]
+        w2_plane = [sb([P, PASS], U8, "w2_plane%d" % a) for a in range(2)]
+        w3_codes = [sb([P, N], U32, "w3_codes%d" % a) for a in range(2)]
+        w3_plane = [sb([P, N], U8, "w3_plane%d" % a) for a in range(2)]
+
+        def pool_round(dst, src):
+            nc.gpsimd.tensor_scalar(dst, src, 1.0, 0.0, MULT, ADD)
+
+        def round_w2(a, u, m0, m1, rounder):
+            rounder(
+                w2_bf[a][:, :, 64 * u + m0 : 64 * u + m1, :].rearrange("p t m j -> p m t j"),
+                w2_raw[a][u][:, :, PACK * m0 : PACK * m1].rearrange("p j (m t) -> p m t j", t=PACK),
+            )
+
+        def quantize(codes, plane, values):
+            nc.vector.quantize_mx(out=codes.bitcast(FP8X4), scales=plane, in_=values)
+
+        def quantize_w2(a):
+            quantize(w2_codes[a][:], w2_plane[a][:], w2_bf[a][:].rearrange("p t m j -> p (t m j)"))
+
+        def round_w3(a, n0, n1, rounder):
+            rounder(w3_bf[a][:, n0:n1, :], w3_raw[a][:, :, n0:n1].rearrange("p t n -> p n t"))
+
+        def quantize_w3(a):
+            quantize(w3_codes[a][:], w3_plane[a][:], w3_bf[a][:].rearrange("p n t -> p (n t)"))
+
+        round_w2(0, 0, 0, 64, nc.scalar.copy)
+        round_w2(0, 1, 0, 24, nc.scalar.copy)
+        round_w2(0, 1, 24, 64, nc.vector.tensor_copy)
+        gains = [held.tile([P, P, PACK], F32, name="gains%d" % i, tag="gains%d" % i) for i in range(2)]
+
+        def spread_gains(i):
+            for t in range(PACK):
+                nc.tensor.transpose(gains[i][:, :, t], gain_slots[i][:, t, :], identity[:])
+
+        nc.scalar.copy(
+            out=gain_slots[1][0:2],
+            in_=gain_rows[1][0:2].rearrange("p (m t) -> p t m", t=PACK),
+        )
+        spread_gains(1)
+        quantize_w2(0)
+        v1_plane = [over([P, S], U8, "v1_plane%d" % a, S * a) for a in range(2)]
+        for a in range(2):
+            nc.vector.tensor_copy(v1_plane[a][:], t1_plane[:, a, :].indirect(list1[:]))
+        for u in range(2):
+            for m0 in (0, 32):
+                round_w2(1, u, m0, m0 + 32, pool_round)
+
+        h2_act = [over([P, S * PACK], F32, "h2_act0", 8192), sb([P, S * PACK], F32, "h2_act1")]
+
+        def sweep_act(a, q0, q1):
+            return h2_act[a][:, PASS * q0 : PASS * q1]
+
+        h2_plane = [sb([P, S], U8, "h2_plane%d" % a) for a in range(2)]
+
+        def activate(dst, bank, func):
+            nc.scalar.activation(
+                dst.rearrange("p (s t) -> p s t", t=PACK), bank[:].rearrange("p t s -> p s t"), func
+            )
+
+        def apply_gain(dst, src, branch, row):
+            width = src.shape[1] // PACK
+            nc.vector.tensor_tensor(
+                dst.rearrange("p (s t) -> p s t", t=PACK),
+                src.rearrange("p (s t) -> p s t", t=PACK),
+                gains[branch][:, row : row + 1, :].to_broadcast([P, width, PACK]),
+                MULT,
+            )
+
+        def sweep_unit(a, q):
+            bank = held.tile([P, PACK, SQ], F32, name="sweep%d%d" % (a, q), tag="bank%d" % ((NQ * a + q) % 3))
+            cols = slice(SQ * q, SQ * (q + 1))
+            for t in range(PACK):
+                chan = slice(P * t, P * (t + 1))
+                nc.tensor.matmul_mx(
+                    out=bank[:, t, :],
+                    lhsT=w2_codes[a][:, chan].bitcast(FP8X4), lhsT_scale=w2_plane[a][:, chan],
+                    rhs=v2_codes[:, cols].bitcast(FP4X4), rhs_scale=v2_plane[:, cols],
+                    start=True, stop=True,
+                )
+            activate(sweep_act(a, q, q + 1), bank, ACT.Silu)
+
+        def sweep_gain(a, q0, q1, dst):
+            apply_gain(dst, sweep_act(a, q0, q1), 1, a)
+
+
+        for q in range(NQ):
+            sweep_unit(0, q)
+        h2_first = sb([P, 2 * PASS], BF16, "h2_first")
+        sweep_gain(0, 0, 1, h2_first[:, 0:PASS])
+        sweep_gain(0, 1, 2, h2_first[:, PASS : 2 * PASS])
+        quantize_w2(1)
+        h2_second = over([P, 2 * PASS], BF16, "h2_second", 4096)
+        sweep_gain(0, 2, 4, h2_second[:])
+        v1_codes = [over([P, S], U32, "v1_codes0", 4096 + 2048), over([P, S], U32, "v1_codes1", 8192 + 6144)]
+        w1_codes = over([P, 2 * 2 * H], U8, "w1_codes", 8192)
+        w1_plane = over([P, 2 * H], U8, "w1_plane", 8192 + 4096)
+        for q in range(NQ):
+            sweep_unit(1, q)
+        nc.vector.tensor_copy(v1_codes[0][:], t1_words[0][:].indirect(list1[:]))
+        nc.vector.tensor_copy(
+            w1_codes[:].bitcast(I32).rearrange("p (x t g w) -> p x g t w", t=PACK, g=32, w=2),
+            w1_raw[:].rearrange("p a (b g t w) -> p (a b) g t w", t=PACK, g=32, w=2),
+        )
+        nc.vector.tensor_copy(
+            w1_plane[:].bitcast(I32).rearrange("p (x t g) -> p x g t", t=PACK, g=32),
+            w1_raw_plane[:].bitcast(I32).rearrange("p a (b g t) -> p (a b) g t", t=PACK, g=32),
+        )
+        nc.vector.tensor_copy(v1_codes[1][:], t1_words[1][:].indirect(list1[:]))
+        gain_slots[0] = sb([P, PACK, P], F32, "gain_slots0", "w2_late")
+        nc.gpsimd.memset(gain_slots[0][:], 0.0)
+        pool_round(
+            gain_slots[0][0:2].rearrange("p t (g e) -> p t g e", e=4),
+            gain_rows[0][0:2].rearrange("p (g t e) -> p t g e", t=PACK, e=4),
+        )
+        spread_gains(0)
+        h2_third = over([P, S * PACK], BF16, "h2_third", 16384)
+        h2_codes = [over([P, S], U32, "h2_codes0", 16384 + 4096), sb([P, S], U32, "h2_codes1")]
+        sweep_gain(1, 0, 4, h2_third[:])
+        quantize(h2_codes[0][:, 0:256], h2_plane[0][:, 0:256], h2_first[:])
+        quantize(h2_codes[0][:, 256:512], h2_plane[0][:, 256:512], h2_second[:])
+        quantize(h2_codes[1][:], h2_plane[1][:], h2_third[:])
+        w3_bf = [sb([P, N, PACK], BF16, "w3_bf0"), sb([P, N, PACK], BF16, "w3_bf1", "h2_act1")]
+        for n0 in range(0, N, 128):
+            round_w3(0, n0, n0 + 128, pool_round)
+        for n0 in range(0, N // 2, 128):
+            round_w3(1, n0, n0 + 128, pool_round)
+
+        h_act = [sb([P, 2, PASS], F32, "h_act%d" % q) for q in range(NQ)]
+        h_bf = [sb([P, 2, PASS], BF16, "h_bf%d" % q, (None, "w3_bf0", "h2_act1", None)[q]) for q in range(NQ)]
+        h_codes = [sb([P, 2, SQ], U32, "h_codes%d" % q) for q in range(NQ)]
+        h_plane = [sb([P, 2, SQ], U8, "h_plane%d" % q) for q in range(NQ)]
+        sums = []
+
+        def history_unit(b, q):
+            bank = held.tile([P, PACK, SQ], F32, name="history%d%d" % (b, q), tag="bank%d" % ((2 * NQ + 2 * q + b) % 3))
+            cols = slice(SQ * q, SQ * (q + 1))
+            for t in range(PACK):
+                for a in range(2):
+                    c0 = H * a + PASS * b + P * t
+                    nc.tensor.matmul_mx(
+                        out=bank[:, t, :],
+                        lhsT=w1_codes[:, 2 * c0 : 2 * (c0 + P)].bitcast(FP4X4),
+                        lhsT_scale=w1_plane[:, c0 : c0 + P],
+                        rhs=v1_codes[a][:, cols].bitcast(FP8X4), rhs_scale=v1_plane[a][:, cols],
+                        start=(a == 0), stop=(a == 1),
+                    )
+            activate(h_act[q][:, b, :], bank, ACT.Gelu_apprx_tanh)
+
+        def history_gain(q):
+            nc.vector.tensor_tensor(
+                h_bf[q][:].rearrange("p b (s t) -> p b s t", t=PACK),
+                h_act[q][:].rearrange("p b (s t) -> p b s t", t=PACK),
+                gains[0][:, 0:2, :].unsqueeze(2).to_broadcast([P, 2, SQ, PACK]),
+                MULT,
+            )
+
+        def history_quantize(q):
+            quantize(
+                h_codes[q][:].rearrange("p b s -> p (b s)"),
+                h_plane[q][:].rearrange("p b s -> p (b s)"),
+                h_bf[q][:].rearrange("p b s -> p (b s)"),
+            )
+
+        def sweep_sum(q):
+            sums.append(held.tile([P, N // P, SQ], F32, name="sums%d" % q, tag="gains1" if q == NQ - 1 else "sums%d" % q))
+            cols = slice(SQ * q, SQ * (q + 1))
+            for a in range(2):
+                for i in range(N // P):
+                    slots = slice(P * i, P * (i + 1))
+                    nc.tensor.matmul_mx(
+                        out=sums[q][:, i, :],
+                        lhsT=w4_codes[:, a, slots].bitcast(FP8X4), lhsT_scale=w4_plane[4 + 4 * a :, slots],
+                        rhs=h2_codes[a][:, cols].bitcast(FP8X4), rhs_scale=h2_plane[a][:, cols],
+                        start=(a == 0 and i == 0), stop=False,
+                    )
+
+        def history_sum(q, b):
+            for i in range(N // P):
+                slots = slice(P * i, P * (i + 1))
+                nc.tensor.matmul_mx(
+                    out=sums[q][:, i, :],
+                    lhsT=w3_codes[b][:, slots].bitcast(FP8X4), lhsT_scale=w3_plane[b][:, slots],
+                    rhs=h_codes[q][:, b, :].bitcast(FP8X4), rhs_scale=h_plane[q][:, b, :],
+                    start=False, stop=(b == 1 and i == N // P - 1),
+                )
+
+        out_rows = out.rearrange("(i p) s -> p i s", p=P)
+
+        def finish(q, engine):
+            half = sb([P, N // P, SQ], F32, "half%d" % q)
+            prob = sb([P, N // P, SQ], F32, "prob%d" % q)
+            nc.scalar.activation(half[:], sums[q][:], ACT.Tanh, scale=0.5)
+            engine.tensor_scalar(prob[:], half[:], 0.5, 0.5, MULT, ADD)
+            nc.sync.dma_start(out=out_rows[:, :, SQ * q : SQ * (q + 1)], in_=prob[:])
+
+        last = NQ - 1
+        for q in range(NQ):
+            for b in range(2):
+                history_unit(b, q)
+        round_w3(1, N // 2, N, nc.scalar.copy)
+        for q in range(NQ):
+            sweep_sum(q)
+        history_gain(0)
+        quantize_w3(0)
+        history_gain(1)
+        history_quantize(0)
+        quantize_w3(1)
+        history_quantize(1)
+        history_gain(2)
+        apply_gain(h_bf[last][:, 0, :], h_act[last][:, 0, :], 0, 0)
+        history_quantize(2)
+        quantize(h_codes[last][:, 0, :], h_plane[last][:, 0, :], h_bf[last][:, 0, :])
+        apply_gain(h_bf[last][:, 1, :], h_act[last][:, 1, :], 0, 1)
+        quantize(h_codes[last][:, 1, :], h_plane[last][:, 1, :], h_bf[last][:, 1, :])
+        for q in range(NQ):
+            for b in range(2):
+                history_sum(q, b)
+            finish(q, nc.vector if q == last else nc.gpsimd)

@@ -177,9 +177,6 @@ def tile_list_parking_occupancy_kernel(
         v1_plane = [over([P, S], U8, "v1_plane%d" % a, S * a) for a in range(2)]
         for a in range(2):
             nc.vector.tensor_copy(v1_plane[a][:], t1_plane[:, a, :].indirect(list1[:]))
-        for u in range(2):
-            for m0 in (0, 32):
-                round_w2(1, u, m0, m0 + 32, pool_round)
 
         h2_act = [over([P, S * PACK], F32, "h2_act0", 8192), sb([P, S * PACK], F32, "h2_act1")]
 
@@ -221,6 +218,10 @@ def tile_list_parking_occupancy_kernel(
 
         for q in range(NQ):
             sweep_unit(0, q)
+        nc.scalar.copy(
+            w2_bf[1][:].rearrange("p t m j -> p m t j"),
+            w2_late[:].rearrange("p j (m t) -> p m t j", t=PACK),
+        )
         h2_first = sb([P, 2 * PASS], BF16, "h2_first")
         sweep_gain(0, 0, 1, h2_first[:, 0:PASS])
         sweep_gain(0, 1, 2, h2_first[:, PASS : 2 * PASS])
@@ -262,7 +263,7 @@ def tile_list_parking_occupancy_kernel(
             round_w3(1, n0, n0 + 128, pool_round)
 
         h_act = [sb([P, 2, PASS], F32, "h_act%d" % q) for q in range(NQ)]
-        h_bf = [sb([P, 2, PASS], BF16, "h_bf%d" % q, (None, "w3_bf0", "h2_act1", None)[q]) for q in range(NQ)]
+        h_bf = [sb([P, 2, PASS], BF16, "h_bf%d" % q, (None, "w3_bf0", None, "h2_act1")[q]) for q in range(NQ)]
         h_codes = [sb([P, 2, SQ], U32, "h_codes%d" % q) for q in range(NQ)]
         h_plane = [sb([P, 2, SQ], U8, "h_plane%d" % q) for q in range(NQ)]
         sums = []
@@ -322,11 +323,9 @@ def tile_list_parking_occupancy_kernel(
 
         out_rows = out.rearrange("(i p) s -> p i s", p=P)
 
-        def finish(q, engine):
-            half = sb([P, N // P, SQ], F32, "half%d" % q)
+        def finish(q):
             prob = sb([P, N // P, SQ], F32, "prob%d" % q)
-            nc.scalar.activation(half[:], sums[q][:], ACT.Tanh, scale=0.5)
-            engine.tensor_scalar(prob[:], half[:], 0.5, 0.5, MULT, ADD)
+            nc.scalar.activation(prob[:], sums[q][:], ACT.Sigmoid)
             nc.sync.dma_start(out=out_rows[:, :, SQ * q : SQ * (q + 1)], in_=prob[:])
 
         last = NQ - 1
@@ -340,15 +339,15 @@ def tile_list_parking_occupancy_kernel(
         quantize_w3(0)
         history_gain(1)
         history_quantize(0)
-        quantize_w3(1)
-        history_quantize(1)
         history_gain(2)
-        apply_gain(h_bf[last][:, 0, :], h_act[last][:, 0, :], 0, 0)
+        history_quantize(1)
+        quantize_w3(1)
         history_quantize(2)
-        quantize(h_codes[last][:, 0, :], h_plane[last][:, 0, :], h_bf[last][:, 0, :])
+        apply_gain(h_bf[last][:, 0, :], h_act[last][:, 0, :], 0, 0)
         apply_gain(h_bf[last][:, 1, :], h_act[last][:, 1, :], 0, 1)
+        quantize(h_codes[last][:, 0, :], h_plane[last][:, 0, :], h_bf[last][:, 0, :])
         quantize(h_codes[last][:, 1, :], h_plane[last][:, 1, :], h_bf[last][:, 1, :])
         for q in range(NQ):
             for b in range(2):
                 history_sum(q, b)
-            finish(q, nc.vector if q == last else nc.gpsimd)
+            finish(q)

@@ -64,7 +64,7 @@ def tile_list_parking_occupancy_kernel(
         t2_words = sb([P, T2], U16, "t2_words")
         t2_plane = sb([P, 1, T2], U8, "t2_plane")
         t1_words = [sb([P, T], U32, "t1_words0"), over([P, T], U32, "t1_words1", 16384)]
-        t1_plane = sb([P, 2, T], U8, "t1_plane")
+        t1_plane = sb([P, T], U8, "t1_plane")
         w1_raw = sb([P, 2, H // 2], I32, "w1_raw")
         w1_raw_plane = sb([P, 2, H], U8, "w1_raw_plane")
         w4_codes = sb([P, 2, N], U32, "w4_codes")
@@ -73,17 +73,17 @@ def tile_list_parking_occupancy_kernel(
         w2_late = sb([P, PACK, PASS], F32, "w2_late")
         w2_raw.append([w2_late[:, :, 0:256], w2_late[:, :, 256:512]])
         w3_raw = [sb([P, PACK, N], F32, "w3_raw%d" % a) for a in range(2)]
-        gain_rows = [sb([P, PASS], F32, "gain_rows%d" % i) for i in range(2)]
+        gain_rows = sb([P, PASS], F32, "gain_rows")
 
         nc.gpsimd.memset(t2_plane[:].bitcast(I32), 0)
         nc.vector.memset(t1_plane[:].bitcast(I32), 0)
         warm = sb([P, 8], F32, "warm")
         nc.gpsimd.memset(warm[:], 0.0)
         nc.scalar.activation(warm[:, 4:5], warm[:, 0:1], ACT.Silu)
-        gain_slots = [None, sb([P, PACK, P], F32, "gain_slots1")]
-        nc.gpsimd.memset(gain_slots[1][:], 0.0)
-        nc.gpsimd.memset(w1_raw_plane[:].bitcast(I32), 0)
-        nc.gpsimd.memset(w4_plane[:].bitcast(I32), 0)
+        gain_slots = sb([P, PACK, P], F32, "gain_slots")
+        nc.gpsimd.memset(gain_slots[:], 0.0)
+        nc.vector.memset(w1_raw_plane[:].bitcast(I32), 0)
+        nc.vector.memset(w4_plane[:].bitcast(I32), 0)
         identity = sb([P, P], F32, "identity")
         make_identity(nc, identity[:])
 
@@ -109,10 +109,11 @@ def tile_list_parking_occupancy_kernel(
         load_scales(nc.sync, t2_plane, tab2_scales)
         load_w2(0, 0)
         load_w2(0, 1)
-        nc.sync.dma_start(out=gain_rows[1][0:2], in_=gs.rearrange("(a c) -> a c", a=2))
+        nc.sync.dma_start(out=gain_rows[GS_ROW : GS_ROW + 2], in_=gs.rearrange("(a c) -> a c", a=2))
+        nc.sync.dma_start(out=gain_rows[0:2], in_=gh.rearrange("(a c) -> a c", a=2))
         nc.sync.dma_start(out=w2_late[:], in_=w2_rows[:, :, PASS : 2 * PASS])
         nc.sync.dma_start(list1[:], offs)
-        load_scales(nc.sync, t1_plane, tab_scales)
+        load_packed_scales(nc.sync, t1_plane, tab_scales, 0)
         load_t1(0)
 
         v2_codes = sb([P, S], U16, "v2_codes")
@@ -122,7 +123,6 @@ def tile_list_parking_occupancy_kernel(
 
         nc.sync.dma_start(out=w1_raw[:], in_=w1_words.bitcast(I32).rearrange("a p c -> p a c"))
         load_scales(nc.sync, w1_raw_plane, w1_scales)
-        nc.sync.dma_start(out=gain_rows[0][0:2], in_=gh.rearrange("(a c) -> a c", a=2))
         load_t1(1)
         load_w3(0)
         load_w3(1)
@@ -162,21 +162,20 @@ def tile_list_parking_occupancy_kernel(
         round_w2(0, 0, 0, 64, nc.scalar.copy)
         round_w2(0, 1, 0, 24, nc.scalar.copy)
         round_w2(0, 1, 24, 64, nc.vector.tensor_copy)
-        gains = [held.tile([P, P, PACK], F32, name="gains%d" % i, tag="gains%d" % i) for i in range(2)]
-
-        def spread_gains(i):
-            for t in range(PACK):
-                nc.tensor.transpose(gains[i][:, :, t], gain_slots[i][:, t, :], identity[:])
-
         nc.scalar.copy(
-            out=gain_slots[1][0:2],
-            in_=gain_rows[1][0:2].rearrange("p (m t) -> p t m", t=PACK),
+            out=gain_slots[GS_ROW : GS_ROW + 2],
+            in_=gain_rows[GS_ROW : GS_ROW + 2].rearrange("p (m t) -> p t m", t=PACK),
         )
-        spread_gains(1)
+        nc.scalar.copy(
+            out=gain_slots[0:2].rearrange("p t (g e) -> p t g e", e=4),
+            in_=gain_rows[0:2].rearrange("p (g t e) -> p t g e", t=PACK, e=4),
+        )
+        gains = held.tile([P, P, PACK], F32, name="gains")
+        for t in range(PACK):
+            nc.tensor.transpose(gains[:, :, t], gain_slots[:, t, :], identity[:])
         quantize_w2(0)
-        v1_plane = [over([P, S], U8, "v1_plane%d" % a, S * a) for a in range(2)]
-        for a in range(2):
-            nc.vector.tensor_copy(v1_plane[a][:], t1_plane[:, a, :].indirect(list1[:]))
+        v1_plane = [over([P, S], U8, "v1_plane0", 0), None]
+        nc.vector.tensor_copy(v1_plane[0][:], t1_plane[:].indirect(list1[:]))
 
         h2_act = [over([P, S * PACK], F32, "h2_act0", 8192), sb([P, S * PACK], F32, "h2_act1")]
 
@@ -190,12 +189,12 @@ def tile_list_parking_occupancy_kernel(
                 dst.rearrange("p (s t) -> p s t", t=PACK), bank[:].rearrange("p t s -> p s t"), func
             )
 
-        def apply_gain(dst, src, branch, row):
+        def apply_gain(dst, src, row):
             width = src.shape[1] // PACK
             nc.vector.tensor_tensor(
                 dst.rearrange("p (s t) -> p s t", t=PACK),
                 src.rearrange("p (s t) -> p s t", t=PACK),
-                gains[branch][:, row : row + 1, :].to_broadcast([P, width, PACK]),
+                gains[:, row : row + 1, :].to_broadcast([P, width, PACK]),
                 MULT,
             )
 
@@ -213,26 +212,27 @@ def tile_list_parking_occupancy_kernel(
             activate(sweep_act(a, q, q + 1), bank, ACT.Silu)
 
         def sweep_gain(a, q0, q1, dst):
-            apply_gain(dst, sweep_act(a, q0, q1), 1, a)
+            apply_gain(dst, sweep_act(a, q0, q1), GS_ROW + a)
 
 
         for q in range(NQ):
             sweep_unit(0, q)
-        nc.scalar.copy(
-            w2_bf[1][:].rearrange("p t m j -> p m t j"),
-            w2_late[:].rearrange("p j (m t) -> p m t j", t=PACK),
-        )
-        h2_first = sb([P, 2 * PASS], BF16, "h2_first")
+        round_w2(1, 0, 0, 64, nc.scalar.copy)
+        for m0 in (0, 32):
+            round_w2(1, 1, m0, m0 + 32, pool_round)
+        v1_plane[1] = sb([P, S], U8, "v1_plane1", "w2_late")
+        nc.gpsimd.memset(v1_plane[1][:].bitcast(I32), 0)
+        nc.gpsimd.dma_start(out=v1_plane[1][:].bitcast(I32)[0 : P - 4], in_=v1_plane[0][:].bitcast(I32)[4:P])
+        h2_first = sb([P, S * PACK], BF16, "h2_first")
         sweep_gain(0, 0, 1, h2_first[:, 0:PASS])
         sweep_gain(0, 1, 2, h2_first[:, PASS : 2 * PASS])
+        sweep_gain(0, 2, 4, h2_first[:, 2 * PASS : 4 * PASS])
         quantize_w2(1)
-        h2_second = over([P, 2 * PASS], BF16, "h2_second", 4096)
-        sweep_gain(0, 2, 4, h2_second[:])
-        v1_codes = [over([P, S], U32, "v1_codes0", 4096 + 2048), over([P, S], U32, "v1_codes1", 8192 + 6144)]
-        w1_codes = over([P, 2 * 2 * H], U8, "w1_codes", 8192)
-        w1_plane = over([P, 2 * H], U8, "w1_plane", 8192 + 4096)
         for q in range(NQ):
             sweep_unit(1, q)
+        v1_codes = [over([P, S], U32, "v1_codes0", 4096), over([P, S], U32, "v1_codes1", 8192 + 6144)]
+        w1_codes = over([P, 2 * 2 * H], U8, "w1_codes", 8192)
+        w1_plane = over([P, 2 * H], U8, "w1_plane", 8192 + 4096)
         nc.vector.tensor_copy(v1_codes[0][:], t1_words[0][:].indirect(list1[:]))
         nc.vector.tensor_copy(
             w1_codes[:].bitcast(I32).rearrange("p (x t g w) -> p x g t w", t=PACK, g=32, w=2),
@@ -243,27 +243,19 @@ def tile_list_parking_occupancy_kernel(
             w1_raw_plane[:].bitcast(I32).rearrange("p a (b g t) -> p (a b) g t", t=PACK, g=32),
         )
         nc.vector.tensor_copy(v1_codes[1][:], t1_words[1][:].indirect(list1[:]))
-        gain_slots[0] = sb([P, PACK, P], F32, "gain_slots0", "w2_late")
-        nc.gpsimd.memset(gain_slots[0][:], 0.0)
-        pool_round(
-            gain_slots[0][0:2].rearrange("p t (g e) -> p t g e", e=4),
-            gain_rows[0][0:2].rearrange("p (g t e) -> p t g e", t=PACK, e=4),
-        )
-        spread_gains(0)
         h2_third = over([P, S * PACK], BF16, "h2_third", 16384)
-        h2_codes = [over([P, S], U32, "h2_codes0", 16384 + 4096), sb([P, S], U32, "h2_codes1")]
+        h2_codes = [sb([P, S], U32, "h2_codes0", "w1_raw"), sb([P, S], U32, "h2_codes1")]
+        quantize(h2_codes[0][:], h2_plane[0][:], h2_first[:])
         sweep_gain(1, 0, 4, h2_third[:])
-        quantize(h2_codes[0][:, 0:256], h2_plane[0][:, 0:256], h2_first[:])
-        quantize(h2_codes[0][:, 256:512], h2_plane[0][:, 256:512], h2_second[:])
         quantize(h2_codes[1][:], h2_plane[1][:], h2_third[:])
-        w3_bf = [sb([P, N, PACK], BF16, "w3_bf0"), sb([P, N, PACK], BF16, "w3_bf1", "h2_act1")]
+        w3_bf = [sb([P, N, PACK], BF16, "w3_bf0"), sb([P, N, PACK], BF16, "w3_bf1")]
         for n0 in range(0, N, 128):
             round_w3(0, n0, n0 + 128, pool_round)
-        for n0 in range(0, N // 2, 128):
+        for n0 in range(0, N, 128):
             round_w3(1, n0, n0 + 128, pool_round)
 
         h_act = [sb([P, 2, PASS], F32, "h_act%d" % q) for q in range(NQ)]
-        h_bf = [sb([P, 2, PASS], BF16, "h_bf%d" % q, (None, "w3_bf0", None, "h2_act1")[q]) for q in range(NQ)]
+        h_bf = [sb([P, 2, PASS], BF16, "h_bf%d" % q, (None, "w3_bf0", "w3_bf1", None)[q]) for q in range(NQ)]
         h_codes = [sb([P, 2, SQ], U32, "h_codes%d" % q) for q in range(NQ)]
         h_plane = [sb([P, 2, SQ], U8, "h_plane%d" % q) for q in range(NQ)]
         sums = []
@@ -287,7 +279,7 @@ def tile_list_parking_occupancy_kernel(
             nc.vector.tensor_tensor(
                 h_bf[q][:].rearrange("p b (s t) -> p b s t", t=PACK),
                 h_act[q][:].rearrange("p b (s t) -> p b s t", t=PACK),
-                gains[0][:, 0:2, :].unsqueeze(2).to_broadcast([P, 2, SQ, PACK]),
+                gains[:, 0:2, :].unsqueeze(2).to_broadcast([P, 2, SQ, PACK]),
                 MULT,
             )
 
@@ -299,7 +291,7 @@ def tile_list_parking_occupancy_kernel(
             )
 
         def sweep_sum(q):
-            sums.append(held.tile([P, N // P, SQ], F32, name="sums%d" % q, tag="gains1" if q == NQ - 1 else "sums%d" % q))
+            sums.append(held.tile([P, N // P, SQ], F32, name="sums%d" % q, tag="bank%d" % (q % 3) if q else "sums0"))
             cols = slice(SQ * q, SQ * (q + 1))
             for a in range(2):
                 for i in range(N // P):
@@ -332,19 +324,18 @@ def tile_list_parking_occupancy_kernel(
         for q in range(NQ):
             for b in range(2):
                 history_unit(b, q)
-        round_w3(1, N // 2, N, nc.scalar.copy)
         for q in range(NQ):
             sweep_sum(q)
         history_gain(0)
         quantize_w3(0)
         history_gain(1)
         history_quantize(0)
-        history_gain(2)
-        history_quantize(1)
         quantize_w3(1)
+        history_quantize(1)
+        history_gain(2)
+        apply_gain(h_bf[last][:, 0, :], h_act[last][:, 0, :], 0)
         history_quantize(2)
-        apply_gain(h_bf[last][:, 0, :], h_act[last][:, 0, :], 0, 0)
-        apply_gain(h_bf[last][:, 1, :], h_act[last][:, 1, :], 0, 1)
+        apply_gain(h_bf[last][:, 1, :], h_act[last][:, 1, :], 1)
         quantize(h_codes[last][:, 0, :], h_plane[last][:, 0, :], h_bf[last][:, 0, :])
         quantize(h_codes[last][:, 1, :], h_plane[last][:, 1, :], h_bf[last][:, 1, :])
         for q in range(NQ):

@@ -24,7 +24,10 @@ PASS = P * PACK
 QUADS = 4
 SQ = 128
 NQ = S // SQ
+RUN = 8
 GS_ROW = 64
+RING = 7
+AHEAD = 4
 
 
 def tile_list_parking_occupancy_kernel(
@@ -43,19 +46,19 @@ def tile_list_parking_occupancy_kernel(
         def over(shape, dtype, name, offset):
             return reuse.tile(shape, dtype, name=name, align_bytes=64, offset=offset)
 
-        def load_scales(queue, plane, scales):
+        def load_scales(plane, scales):
             rows = scales.bitcast(I32)
             for quad in range(QUADS):
-                queue.dma_start(
+                nc.sync.dma_start(
                     out=plane[:].bitcast(I32)[32 * quad : 32 * quad + 4],
                     in_=rows[:, 4 * quad : 4 * quad + 4, :].rearrange("a r c -> r a c"),
                 )
 
-        def load_packed_scales(queue, plane, scales, row):
+        def load_stacked_scales(plane, scales):
             rows = scales.bitcast(I32)
             for quad in range(QUADS):
-                queue.dma_start(
-                    out=plane[:].bitcast(I32)[32 * quad + row : 32 * quad + row + 8],
+                nc.sync.dma_start(
+                    out=plane[:].bitcast(I32)[32 * quad : 32 * quad + 8],
                     in_=rows[:, 4 * quad : 4 * quad + 4, :],
                 )
 
@@ -63,35 +66,34 @@ def tile_list_parking_occupancy_kernel(
         list2 = keep.tile([P, S // 16], U16, name="list2")
         t2_words = sb([P, T2], U16, "t2_words")
         t2_plane = sb([P, 1, T2], U8, "t2_plane")
-        t1_words = [sb([P, T], U32, "t1_words0"), over([P, T], U32, "t1_words1", 16384)]
-        t1_plane = sb([P, T], U8, "t1_plane")
+        t1_words = [over([P, T], U32, "t1_words%d" % a, 4 * T * a) for a in range(2)]
+        t1_plane = over([P, T], U8, "t1_plane", 8 * T)
         w1_raw = sb([P, 2, H // 2], I32, "w1_raw")
         w1_raw_plane = sb([P, 2, H], U8, "w1_raw_plane")
         w4_codes = sb([P, 2, N], U32, "w4_codes")
-        w4_plane = sb([P, N], U8, "w4_plane")
-        w2_raw = [[sb([P, PACK, 256], F32, "w2_raw%d%d" % (a, u)) for u in range(2)] for a in range(1)]
-        w2_late = sb([P, PACK, PASS], F32, "w2_late")
-        w2_raw.append([w2_late[:, :, 0:256], w2_late[:, :, 256:512]])
+        w4_plane = sb([P, 2, N], U8, "w4_plane")
+        w2_raw = [sb([P, PACK, 256], F32, "w2_raw%d" % u) for u in range(4)]
         w3_raw = [sb([P, PACK, N], F32, "w3_raw%d" % a) for a in range(2)]
         gain_rows = sb([P, PASS], F32, "gain_rows")
+        gain_slots = sb([P, PACK, P], F32, "gain_slots")
+        v1_plane = [sb([P, S], U8, "v1_plane%d" % a) for a in range(2)]
+        identity = sb([P, P], F32, "identity")
+        warm = sb([P, 8], F32, "warm")
 
         nc.gpsimd.memset(t2_plane[:].bitcast(I32), 0)
         nc.vector.memset(t1_plane[:].bitcast(I32), 0)
-        warm = sb([P, 8], F32, "warm")
-        nc.gpsimd.memset(warm[:], 0.0)
-        nc.scalar.activation(warm[:, 4:5], warm[:, 0:1], ACT.Silu)
-        gain_slots = sb([P, PACK, P], F32, "gain_slots")
-        nc.gpsimd.memset(gain_slots[:], 0.0)
         nc.vector.memset(w1_raw_plane[:].bitcast(I32), 0)
         nc.vector.memset(w4_plane[:].bitcast(I32), 0)
-        identity = sb([P, P], F32, "identity")
+        nc.vector.memset(v1_plane[1][:].bitcast(I32), 0)
+        nc.gpsimd.memset(warm[:], 0.0)
+        nc.scalar.activation(warm[:, 4:5], warm[:, 0:1], ACT.Silu)
+        nc.vector.memset(gain_slots[:], 0.0)
         make_identity(nc, identity[:])
 
         w2_rows = w2.rearrange("(p j) c -> p j c", j=PACK)
 
-        def load_w2(a, u):
-            c0 = PASS * a + 256 * u
-            nc.sync.dma_start(out=w2_raw[a][u][:], in_=w2_rows[:, :, c0 : c0 + 256])
+        def load_w2(u):
+            nc.sync.dma_start(out=w2_raw[u][:], in_=w2_rows[:, :, 256 * u : 256 * (u + 1)])
 
         def load_t1(a):
             nc.sync.dma_start(
@@ -99,52 +101,48 @@ def tile_list_parking_occupancy_kernel(
                 in_=tab_words[a].rearrange("p t i -> p (t i)").bitcast(I32),
             )
 
-        def load_w3(a):
-            rows = w3[PASS * a : PASS * (a + 1), :].rearrange("(g t e) n -> e g t n", t=PACK, e=4)
-            for e in range(4):
-                nc.sync.dma_start(out=w3_raw[a][e:P:4], in_=rows[e])
+        w3_rows = w3.rearrange("(b g t e) n -> b t g e n", b=2, t=PACK, e=RUN)
+
+        def load_w3(b):
+            for t in range(PACK):
+                nc.sync.dma_start(out=w3_raw[b][:, t, :], in_=w3_rows[b, t])
 
         nc.sync.dma_start(out=t2_words[:].bitcast(I32), in_=tab2_words[0].bitcast(I32))
         nc.sync.dma_start(list2[:], offs2)
-        load_scales(nc.sync, t2_plane, tab2_scales)
-        load_w2(0, 0)
-        load_w2(0, 1)
+        load_scales(t2_plane, tab2_scales)
+        load_w2(0)
+        load_w2(1)
+        nc.sync.dma_start(list1[:], offs)
         nc.sync.dma_start(out=gain_rows[GS_ROW : GS_ROW + 2], in_=gs.rearrange("(a c) -> a c", a=2))
         nc.sync.dma_start(out=gain_rows[0:2], in_=gh.rearrange("(a c) -> a c", a=2))
-        nc.sync.dma_start(out=w2_late[:], in_=w2_rows[:, :, PASS : 2 * PASS])
-        nc.sync.dma_start(list1[:], offs)
-        load_packed_scales(nc.sync, t1_plane, tab_scales, 0)
+        load_w2(2)
+        load_stacked_scales(t1_plane, tab_scales)
+        load_w2(3)
         load_t1(0)
+        load_scales(w1_raw_plane, w1_scales)
+        nc.sync.dma_start(out=w1_raw[:], in_=w1_words.bitcast(I32).rearrange("a p c -> p a c"))
+        load_t1(1)
 
         v2_codes = sb([P, S], U16, "v2_codes")
         v2_plane = sb([P, S], U8, "v2_plane")
         nc.vector.tensor_copy(v2_codes[:], t2_words[:].indirect(list2[:]))
         nc.vector.tensor_copy(v2_plane[:], t2_plane[:, 0, :].indirect(list2[:]))
 
-        nc.sync.dma_start(out=w1_raw[:], in_=w1_words.bitcast(I32).rearrange("a p c -> p a c"))
-        load_scales(nc.sync, w1_raw_plane, w1_scales)
-        load_t1(1)
-        load_w3(0)
-        load_w3(1)
-        nc.sync.dma_start(
-            out=w4_codes[:].bitcast(I32),
-            in_=w4_words.rearrange("a p c i -> p a (c i)").bitcast(I32),
-        )
-        load_packed_scales(nc.sync, w4_plane, w4_scales, 4)
-
-        w2_bf = [over([P, PACK, P, PACK], BF16, "w2_bf%d" % a, 4096 * a) for a in range(2)]
+        w2_bf = [over([P, PACK, P, PACK], BF16, "w2_bf%d" % a, 10 * T + 4096 * a) for a in range(2)]
         w2_codes = [sb([P, PASS], U32, "w2_codes%d" % a) for a in range(2)]
         w2_plane = [sb([P, PASS], U8, "w2_plane%d" % a) for a in range(2)]
-        w3_codes = [sb([P, N], U32, "w3_codes%d" % a) for a in range(2)]
-        w3_plane = [sb([P, N], U8, "w3_plane%d" % a) for a in range(2)]
+        w3_bf = [sb([P, N, PACK], BF16, "w3_bf%d" % b) for b in range(2)]
+        w3_codes = [sb([P, N], U32, "w3_codes%d" % b) for b in range(2)]
+        w3_plane = [sb([P, N], U8, "w3_plane%d" % b) for b in range(2)]
 
         def pool_round(dst, src):
             nc.gpsimd.tensor_scalar(dst, src, 1.0, 0.0, MULT, ADD)
 
-        def round_w2(a, u, m0, m1, rounder):
+        def round_w2(u, m0, m1, rounder):
+            base = 64 * (u % 2)
             rounder(
-                w2_bf[a][:, :, 64 * u + m0 : 64 * u + m1, :].rearrange("p t m j -> p m t j"),
-                w2_raw[a][u][:, :, PACK * m0 : PACK * m1].rearrange("p j (m t) -> p m t j", t=PACK),
+                w2_bf[u // 2][:, :, base + m0 : base + m1, :].rearrange("p t m j -> p m t j"),
+                w2_raw[u][:, :, PACK * m0 : PACK * m1].rearrange("p j (m t) -> p m t j", t=PACK),
             )
 
         def quantize(codes, plane, values):
@@ -153,36 +151,45 @@ def tile_list_parking_occupancy_kernel(
         def quantize_w2(a):
             quantize(w2_codes[a][:], w2_plane[a][:], w2_bf[a][:].rearrange("p t m j -> p (t m j)"))
 
-        def round_w3(a, n0, n1, rounder):
-            rounder(w3_bf[a][:, n0:n1, :], w3_raw[a][:, :, n0:n1].rearrange("p t n -> p n t"))
+        def round_w3(b, n0, n1, rounder):
+            rounder(w3_bf[b][:, n0:n1, :], w3_raw[b][:, :, n0:n1].rearrange("p t n -> p n t"))
 
-        def quantize_w3(a):
-            quantize(w3_codes[a][:], w3_plane[a][:], w3_bf[a][:].rearrange("p n t -> p (n t)"))
+        def quantize_w3(b):
+            quantize(w3_codes[b][:], w3_plane[b][:], w3_bf[b][:].rearrange("p n t -> p (n t)"))
 
-        round_w2(0, 0, 0, 64, nc.scalar.copy)
-        round_w2(0, 1, 0, 24, nc.scalar.copy)
-        round_w2(0, 1, 24, 64, nc.vector.tensor_copy)
-        nc.scalar.copy(
-            out=gain_slots[GS_ROW : GS_ROW + 2],
-            in_=gain_rows[GS_ROW : GS_ROW + 2].rearrange("p (m t) -> p t m", t=PACK),
+        round_w2(0, 0, 64, nc.scalar.copy)
+        round_w2(1, 0, 32, nc.scalar.copy)
+        round_w2(1, 32, 64, nc.vector.tensor_copy)
+        quantize_w2(0)
+        pool_round(
+            gain_slots[GS_ROW : GS_ROW + 2],
+            gain_rows[GS_ROW : GS_ROW + 2].rearrange("p (m t) -> p t m", t=PACK),
         )
-        nc.scalar.copy(
-            out=gain_slots[0:2].rearrange("p t (g e) -> p t g e", e=4),
-            in_=gain_rows[0:2].rearrange("p (g t e) -> p t g e", t=PACK, e=4),
+        pool_round(
+            gain_slots[0:2].rearrange("p t (g e) -> p t g e", e=RUN),
+            gain_rows[0:2].rearrange("p (g t e) -> p t g e", t=PACK, e=RUN),
         )
         gains = held.tile([P, P, PACK], F32, name="gains")
         for t in range(PACK):
             nc.tensor.transpose(gains[:, :, t], gain_slots[:, t, :], identity[:])
-        quantize_w2(0)
-        v1_plane = [over([P, S], U8, "v1_plane0", 0), None]
         nc.vector.tensor_copy(v1_plane[0][:], t1_plane[:].indirect(list1[:]))
+        nc.sync.dma_start(out=v1_plane[1][:].bitcast(I32)[0 : P - 4], in_=v1_plane[0][:].bitcast(I32)[4:P])
+        load_scales(w4_plane, w4_scales)
+        nc.sync.dma_start(
+            out=w4_codes[:].bitcast(I32),
+            in_=w4_words.rearrange("a p c i -> p a (c i)").bitcast(I32),
+        )
+        load_w3(0)
+        load_w3(1)
 
-        h2_act = [over([P, S * PACK], F32, "h2_act0", 8192), sb([P, S * PACK], F32, "h2_act1")]
-
-        def sweep_act(a, q0, q1):
-            return h2_act[a][:, PASS * q0 : PASS * q1]
-
+        h2_act = [sb([P, S * PACK], F32, "h2_act%d" % a) for a in range(2)]
+        h2_first = over([P, S * PACK], BF16, "h2_first", 8 * T)
+        h2_second = over([P, S * PACK], BF16, "h2_second", 4 * T)
+        h2_codes = [over([P, S], U32, "h2_codes0", 0), sb([P, S], U32, "h2_codes1")]
         h2_plane = [sb([P, S], U8, "h2_plane%d" % a) for a in range(2)]
+
+        def bank_tile(name, index):
+            return held.tile([P, PACK, SQ], F32, name=name, tag="bank%d" % (index % RING))
 
         def activate(dst, bank, func):
             nc.scalar.activation(
@@ -199,7 +206,7 @@ def tile_list_parking_occupancy_kernel(
             )
 
         def sweep_unit(a, q):
-            bank = held.tile([P, PACK, SQ], F32, name="sweep%d%d" % (a, q), tag="bank%d" % ((NQ * a + q) % 3))
+            bank = bank_tile("sweep%d%d" % (a, q), NQ * a + q + RING - 1)
             cols = slice(SQ * q, SQ * (q + 1))
             for t in range(PACK):
                 chan = slice(P * t, P * (t + 1))
@@ -209,71 +216,68 @@ def tile_list_parking_occupancy_kernel(
                     rhs=v2_codes[:, cols].bitcast(FP4X4), rhs_scale=v2_plane[:, cols],
                     start=True, stop=True,
                 )
-            activate(sweep_act(a, q, q + 1), bank, ACT.Silu)
+            activate(h2_act[a][:, PASS * q : PASS * (q + 1)], bank, ACT.Silu)
 
-        def sweep_gain(a, q0, q1, dst):
-            apply_gain(dst, sweep_act(a, q0, q1), GS_ROW + a)
+        def first_gain(q0, q1):
+            cols = slice(PASS * q0, PASS * q1)
+            apply_gain(h2_first[:, cols], h2_act[0][:, cols], GS_ROW)
 
+        def second_gain():
+            apply_gain(h2_second[:], h2_act[1][:], GS_ROW + 1)
 
+        round_w2(2, 0, 32, nc.scalar.copy)
         for q in range(NQ):
             sweep_unit(0, q)
-        round_w2(1, 0, 0, 64, nc.scalar.copy)
+        round_w2(2, 32, 64, nc.scalar.copy)
         for m0 in (0, 32):
-            round_w2(1, 1, m0, m0 + 32, pool_round)
-        v1_plane[1] = sb([P, S], U8, "v1_plane1", "w2_late")
-        nc.gpsimd.memset(v1_plane[1][:].bitcast(I32), 0)
-        nc.gpsimd.dma_start(out=v1_plane[1][:].bitcast(I32)[0 : P - 4], in_=v1_plane[0][:].bitcast(I32)[4:P])
-        h2_first = sb([P, S * PACK], BF16, "h2_first")
-        sweep_gain(0, 0, 1, h2_first[:, 0:PASS])
-        sweep_gain(0, 1, 2, h2_first[:, PASS : 2 * PASS])
-        sweep_gain(0, 2, 4, h2_first[:, 2 * PASS : 4 * PASS])
+            round_w2(3, m0, m0 + 32, pool_round)
+        first_gain(0, 2)
+        first_gain(2, 4)
         quantize_w2(1)
         for q in range(NQ):
             sweep_unit(1, q)
-        v1_codes = [over([P, S], U32, "v1_codes0", 4096), over([P, S], U32, "v1_codes1", 8192 + 6144)]
-        w1_codes = over([P, 2 * 2 * H], U8, "w1_codes", 8192)
-        w1_plane = over([P, 2 * H], U8, "w1_plane", 8192 + 4096)
+        v1_codes = [over([P, S], U32, "v1_codes0", 10 * T + 4096), sb([P, S], U32, "v1_codes1")]
+        w1_codes = sb([P, 2 * 2 * H], U8, "w1_codes")
+        w1_plane = sb([P, 2 * H], U8, "w1_plane")
         nc.vector.tensor_copy(v1_codes[0][:], t1_words[0][:].indirect(list1[:]))
         nc.vector.tensor_copy(
-            w1_codes[:].bitcast(I32).rearrange("p (x t g w) -> p x g t w", t=PACK, g=32, w=2),
-            w1_raw[:].rearrange("p a (b g t w) -> p (a b) g t w", t=PACK, g=32, w=2),
+            w1_codes[:].bitcast(I32).rearrange("p (x t g w) -> p x g t w", t=PACK, g=16, w=4),
+            w1_raw[:].rearrange("p a (b g t w) -> p (a b) g t w", t=PACK, g=16, w=4),
         )
         nc.vector.tensor_copy(
-            w1_plane[:].bitcast(I32).rearrange("p (x t g) -> p x g t", t=PACK, g=32),
-            w1_raw_plane[:].bitcast(I32).rearrange("p a (b g t) -> p (a b) g t", t=PACK, g=32),
+            w1_plane[:].bitcast(I32).rearrange("p (x t g w) -> p x g t w", t=PACK, g=16, w=2),
+            w1_raw_plane[:].bitcast(I32).rearrange("p a (b g t w) -> p (a b) g t w", t=PACK, g=16, w=2),
         )
-        nc.vector.tensor_copy(v1_codes[1][:], t1_words[1][:].indirect(list1[:]))
-        h2_third = over([P, S * PACK], BF16, "h2_third", 16384)
-        h2_codes = [sb([P, S], U32, "h2_codes0", "w1_raw"), sb([P, S], U32, "h2_codes1")]
         quantize(h2_codes[0][:], h2_plane[0][:], h2_first[:])
-        sweep_gain(1, 0, 4, h2_third[:])
-        quantize(h2_codes[1][:], h2_plane[1][:], h2_third[:])
-        w3_bf = [sb([P, N, PACK], BF16, "w3_bf0"), sb([P, N, PACK], BF16, "w3_bf1")]
-        for n0 in range(0, N, 128):
-            round_w3(0, n0, n0 + 128, pool_round)
-        for n0 in range(0, N, 128):
-            round_w3(1, n0, n0 + 128, pool_round)
+        for u in range(2):
+            nc.vector.tensor_copy(
+                v1_codes[1][:, 256 * u : 256 * (u + 1)], t1_words[1][:].indirect(list1[:, 16 * u : 16 * (u + 1)])
+            )
+        second_gain()
 
         h_act = [sb([P, 2, PASS], F32, "h_act%d" % q) for q in range(NQ)]
-        h_bf = [sb([P, 2, PASS], BF16, "h_bf%d" % q, (None, "w3_bf0", "w3_bf1", None)[q]) for q in range(NQ)]
+        h_bf = [sb([P, 2, PASS], BF16, "h_bf%d" % q) for q in range(2)]
         h_codes = [sb([P, 2, SQ], U32, "h_codes%d" % q) for q in range(NQ)]
         h_plane = [sb([P, 2, SQ], U8, "h_plane%d" % q) for q in range(NQ)]
         sums = []
+        banks = {}
 
-        def history_unit(b, q):
-            bank = held.tile([P, PACK, SQ], F32, name="history%d%d" % (b, q), tag="bank%d" % ((2 * NQ + 2 * q + b) % 3))
+        def history_pass(unit, a):
+            q, b = divmod(unit, 2)
+            if a == 0:
+                banks[unit] = bank_tile("history%d" % unit, unit)
             cols = slice(SQ * q, SQ * (q + 1))
             for t in range(PACK):
-                for a in range(2):
-                    c0 = H * a + PASS * b + P * t
-                    nc.tensor.matmul_mx(
-                        out=bank[:, t, :],
-                        lhsT=w1_codes[:, 2 * c0 : 2 * (c0 + P)].bitcast(FP4X4),
-                        lhsT_scale=w1_plane[:, c0 : c0 + P],
-                        rhs=v1_codes[a][:, cols].bitcast(FP8X4), rhs_scale=v1_plane[a][:, cols],
-                        start=(a == 0), stop=(a == 1),
-                    )
-            activate(h_act[q][:, b, :], bank, ACT.Gelu_apprx_tanh)
+                c0 = H * a + PASS * b + P * t
+                nc.tensor.matmul_mx(
+                    out=banks[unit][:, t, :],
+                    lhsT=w1_codes[:, 2 * c0 : 2 * (c0 + P)].bitcast(FP4X4),
+                    lhsT_scale=w1_plane[:, c0 : c0 + P],
+                    rhs=v1_codes[a][:, cols].bitcast(FP8X4), rhs_scale=v1_plane[a][:, cols],
+                    start=(a == 0 and t == 0), stop=(a == 1 and t == PACK - 1),
+                )
+            if a == 1:
+                activate(h_act[q][:, b, :], banks[unit], ACT.Gelu_apprx_tanh)
 
         def history_gain(q):
             nc.vector.tensor_tensor(
@@ -290,18 +294,18 @@ def tile_list_parking_occupancy_kernel(
                 h_bf[q][:].rearrange("p b s -> p (b s)"),
             )
 
-        def sweep_sum(q):
-            sums.append(held.tile([P, N // P, SQ], F32, name="sums%d" % q, tag="bank%d" % (q % 3) if q else "sums0"))
+        def sweep_sum(q, a):
+            if a == 0:
+                sums.append(bank_tile("sums%d" % q, q + 1))
             cols = slice(SQ * q, SQ * (q + 1))
-            for a in range(2):
-                for i in range(N // P):
-                    slots = slice(P * i, P * (i + 1))
-                    nc.tensor.matmul_mx(
-                        out=sums[q][:, i, :],
-                        lhsT=w4_codes[:, a, slots].bitcast(FP8X4), lhsT_scale=w4_plane[4 + 4 * a :, slots],
-                        rhs=h2_codes[a][:, cols].bitcast(FP8X4), rhs_scale=h2_plane[a][:, cols],
-                        start=(a == 0 and i == 0), stop=False,
-                    )
+            for i in range(N // P):
+                slots = slice(P * i, P * (i + 1))
+                nc.tensor.matmul_mx(
+                    out=sums[q][:, i, :],
+                    lhsT=w4_codes[:, a, slots].bitcast(FP8X4), lhsT_scale=w4_plane[:, a, slots],
+                    rhs=h2_codes[a][:, cols].bitcast(FP8X4), rhs_scale=h2_plane[a][:, cols],
+                    start=(a == 0 and i == 0), stop=False,
+                )
 
         def history_sum(q, b):
             for i in range(N // P):
@@ -321,20 +325,31 @@ def tile_list_parking_occupancy_kernel(
             nc.sync.dma_start(out=out_rows[:, :, SQ * q : SQ * (q + 1)], in_=prob[:])
 
         last = NQ - 1
-        for q in range(NQ):
-            for b in range(2):
-                history_unit(b, q)
-        for q in range(NQ):
-            sweep_sum(q)
+        for unit in range(AHEAD):
+            history_pass(unit, 0)
+        for unit in range(2 * NQ):
+            if unit >= AHEAD:
+                history_pass(unit, 0)
+            history_pass(unit, 1)
+        for n0 in range(0, N, 128):
+            round_w3(0, n0, n0 + 128, pool_round)
+        round_w3(1, 0, 128, pool_round)
+        round_w3(1, 128, N, nc.scalar.copy)
         history_gain(0)
-        quantize_w3(0)
+        quantize(h2_codes[1][:], h2_plane[1][:], h2_second[:])
+        for q in range(NQ):
+            for a in range(2):
+                sweep_sum(q, a)
         history_gain(1)
         history_quantize(0)
-        quantize_w3(1)
+        quantize_w3(0)
         history_quantize(1)
+        h_bf.append(sb([P, 2, PASS], BF16, "h_bf2", "w3_bf0"))
         history_gain(2)
-        apply_gain(h_bf[last][:, 0, :], h_act[last][:, 0, :], 0)
+        quantize_w3(1)
         history_quantize(2)
+        h_bf.append(sb([P, 2, PASS], BF16, "h_bf3", "w3_bf1"))
+        apply_gain(h_bf[last][:, 0, :], h_act[last][:, 0, :], 0)
         apply_gain(h_bf[last][:, 1, :], h_act[last][:, 1, :], 1)
         quantize(h_codes[last][:, 0, :], h_plane[last][:, 0, :], h_bf[last][:, 0, :])
         quantize(h_codes[last][:, 1, :], h_plane[last][:, 1, :], h_bf[last][:, 1, :])

@@ -47,19 +47,15 @@ def tile_list_parking_occupancy_kernel(
             return reuse.tile(shape, dtype, name=name, align_bytes=64, offset=offset)
 
         def load_scales(plane, scales):
-            rows = scales.bitcast(I32)
-            for quad in range(QUADS):
-                nc.sync.dma_start(
-                    out=plane[:].bitcast(I32)[32 * quad : 32 * quad + 4],
-                    in_=rows[:, 4 * quad : 4 * quad + 4, :].rearrange("a r c -> r a c"),
-                )
+            rows = scales.bitcast(I32).rearrange("a (q r) c -> r q a c", r=4)
+            for r in range(4):
+                nc.sync.dma_start(out=plane[:].bitcast(I32)[r:P:32], in_=rows[r])
 
-        def load_stacked_scales(plane, scales):
-            rows = scales.bitcast(I32)
-            for quad in range(QUADS):
+        def place_scales(a):
+            for r in range(4):
                 nc.sync.dma_start(
-                    out=plane[:].bitcast(I32)[32 * quad : 32 * quad + 8],
-                    in_=rows[:, 4 * quad : 4 * quad + 4, :],
+                    out=v1_plane[a][:].bitcast(I32)[r:P:32],
+                    in_=v1_rows[:].bitcast(I32)[8 * r + 4 * a : P : 32],
                 )
 
         list1 = keep.tile([P, S // 16], U16, name="list1")
@@ -72,11 +68,14 @@ def tile_list_parking_occupancy_kernel(
         w1_raw_plane = sb([P, 2, H], U8, "w1_raw_plane")
         w4_codes = sb([P, 2, N], U32, "w4_codes")
         w4_plane = sb([P, 2, N], U8, "w4_plane")
-        w2_raw = [sb([P, PACK, 256], F32, "w2_raw%d" % u) for u in range(4)]
+        w2_raw = [sb([P, PACK, 256], F32, "w2_raw%d" % u) for u in range(2)]
+        w2_late = sb([P, PACK, PASS], F32, "w2_late")
+        w2_raw.extend([w2_late[:, :, 0:256], w2_late[:, :, 256:512]])
         w3_raw = [sb([P, PACK, N], F32, "w3_raw%d" % a) for a in range(2)]
         gain_rows = sb([P, PASS], F32, "gain_rows")
         gain_slots = sb([P, PACK, P], F32, "gain_slots")
         v1_plane = [sb([P, S], U8, "v1_plane%d" % a) for a in range(2)]
+        v1_rows = sb([P, S], U8, "v1_rows")
         identity = sb([P, P], F32, "identity")
         warm = sb([P, 8], F32, "warm")
 
@@ -84,7 +83,8 @@ def tile_list_parking_occupancy_kernel(
         nc.vector.memset(t1_plane[:].bitcast(I32), 0)
         nc.vector.memset(w1_raw_plane[:].bitcast(I32), 0)
         nc.vector.memset(w4_plane[:].bitcast(I32), 0)
-        nc.vector.memset(v1_plane[1][:].bitcast(I32), 0)
+        for a in range(2):
+            nc.vector.memset(v1_plane[a][:].bitcast(I32), 0)
         nc.gpsimd.memset(warm[:], 0.0)
         nc.scalar.activation(warm[:, 4:5], warm[:, 0:1], ACT.Silu)
         nc.vector.memset(gain_slots[:], 0.0)
@@ -115,13 +115,12 @@ def tile_list_parking_occupancy_kernel(
         nc.sync.dma_start(list1[:], offs)
         nc.sync.dma_start(out=gain_rows[GS_ROW : GS_ROW + 2], in_=gs.rearrange("(a c) -> a c", a=2))
         nc.sync.dma_start(out=gain_rows[0:2], in_=gh.rearrange("(a c) -> a c", a=2))
-        load_w2(2)
-        load_stacked_scales(t1_plane, tab_scales)
-        load_w2(3)
+        for a in range(2):
+            nc.sync.dma_start(out=t1_plane[:].bitcast(I32)[4 * a : P : 8], in_=tab_scales[a].bitcast(I32))
+        nc.sync.dma_start(out=w2_late[:], in_=w2_rows[:, :, PASS : 2 * PASS])
         load_t1(0)
         load_scales(w1_raw_plane, w1_scales)
         nc.sync.dma_start(out=w1_raw[:], in_=w1_words.bitcast(I32).rearrange("a p c -> p a c"))
-        load_t1(1)
 
         v2_codes = sb([P, S], U16, "v2_codes")
         v2_plane = sb([P, S], U8, "v2_plane")
@@ -172,13 +171,15 @@ def tile_list_parking_occupancy_kernel(
         gains = held.tile([P, P, PACK], F32, name="gains")
         for t in range(PACK):
             nc.tensor.transpose(gains[:, :, t], gain_slots[:, t, :], identity[:])
-        nc.vector.tensor_copy(v1_plane[0][:], t1_plane[:].indirect(list1[:]))
-        nc.sync.dma_start(out=v1_plane[1][:].bitcast(I32)[0 : P - 4], in_=v1_plane[0][:].bitcast(I32)[4:P])
-        load_scales(w4_plane, w4_scales)
+        nc.vector.tensor_copy(v1_rows[:], t1_plane[:].indirect(list1[:]))
+        place_scales(0)
+        load_t1(1)
+        place_scales(1)
         nc.sync.dma_start(
             out=w4_codes[:].bitcast(I32),
             in_=w4_words.rearrange("a p c i -> p a (c i)").bitcast(I32),
         )
+        load_scales(w4_plane, w4_scales)
         load_w3(0)
         load_w3(1)
 
@@ -225,10 +226,9 @@ def tile_list_parking_occupancy_kernel(
         def second_gain():
             apply_gain(h2_second[:], h2_act[1][:], GS_ROW + 1)
 
-        round_w2(2, 0, 32, nc.scalar.copy)
         for q in range(NQ):
             sweep_unit(0, q)
-        round_w2(2, 32, 64, nc.scalar.copy)
+        round_w2(2, 0, 64, nc.scalar.copy)
         for m0 in (0, 32):
             round_w2(3, m0, m0 + 32, pool_round)
         first_gain(0, 2)

@@ -46,10 +46,10 @@ def tile_list_parking_occupancy_kernel(
         def over(shape, dtype, name, offset):
             return reuse.tile(shape, dtype, name=name, align_bytes=64, offset=offset)
 
-        def load_scales(plane, scales):
+        def load_scales(plane, scales, queue=nc.sync):
             rows = scales.bitcast(I32).rearrange("a (q r) c -> r q a c", r=4)
             for r in range(4):
-                nc.sync.dma_start(out=plane[:].bitcast(I32)[r:P:32], in_=rows[r])
+                queue.dma_start(out=plane[:].bitcast(I32)[r:P:32], in_=rows[r])
 
         def place_scales(a):
             for r in range(4):
@@ -72,7 +72,7 @@ def tile_list_parking_occupancy_kernel(
         w2_late = sb([P, PACK, PASS], F32, "w2_late")
         w2_raw.extend([w2_late[:, :, 0:256], w2_late[:, :, 256:512]])
         w3_raw = [sb([P, PACK, N], F32, "w3_raw%d" % a) for a in range(2)]
-        gain_rows = sb([P, PASS], F32, "gain_rows")
+        gain_rows = over([P, PASS], F32, "gain_rows", 14 * T)
         gain_slots = sb([P, PACK, P], F32, "gain_slots")
         v1_plane = [sb([P, S], U8, "v1_plane%d" % a) for a in range(2)]
         v1_rows = sb([P, S], U8, "v1_rows")
@@ -80,8 +80,8 @@ def tile_list_parking_occupancy_kernel(
         warm = sb([P, 8], F32, "warm")
 
         nc.gpsimd.memset(t2_plane[:].bitcast(I32), 0)
-        nc.vector.memset(t1_plane[:].bitcast(I32), 0)
         nc.vector.memset(w1_raw_plane[:].bitcast(I32), 0)
+        nc.vector.memset(t1_plane[:].bitcast(I32), 0)
         nc.vector.memset(w4_plane[:].bitcast(I32), 0)
         for a in range(2):
             nc.vector.memset(v1_plane[a][:].bitcast(I32), 0)
@@ -89,6 +89,7 @@ def tile_list_parking_occupancy_kernel(
         nc.scalar.activation(warm[:, 4:5], warm[:, 0:1], ACT.Silu)
         nc.vector.memset(gain_slots[:], 0.0)
         make_identity(nc, identity[:])
+        load_scales(w1_raw_plane, w1_scales, nc.gpsimd)
 
         w2_rows = w2.rearrange("(p j) c -> p j c", j=PACK)
 
@@ -103,10 +104,6 @@ def tile_list_parking_occupancy_kernel(
 
         w3_rows = w3.rearrange("(b g t e) n -> b t g e n", b=2, t=PACK, e=RUN)
 
-        def load_w3(b):
-            for t in range(PACK):
-                nc.sync.dma_start(out=w3_raw[b][:, t, :], in_=w3_rows[b, t])
-
         nc.sync.dma_start(out=t2_words[:].bitcast(I32), in_=tab2_words[0].bitcast(I32))
         nc.sync.dma_start(list2[:], offs2)
         load_scales(t2_plane, tab2_scales)
@@ -119,7 +116,6 @@ def tile_list_parking_occupancy_kernel(
             nc.sync.dma_start(out=t1_plane[:].bitcast(I32)[4 * a : P : 8], in_=tab_scales[a].bitcast(I32))
         nc.sync.dma_start(out=w2_late[:], in_=w2_rows[:, :, PASS : 2 * PASS])
         load_t1(0)
-        load_scales(w1_raw_plane, w1_scales)
         nc.sync.dma_start(out=w1_raw[:], in_=w1_words.bitcast(I32).rearrange("a p c -> p a c"))
 
         v2_codes = sb([P, S], U16, "v2_codes")
@@ -160,11 +156,11 @@ def tile_list_parking_occupancy_kernel(
         round_w2(1, 0, 32, nc.scalar.copy)
         round_w2(1, 32, 64, nc.vector.tensor_copy)
         quantize_w2(0)
-        pool_round(
+        nc.scalar.copy(
             gain_slots[GS_ROW : GS_ROW + 2],
             gain_rows[GS_ROW : GS_ROW + 2].rearrange("p (m t) -> p t m", t=PACK),
         )
-        pool_round(
+        nc.scalar.copy(
             gain_slots[0:2].rearrange("p t (g e) -> p t g e", e=RUN),
             gain_rows[0:2].rearrange("p (g t e) -> p t g e", t=PACK, e=RUN),
         )
@@ -179,14 +175,17 @@ def tile_list_parking_occupancy_kernel(
             out=w4_codes[:].bitcast(I32),
             in_=w4_words.rearrange("a p c i -> p a (c i)").bitcast(I32),
         )
-        load_scales(w4_plane, w4_scales)
-        load_w3(0)
-        load_w3(1)
+        w4_rows = w4_scales.bitcast(I32).rearrange("a (q r) c -> r q a c", r=4)
+        for piece in range(2 * PACK):
+            b, t = divmod(piece, PACK)
+            nc.sync.dma_start(out=w3_raw[b][:, t, :], in_=w3_rows[b, t])
+            if 1 <= piece <= 4:
+                nc.sync.dma_start(out=w4_plane[:].bitcast(I32)[piece - 1 : P : 32], in_=w4_rows[piece - 1])
 
-        h2_act = [sb([P, S * PACK], F32, "h2_act%d" % a) for a in range(2)]
+        h2_act = [over([P, S * PACK], F32, "h2_act0", 14 * T), sb([P, S * PACK], F32, "h2_act1")]
         h2_first = over([P, S * PACK], BF16, "h2_first", 8 * T)
-        h2_second = over([P, S * PACK], BF16, "h2_second", 4 * T)
-        h2_codes = [over([P, S], U32, "h2_codes0", 0), sb([P, S], U32, "h2_codes1")]
+        h2_second = [None, over([P, 2 * PASS], BF16, "h2_second1", 4 * T)]
+        h2_codes = [over([P, S], U32, "h2_codes0", 0), over([P, S], U32, "h2_codes1", 4 * T + 4096)]
         h2_plane = [sb([P, S], U8, "h2_plane%d" % a) for a in range(2)]
 
         def bank_tile(name, index):
@@ -223,8 +222,12 @@ def tile_list_parking_occupancy_kernel(
             cols = slice(PASS * q0, PASS * q1)
             apply_gain(h2_first[:, cols], h2_act[0][:, cols], GS_ROW)
 
-        def second_gain():
-            apply_gain(h2_second[:], h2_act[1][:], GS_ROW + 1)
+        def second_gain(u):
+            apply_gain(h2_second[u][:], h2_act[1][:, 2 * PASS * u : 2 * PASS * (u + 1)], GS_ROW + 1)
+
+        def second_quantize(u):
+            cols = slice(2 * SQ * u, 2 * SQ * (u + 1))
+            quantize(h2_codes[1][:, cols], h2_plane[1][:, cols], h2_second[u][:])
 
         for q in range(NQ):
             sweep_unit(0, q)
@@ -249,11 +252,14 @@ def tile_list_parking_occupancy_kernel(
             w1_raw_plane[:].bitcast(I32).rearrange("p a (b g t w) -> p (a b) g t w", t=PACK, g=16, w=2),
         )
         quantize(h2_codes[0][:], h2_plane[0][:], h2_first[:])
+        h2_second[0] = sb([P, 2 * PASS], BF16, "h2_second0", "w1_raw")
+        second_gain(0)
         for u in range(2):
             nc.vector.tensor_copy(
                 v1_codes[1][:, 256 * u : 256 * (u + 1)], t1_words[1][:].indirect(list1[:, 16 * u : 16 * (u + 1)])
             )
-        second_gain()
+        second_gain(1)
+        second_quantize(0)
 
         h_act = [sb([P, 2, PASS], F32, "h_act%d" % q) for q in range(NQ)]
         h_bf = [sb([P, 2, PASS], BF16, "h_bf%d" % q) for q in range(2)]
@@ -334,9 +340,10 @@ def tile_list_parking_occupancy_kernel(
         for n0 in range(0, N, 128):
             round_w3(0, n0, n0 + 128, pool_round)
         round_w3(1, 0, 128, pool_round)
-        round_w3(1, 128, N, nc.scalar.copy)
+        round_w3(1, 128, 256, pool_round)
+        round_w3(1, 256, N, nc.scalar.copy)
         history_gain(0)
-        quantize(h2_codes[1][:], h2_plane[1][:], h2_second[:])
+        second_quantize(1)
         for q in range(NQ):
             for a in range(2):
                 sweep_sum(q, a)

@@ -25,8 +25,7 @@ QUADS = 4
 SQ = 128
 NQ = S // SQ
 RUN = 8
-GS_ROW = 64
-RING = 7
+RING = 6
 AHEAD = 4
 
 
@@ -68,18 +67,17 @@ def tile_list_parking_occupancy_kernel(
         w1_raw_plane = sb([P, 2, H], U8, "w1_raw_plane")
         w4_codes = sb([P, 2, N], U32, "w4_codes")
         w4_plane = sb([P, 2, N], U8, "w4_plane")
-        w2_raw = [sb([P, PACK, 256], F32, "w2_raw%d" % u) for u in range(2)]
-        w2_late = sb([P, PACK, PASS], F32, "w2_late")
-        w2_raw.extend([w2_late[:, :, 0:256], w2_late[:, :, 256:512]])
+        w2_raw = [sb([P, PACK, PASS], F32, "w2_raw%d" % a) for a in range(2)]
         w3_raw = [sb([P, PACK, N], F32, "w3_raw%d" % a) for a in range(2)]
-        gain_rows = over([P, PASS], F32, "gain_rows", 14 * T)
-        gain_slots = sb([P, PACK, P], F32, "gain_slots")
+        gs_rows = sb([P, PASS], F32, "gs_rows")
+        gh_rows = sb([P, 2 * P], F32, "gh_rows")
         v1_plane = [sb([P, S], U8, "v1_plane%d" % a) for a in range(2)]
         v1_rows = sb([P, S], U8, "v1_rows")
         identity = sb([P, P], F32, "identity")
         warm = sb([P, 8], F32, "warm")
 
         nc.gpsimd.memset(t2_plane[:].bitcast(I32), 0)
+        nc.vector.memset(gs_rows[:], 0.0)
         nc.vector.memset(w1_raw_plane[:].bitcast(I32), 0)
         nc.vector.memset(t1_plane[:].bitcast(I32), 0)
         nc.vector.memset(w4_plane[:].bitcast(I32), 0)
@@ -87,14 +85,14 @@ def tile_list_parking_occupancy_kernel(
             nc.vector.memset(v1_plane[a][:].bitcast(I32), 0)
         nc.gpsimd.memset(warm[:], 0.0)
         nc.scalar.activation(warm[:, 4:5], warm[:, 0:1], ACT.Silu)
-        nc.vector.memset(gain_slots[:], 0.0)
+        nc.vector.memset(gh_rows[:], 0.0)
         make_identity(nc, identity[:])
         load_scales(w1_raw_plane, w1_scales, nc.gpsimd)
 
         w2_rows = w2.rearrange("(p j) c -> p j c", j=PACK)
 
-        def load_w2(u):
-            nc.sync.dma_start(out=w2_raw[u][:], in_=w2_rows[:, :, 256 * u : 256 * (u + 1)])
+        def load_w2(a):
+            nc.sync.dma_start(out=w2_raw[a][:], in_=w2_rows[:, :, PASS * a : PASS * (a + 1)])
 
         def load_t1(a):
             nc.sync.dma_start(
@@ -107,14 +105,16 @@ def tile_list_parking_occupancy_kernel(
         nc.sync.dma_start(out=t2_words[:].bitcast(I32), in_=tab2_words[0].bitcast(I32))
         nc.sync.dma_start(list2[:], offs2)
         load_scales(t2_plane, tab2_scales)
+        nc.sync.dma_start(out=gs_rows[0:2], in_=gs.rearrange("(a c) -> a c", a=2))
         load_w2(0)
-        load_w2(1)
         nc.sync.dma_start(list1[:], offs)
-        nc.sync.dma_start(out=gain_rows[GS_ROW : GS_ROW + 2], in_=gs.rearrange("(a c) -> a c", a=2))
-        nc.sync.dma_start(out=gain_rows[0:2], in_=gh.rearrange("(a c) -> a c", a=2))
         for a in range(2):
             nc.sync.dma_start(out=t1_plane[:].bitcast(I32)[4 * a : P : 8], in_=tab_scales[a].bitcast(I32))
-        nc.sync.dma_start(out=w2_late[:], in_=w2_rows[:, :, PASS : 2 * PASS])
+        load_w2(1)
+        nc.sync.dma_start(
+            out=gh_rows[0:PACK].rearrange("t (x e) -> t x e", e=RUN),
+            in_=gh.rearrange("(x t e) -> t x e", t=PACK, e=RUN),
+        )
         load_t1(0)
         nc.sync.dma_start(out=w1_raw[:], in_=w1_words.bitcast(I32).rearrange("a p c -> p a c"))
 
@@ -133,11 +133,10 @@ def tile_list_parking_occupancy_kernel(
         def pool_round(dst, src):
             nc.gpsimd.tensor_scalar(dst, src, 1.0, 0.0, MULT, ADD)
 
-        def round_w2(u, m0, m1, rounder):
-            base = 64 * (u % 2)
+        def round_w2(a, m0, m1, rounder):
             rounder(
-                w2_bf[u // 2][:, :, base + m0 : base + m1, :].rearrange("p t m j -> p m t j"),
-                w2_raw[u][:, :, PACK * m0 : PACK * m1].rearrange("p j (m t) -> p m t j", t=PACK),
+                w2_bf[a][:, :, m0:m1, :].rearrange("p t m j -> p m t j"),
+                w2_raw[a][:, :, PACK * m0 : PACK * m1].rearrange("p j (m t) -> p m t j", t=PACK),
             )
 
         def quantize(codes, plane, values):
@@ -152,21 +151,12 @@ def tile_list_parking_occupancy_kernel(
         def quantize_w3(b):
             quantize(w3_codes[b][:], w3_plane[b][:], w3_bf[b][:].rearrange("p n t -> p (n t)"))
 
-        round_w2(0, 0, 64, nc.scalar.copy)
-        round_w2(1, 0, 32, nc.scalar.copy)
-        round_w2(1, 32, 64, nc.vector.tensor_copy)
-        quantize_w2(0)
-        nc.scalar.copy(
-            gain_slots[GS_ROW : GS_ROW + 2],
-            gain_rows[GS_ROW : GS_ROW + 2].rearrange("p (m t) -> p t m", t=PACK),
-        )
-        nc.scalar.copy(
-            gain_slots[0:2].rearrange("p t (g e) -> p t g e", e=RUN),
-            gain_rows[0:2].rearrange("p (g t e) -> p t g e", t=PACK, e=RUN),
-        )
-        gains = held.tile([P, P, PACK], F32, name="gains")
+        sweep_gains = held.tile([P, PACK, P], F32, name="sweep_gains")
         for t in range(PACK):
-            nc.tensor.transpose(gains[:, :, t], gain_slots[:, t, :], identity[:])
+            nc.tensor.transpose(sweep_gains[:, t, :], gs_rows[:, t:PASS:PACK], identity[:])
+        round_w2(0, 0, 44, nc.scalar.copy)
+        round_w2(0, 44, P, nc.vector.tensor_copy)
+        quantize_w2(0)
         nc.vector.tensor_copy(v1_rows[:], t1_plane[:].indirect(list1[:]))
         place_scales(0)
         load_t1(1)
@@ -182,9 +172,11 @@ def tile_list_parking_occupancy_kernel(
             if 1 <= piece <= 4:
                 nc.sync.dma_start(out=w4_plane[:].bitcast(I32)[piece - 1 : P : 32], in_=w4_rows[piece - 1])
 
-        h2_act = [over([P, S * PACK], F32, "h2_act0", 14 * T), sb([P, S * PACK], F32, "h2_act1")]
+        h2_act = [sb([P, S * PACK], F32, "h2_act%d" % a) for a in range(2)]
         h2_first = over([P, S * PACK], BF16, "h2_first", 8 * T)
-        h2_second = [None, over([P, 2 * PASS], BF16, "h2_second1", 4 * T)]
+        h2_second = [over([P, 2 * PASS], BF16, "h2_second0", 4 * T), sb([P, 2 * PASS], BF16, "h2_second1")]
+        pool_gain = sb([P, 1, PACK], F32, "pool_gain")
+        nc.scalar.copy(pool_gain[:], sweep_gains[:, :, 1:2].rearrange("p t a -> p a t"))
         h2_codes = [over([P, S], U32, "h2_codes0", 0), over([P, S], U32, "h2_codes1", 4 * T + 4096)]
         h2_plane = [sb([P, S], U8, "h2_plane%d" % a) for a in range(2)]
 
@@ -196,12 +188,12 @@ def tile_list_parking_occupancy_kernel(
                 dst.rearrange("p (s t) -> p s t", t=PACK), bank[:].rearrange("p t s -> p s t"), func
             )
 
-        def apply_gain(dst, src, row):
+        def apply_gain(dst, src, gain):
             width = src.shape[1] // PACK
             nc.vector.tensor_tensor(
                 dst.rearrange("p (s t) -> p s t", t=PACK),
                 src.rearrange("p (s t) -> p s t", t=PACK),
-                gains[:, row : row + 1, :].to_broadcast([P, width, PACK]),
+                gain.to_broadcast([P, width, PACK]),
                 MULT,
             )
 
@@ -220,10 +212,13 @@ def tile_list_parking_occupancy_kernel(
 
         def first_gain(q0, q1):
             cols = slice(PASS * q0, PASS * q1)
-            apply_gain(h2_first[:, cols], h2_act[0][:, cols], GS_ROW)
+            apply_gain(h2_first[:, cols], h2_act[0][:, cols], sweep_gains[:, :, 0:1].rearrange("p t a -> p a t"))
 
         def second_gain(u):
-            apply_gain(h2_second[u][:], h2_act[1][:, 2 * PASS * u : 2 * PASS * (u + 1)], GS_ROW + 1)
+            apply_gain(
+                h2_second[u][:], h2_act[1][:, 2 * PASS * u : 2 * PASS * (u + 1)],
+                sweep_gains[:, :, 1:2].rearrange("p t a -> p a t"),
+            )
 
         def second_quantize(u):
             cols = slice(2 * SQ * u, 2 * SQ * (u + 1))
@@ -231,17 +226,21 @@ def tile_list_parking_occupancy_kernel(
 
         for q in range(NQ):
             sweep_unit(0, q)
-        round_w2(2, 0, 64, nc.scalar.copy)
-        for m0 in (0, 32):
-            round_w2(3, m0, m0 + 32, pool_round)
-        first_gain(0, 2)
+        round_w2(1, 0, 32, nc.scalar.copy)
+        for m0 in (32, 64, 96):
+            round_w2(1, m0, m0 + 32, pool_round)
+        history_gains = held.tile([P, 2, P], F32, name="history_gains")
+        for b in range(2):
+            nc.tensor.transpose(history_gains[:, b, :], gh_rows[:, P * b : P * (b + 1)], identity[:])
+        first_gain(0, 1)
+        first_gain(1, 2)
         first_gain(2, 4)
         quantize_w2(1)
         for q in range(NQ):
             sweep_unit(1, q)
-        v1_codes = [over([P, S], U32, "v1_codes0", 10 * T + 4096), sb([P, S], U32, "v1_codes1")]
-        w1_codes = sb([P, 2 * 2 * H], U8, "w1_codes")
-        w1_plane = sb([P, 2 * H], U8, "w1_plane")
+        v1_codes = [over([P, S], U32, "v1_codes0", 10 * T + 3072), sb([P, S], U32, "v1_codes1")]
+        w1_codes = over([P, 2 * 2 * H], U8, "w1_codes", 10 * T + 7168)
+        w1_plane = over([P, 2 * H], U8, "w1_plane", 10 * T + 5120)
         nc.vector.tensor_copy(v1_codes[0][:], t1_words[0][:].indirect(list1[:]))
         nc.vector.tensor_copy(
             w1_codes[:].bitcast(I32).rearrange("p (x t g w) -> p x g t w", t=PACK, g=16, w=4),
@@ -252,14 +251,19 @@ def tile_list_parking_occupancy_kernel(
             w1_raw_plane[:].bitcast(I32).rearrange("p a (b g t w) -> p (a b) g t w", t=PACK, g=16, w=2),
         )
         quantize(h2_codes[0][:], h2_plane[0][:], h2_first[:])
-        h2_second[0] = sb([P, 2 * PASS], BF16, "h2_second0", "w1_raw")
-        second_gain(0)
         for u in range(2):
             nc.vector.tensor_copy(
                 v1_codes[1][:, 256 * u : 256 * (u + 1)], t1_words[1][:].indirect(list1[:, 16 * u : 16 * (u + 1)])
             )
-        second_gain(1)
-        second_quantize(0)
+        second_gain(0)
+        for q in (2, 3):
+            nc.gpsimd.tensor_tensor(
+                h2_second[1][:, PASS * (q - 2) : PASS * (q - 1)].rearrange("p (s t) -> p s t", t=PACK),
+                h2_act[1][:, PASS * q : PASS * (q + 1)].rearrange("p (s t) -> p s t", t=PACK),
+                pool_gain[:].to_broadcast([P, SQ, PACK]),
+                MULT,
+            )
+        second_quantize(1)
 
         h_act = [sb([P, 2, PASS], F32, "h_act%d" % q) for q in range(NQ)]
         h_bf = [sb([P, 2, PASS], BF16, "h_bf%d" % q) for q in range(2)]
@@ -289,7 +293,7 @@ def tile_list_parking_occupancy_kernel(
             nc.vector.tensor_tensor(
                 h_bf[q][:].rearrange("p b (s t) -> p b s t", t=PACK),
                 h_act[q][:].rearrange("p b (s t) -> p b s t", t=PACK),
-                gains[:, 0:2, :].unsqueeze(2).to_broadcast([P, 2, SQ, PACK]),
+                history_gains[:, :, 0:PACK].unsqueeze(2).to_broadcast([P, 2, SQ, PACK]),
                 MULT,
             )
 
@@ -302,7 +306,7 @@ def tile_list_parking_occupancy_kernel(
 
         def sweep_sum(q, a):
             if a == 0:
-                sums.append(bank_tile("sums%d" % q, q + 1))
+                sums.append(bank_tile("sums%d" % q, q + 2))
             cols = slice(SQ * q, SQ * (q + 1))
             for i in range(N // P):
                 slots = slice(P * i, P * (i + 1))
@@ -343,7 +347,7 @@ def tile_list_parking_occupancy_kernel(
         round_w3(1, 128, 256, pool_round)
         round_w3(1, 256, N, nc.scalar.copy)
         history_gain(0)
-        second_quantize(1)
+        second_quantize(0)
         for q in range(NQ):
             for a in range(2):
                 sweep_sum(q, a)
@@ -356,8 +360,8 @@ def tile_list_parking_occupancy_kernel(
         quantize_w3(1)
         history_quantize(2)
         h_bf.append(sb([P, 2, PASS], BF16, "h_bf3", "w3_bf1"))
-        apply_gain(h_bf[last][:, 0, :], h_act[last][:, 0, :], 0)
-        apply_gain(h_bf[last][:, 1, :], h_act[last][:, 1, :], 1)
+        apply_gain(h_bf[last][:, 0, :], h_act[last][:, 0, :], history_gains[:, 0:1, 0:PACK])
+        apply_gain(h_bf[last][:, 1, :], h_act[last][:, 1, :], history_gains[:, 1:2, 0:PACK])
         quantize(h_codes[last][:, 0, :], h_plane[last][:, 0, :], h_bf[last][:, 0, :])
         quantize(h_codes[last][:, 1, :], h_plane[last][:, 1, :], h_bf[last][:, 1, :])
         for q in range(NQ):

@@ -45,10 +45,10 @@ def tile_list_parking_occupancy_kernel(
         def over(shape, dtype, name, offset):
             return reuse.tile(shape, dtype, name=name, align_bytes=64, offset=offset)
 
-        def load_scales(plane, scales, queue=nc.sync):
+        def load_scales(plane, scales):
             rows = scales.bitcast(I32).rearrange("a (q r) c -> r q a c", r=4)
             for r in range(4):
-                queue.dma_start(out=plane[:].bitcast(I32)[r:P:32], in_=rows[r])
+                nc.sync.dma_start(out=plane[:].bitcast(I32)[r:P:32], in_=rows[r])
 
         def place_scales(a):
             for r in range(4):
@@ -67,7 +67,9 @@ def tile_list_parking_occupancy_kernel(
         w1_raw_plane = sb([P, 2, H], U8, "w1_raw_plane")
         w4_codes = sb([P, 2, N], U32, "w4_codes")
         w4_plane = sb([P, 2, N], U8, "w4_plane")
-        w2_raw = [sb([P, PACK, PASS], F32, "w2_raw%d" % a) for a in range(2)]
+        w2_first = sb([P, PACK, PASS], F32, "w2_first")
+        w2_third = over([P, PACK, PASS // 2], F32, "w2_third", 17 * T)
+        w2_fourth = sb([P, PACK, PASS // 2], F32, "w2_fourth")
         w3_raw = [sb([P, PACK, N], F32, "w3_raw%d" % a) for a in range(2)]
         gs_rows = sb([P, PASS], F32, "gs_rows")
         gh_rows = sb([P, 2 * P], F32, "gh_rows")
@@ -87,12 +89,11 @@ def tile_list_parking_occupancy_kernel(
         nc.scalar.activation(warm[:, 4:5], warm[:, 0:1], ACT.Silu)
         nc.vector.memset(gh_rows[:], 0.0)
         make_identity(nc, identity[:])
-        load_scales(w1_raw_plane, w1_scales, nc.gpsimd)
 
         w2_rows = w2.rearrange("(p j) c -> p j c", j=PACK)
 
-        def load_w2(a):
-            nc.sync.dma_start(out=w2_raw[a][:], in_=w2_rows[:, :, PASS * a : PASS * (a + 1)])
+        def load_w2(raw, c0):
+            nc.sync.dma_start(out=raw[:], in_=w2_rows[:, :, c0 : c0 + raw.shape[2]])
 
         def load_t1(a):
             nc.sync.dma_start(
@@ -106,16 +107,18 @@ def tile_list_parking_occupancy_kernel(
         nc.sync.dma_start(list2[:], offs2)
         load_scales(t2_plane, tab2_scales)
         nc.sync.dma_start(out=gs_rows[0:2], in_=gs.rearrange("(a c) -> a c", a=2))
-        load_w2(0)
+        load_w2(w2_first, 0)
         nc.sync.dma_start(list1[:], offs)
         for a in range(2):
             nc.sync.dma_start(out=t1_plane[:].bitcast(I32)[4 * a : P : 8], in_=tab_scales[a].bitcast(I32))
-        load_w2(1)
+        load_w2(w2_third, PASS)
+        load_w2(w2_fourth, PASS + PASS // 2)
         nc.sync.dma_start(
             out=gh_rows[0:PACK].rearrange("t (x e) -> t x e", e=RUN),
             in_=gh.rearrange("(x t e) -> t x e", t=PACK, e=RUN),
         )
         load_t1(0)
+        load_scales(w1_raw_plane, w1_scales)
         nc.sync.dma_start(out=w1_raw[:], in_=w1_words.bitcast(I32).rearrange("a p c -> p a c"))
 
         v2_codes = sb([P, S], U16, "v2_codes")
@@ -123,20 +126,19 @@ def tile_list_parking_occupancy_kernel(
         nc.vector.tensor_copy(v2_codes[:], t2_words[:].indirect(list2[:]))
         nc.vector.tensor_copy(v2_plane[:], t2_plane[:, 0, :].indirect(list2[:]))
 
-        w2_bf = [over([P, PACK, P, PACK], BF16, "w2_bf%d" % a, 10 * T + 4096 * a) for a in range(2)]
+        w2_bf = [over([P, PACK, P, PACK], BF16, "w2_bf%d" % a, 11 * T + 4096 * a) for a in range(2)]
         w2_codes = [sb([P, PASS], U32, "w2_codes%d" % a) for a in range(2)]
         w2_plane = [sb([P, PASS], U8, "w2_plane%d" % a) for a in range(2)]
-        w3_bf = [sb([P, N, PACK], BF16, "w3_bf%d" % b) for b in range(2)]
         w3_codes = [sb([P, N], U32, "w3_codes%d" % b) for b in range(2)]
         w3_plane = [sb([P, N], U8, "w3_plane%d" % b) for b in range(2)]
 
         def pool_round(dst, src):
             nc.gpsimd.tensor_scalar(dst, src, 1.0, 0.0, MULT, ADD)
 
-        def round_w2(a, m0, m1, rounder):
+        def round_w2(a, raw, base, m0, m1, rounder):
             rounder(
-                w2_bf[a][:, :, m0:m1, :].rearrange("p t m j -> p m t j"),
-                w2_raw[a][:, :, PACK * m0 : PACK * m1].rearrange("p j (m t) -> p m t j", t=PACK),
+                w2_bf[a][:, :, base + m0 : base + m1, :].rearrange("p t m j -> p m t j"),
+                raw[:, :, PACK * m0 : PACK * m1].rearrange("p j (m t) -> p m t j", t=PACK),
             )
 
         def quantize(codes, plane, values):
@@ -151,11 +153,11 @@ def tile_list_parking_occupancy_kernel(
         def quantize_w3(b):
             quantize(w3_codes[b][:], w3_plane[b][:], w3_bf[b][:].rearrange("p n t -> p (n t)"))
 
-        sweep_gains = held.tile([P, PACK, P], F32, name="sweep_gains")
+        sweep_gains = held.tile([P, P, PACK], F32, name="sweep_gains")
         for t in range(PACK):
-            nc.tensor.transpose(sweep_gains[:, t, :], gs_rows[:, t:PASS:PACK], identity[:])
-        round_w2(0, 0, 44, nc.scalar.copy)
-        round_w2(0, 44, P, nc.vector.tensor_copy)
+            nc.tensor.transpose(sweep_gains[:, :, t], gs_rows[:, t:PASS:PACK], identity[:])
+        round_w2(0, w2_first, 0, 0, 44, nc.scalar.copy)
+        round_w2(0, w2_first, 0, 44, P, nc.vector.tensor_copy)
         quantize_w2(0)
         nc.vector.tensor_copy(v1_rows[:], t1_plane[:].indirect(list1[:]))
         place_scales(0)
@@ -172,12 +174,12 @@ def tile_list_parking_occupancy_kernel(
             if 1 <= piece <= 4:
                 nc.sync.dma_start(out=w4_plane[:].bitcast(I32)[piece - 1 : P : 32], in_=w4_rows[piece - 1])
 
-        h2_act = [sb([P, S * PACK], F32, "h2_act%d" % a) for a in range(2)]
+        round_w2(1, w2_third, 0, 0, 64, nc.scalar.copy)
+        h2_act = [over([P, S * PACK], F32, "h2_act0", 17 * T), sb([P, S * PACK], F32, "h2_act1")]
         h2_first = over([P, S * PACK], BF16, "h2_first", 8 * T)
-        h2_second = [over([P, 2 * PASS], BF16, "h2_second0", 4 * T), sb([P, 2 * PASS], BF16, "h2_second1")]
-        pool_gain = sb([P, 1, PACK], F32, "pool_gain")
-        nc.scalar.copy(pool_gain[:], sweep_gains[:, :, 1:2].rearrange("p t a -> p a t"))
-        h2_codes = [over([P, S], U32, "h2_codes0", 0), over([P, S], U32, "h2_codes1", 4 * T + 4096)]
+        pool_gain = sb([P, 2, PACK], F32, "pool_gain")
+        nc.scalar.copy(pool_gain[:], sweep_gains[:, 0:2, :])
+        h2_codes = [None, over([P, S], U32, "h2_codes1", 4 * T + 4096)]
         h2_plane = [sb([P, S], U8, "h2_plane%d" % a) for a in range(2)]
 
         def bank_tile(name, index):
@@ -210,37 +212,36 @@ def tile_list_parking_occupancy_kernel(
                 )
             activate(h2_act[a][:, PASS * q : PASS * (q + 1)], bank, ACT.Silu)
 
-        def first_gain(q0, q1):
-            cols = slice(PASS * q0, PASS * q1)
-            apply_gain(h2_first[:, cols], h2_act[0][:, cols], sweep_gains[:, :, 0:1].rearrange("p t a -> p a t"))
-
-        def second_gain(u):
-            apply_gain(
-                h2_second[u][:], h2_act[1][:, 2 * PASS * u : 2 * PASS * (u + 1)],
-                sweep_gains[:, :, 1:2].rearrange("p t a -> p a t"),
+        def pool_apply_gain(dst, a, q):
+            cols = slice(PASS * q, PASS * (q + 1))
+            nc.gpsimd.tensor_tensor(
+                dst[:, cols].rearrange("p (s t) -> p s t", t=PACK),
+                h2_act[a][:, cols].rearrange("p (s t) -> p s t", t=PACK),
+                pool_gain[:, a : a + 1, :].to_broadcast([P, SQ, PACK]),
+                MULT,
             )
 
-        def second_quantize(u):
-            cols = slice(2 * SQ * u, 2 * SQ * (u + 1))
-            quantize(h2_codes[1][:, cols], h2_plane[1][:, cols], h2_second[u][:])
+        def first_gain(q0, q1):
+            cols = slice(PASS * q0, PASS * q1)
+            apply_gain(h2_first[:, cols], h2_act[0][:, cols], sweep_gains[:, 0:1, :])
 
         for q in range(NQ):
             sweep_unit(0, q)
-        round_w2(1, 0, 32, nc.scalar.copy)
-        for m0 in (32, 64, 96):
-            round_w2(1, m0, m0 + 32, pool_round)
+        for m0 in (0, 32):
+            round_w2(1, w2_fourth, 64, m0, m0 + 32, pool_round)
         history_gains = held.tile([P, 2, P], F32, name="history_gains")
         for b in range(2):
             nc.tensor.transpose(history_gains[:, b, :], gh_rows[:, P * b : P * (b + 1)], identity[:])
         first_gain(0, 1)
         first_gain(1, 2)
-        first_gain(2, 4)
         quantize_w2(1)
+        first_gain(2, 3)
+        pool_apply_gain(h2_first, 0, 3)
         for q in range(NQ):
             sweep_unit(1, q)
-        v1_codes = [over([P, S], U32, "v1_codes0", 10 * T + 3072), sb([P, S], U32, "v1_codes1")]
-        w1_codes = over([P, 2 * 2 * H], U8, "w1_codes", 10 * T + 7168)
-        w1_plane = over([P, 2 * H], U8, "w1_plane", 10 * T + 5120)
+        v1_codes = [over([P, S], U32, "v1_codes0", 11 * T + 3072), sb([P, S], U32, "v1_codes1")]
+        w1_codes = over([P, 2 * 2 * H], U8, "w1_codes", 11 * T + 7168)
+        w1_plane = over([P, 2 * H], U8, "w1_plane", 11 * T + 5120)
         nc.vector.tensor_copy(v1_codes[0][:], t1_words[0][:].indirect(list1[:]))
         nc.vector.tensor_copy(
             w1_codes[:].bitcast(I32).rearrange("p (x t g w) -> p x g t w", t=PACK, g=16, w=4),
@@ -250,23 +251,22 @@ def tile_list_parking_occupancy_kernel(
             w1_plane[:].bitcast(I32).rearrange("p (x t g w) -> p x g t w", t=PACK, g=16, w=2),
             w1_raw_plane[:].bitcast(I32).rearrange("p a (b g t w) -> p (a b) g t w", t=PACK, g=16, w=2),
         )
+        h2_codes[0] = sb([P, S], U32, "h2_codes0", "w1_raw")
         quantize(h2_codes[0][:], h2_plane[0][:], h2_first[:])
+        stage = over([P, 5 * PASS], BF16, "stage", 8 * T)
+        w3_bf = [stage[:, 0 : 4 * PASS].rearrange("p (n t) -> p n t", t=PACK), sb([P, N, PACK], BF16, "w3_bf1")]
+        apply_gain(stage[:, 0 : 2 * PASS], h2_act[1][:, 0 : 2 * PASS], sweep_gains[:, 1:2, :])
+        for q in (2, 3):
+            pool_apply_gain(stage, 1, q)
         for u in range(2):
             nc.vector.tensor_copy(
                 v1_codes[1][:, 256 * u : 256 * (u + 1)], t1_words[1][:].indirect(list1[:, 16 * u : 16 * (u + 1)])
             )
-        second_gain(0)
-        for q in (2, 3):
-            nc.gpsimd.tensor_tensor(
-                h2_second[1][:, PASS * (q - 2) : PASS * (q - 1)].rearrange("p (s t) -> p s t", t=PACK),
-                h2_act[1][:, PASS * q : PASS * (q + 1)].rearrange("p (s t) -> p s t", t=PACK),
-                pool_gain[:].to_broadcast([P, SQ, PACK]),
-                MULT,
-            )
-        second_quantize(1)
+        quantize(h2_codes[1][:], h2_plane[1][:], stage[:, 0 : 4 * PASS])
 
         h_act = [sb([P, 2, PASS], F32, "h_act%d" % q) for q in range(NQ)]
-        h_bf = [sb([P, 2, PASS], BF16, "h_bf%d" % q) for q in range(2)]
+        h_bf = [stage[:, 3 * PASS : 5 * PASS].rearrange("p (b s) -> p b s", b=2)]
+        h_bf.extend(sb([P, 2, PASS], BF16, "h_bf%d" % q) for q in (1, 2))
         h_codes = [sb([P, 2, SQ], U32, "h_codes%d" % q) for q in range(NQ)]
         h_plane = [sb([P, 2, SQ], U8, "h_plane%d" % q) for q in range(NQ)]
         sums = []
@@ -275,7 +275,7 @@ def tile_list_parking_occupancy_kernel(
         def history_pass(unit, a):
             q, b = divmod(unit, 2)
             if a == 0:
-                banks[unit] = bank_tile("history%d" % unit, unit)
+                banks[unit] = bank_tile("history%d" % unit, unit + 1)
             cols = slice(SQ * q, SQ * (q + 1))
             for t in range(PACK):
                 c0 = H * a + PASS * b + P * t
@@ -306,7 +306,7 @@ def tile_list_parking_occupancy_kernel(
 
         def sweep_sum(q, a):
             if a == 0:
-                sums.append(bank_tile("sums%d" % q, q + 2))
+                sums.append(bank_tile("sums%d" % q, q + 3))
             cols = slice(SQ * q, SQ * (q + 1))
             for i in range(N // P):
                 slots = slice(P * i, P * (i + 1))
@@ -331,8 +331,10 @@ def tile_list_parking_occupancy_kernel(
 
         def finish(q):
             prob = sb([P, N // P, SQ], F32, "prob%d" % q)
-            nc.scalar.activation(prob[:], sums[q][:], ACT.Sigmoid)
-            nc.sync.dma_start(out=out_rows[:, :, SQ * q : SQ * (q + 1)], in_=prob[:])
+            parts = ((0, 2, nc.sync), (2, 4, nc.scalar)) if q == NQ - 1 else ((0, 4, nc.sync),)
+            for i0, i1, queue in parts:
+                nc.scalar.activation(prob[:, i0:i1, :], sums[q][:, i0:i1, :], ACT.Sigmoid)
+                queue.dma_start(out=out_rows[:, i0:i1, SQ * q : SQ * (q + 1)], in_=prob[:, i0:i1, :])
 
         last = NQ - 1
         for unit in range(AHEAD):
@@ -341,27 +343,24 @@ def tile_list_parking_occupancy_kernel(
             if unit >= AHEAD:
                 history_pass(unit, 0)
             history_pass(unit, 1)
-        for n0 in range(0, N, 128):
-            round_w3(0, n0, n0 + 128, pool_round)
-        round_w3(1, 0, 128, pool_round)
-        round_w3(1, 128, 256, pool_round)
-        round_w3(1, 256, N, nc.scalar.copy)
-        history_gain(0)
-        second_quantize(0)
         for q in range(NQ):
             for a in range(2):
                 sweep_sum(q, a)
+        history_gain(0)
+        for n0 in range(0, 384, 128):
+            round_w3(0, n0, n0 + 128, pool_round)
+        round_w3(1, 0, N, nc.scalar.copy)
         history_gain(1)
         history_quantize(0)
-        quantize_w3(0)
-        history_quantize(1)
-        h_bf.append(sb([P, 2, PASS], BF16, "h_bf2", "w3_bf0"))
+        round_w3(0, 384, N, pool_round)
         history_gain(2)
+        history_quantize(1)
+        quantize_w3(0)
         quantize_w3(1)
-        history_quantize(2)
         h_bf.append(sb([P, 2, PASS], BF16, "h_bf3", "w3_bf1"))
         apply_gain(h_bf[last][:, 0, :], h_act[last][:, 0, :], history_gains[:, 0:1, 0:PACK])
         apply_gain(h_bf[last][:, 1, :], h_act[last][:, 1, :], history_gains[:, 1:2, 0:PACK])
+        history_quantize(2)
         quantize(h_codes[last][:, 0, :], h_plane[last][:, 0, :], h_bf[last][:, 0, :])
         quantize(h_codes[last][:, 1, :], h_plane[last][:, 1, :], h_bf[last][:, 1, :])
         for q in range(NQ):

@@ -23,10 +23,10 @@ PACK = 4
 PASS = P * PACK
 QUADS = 4
 SQ = 128
-NQ = S // SQ
+HALF = S // 2
 RUN = 8
 RING = 6
-AHEAD = 4
+AHEAD = 3
 
 
 def tile_list_parking_occupancy_kernel(
@@ -175,71 +175,63 @@ def tile_list_parking_occupancy_kernel(
                 nc.sync.dma_start(out=w4_plane[:].bitcast(I32)[piece - 1 : P : 32], in_=w4_rows[piece - 1])
 
         round_w2(1, w2_third, 0, 0, 64, nc.scalar.copy)
-        h2_act = [over([P, S * PACK], F32, "h2_act0", 17 * T), sb([P, S * PACK], F32, "h2_act1")]
+        h2_act = [over([P, PACK, S], F32, "h2_act0", 17 * T), sb([P, PACK, S], F32, "h2_act1")]
         h2_first = over([P, S * PACK], BF16, "h2_first", 8 * T)
+        h2_second = [over([P, HALF * PACK], BF16, "h2_second%d" % u, 4 * T + 4 * T * u) for u in range(1)]
+        h2_second.append(over([P, HALF * PACK], BF16, "h2_second1", 2 * T))
         pool_gain = sb([P, 2, PACK], F32, "pool_gain")
         nc.scalar.copy(pool_gain[:], sweep_gains[:, 0:2, :])
-        h2_codes = [None, over([P, S], U32, "h2_codes1", 4 * T + 4096)]
+        h2_codes = [over([P, S], U32, "h2_codes%d" % a, (6 + a) * T) for a in range(2)]
         h2_plane = [sb([P, S], U8, "h2_plane%d" % a) for a in range(2)]
 
-        def bank_tile(name, index):
-            return held.tile([P, PACK, SQ], F32, name=name, tag="bank%d" % (index % RING))
+        def bank_tile(name, index, shape):
+            return held.tile(shape, F32, name=name, tag="bank%d" % (index % RING))
 
-        def activate(dst, bank, func):
-            nc.scalar.activation(
-                dst.rearrange("p (s t) -> p s t", t=PACK), bank[:].rearrange("p t s -> p s t"), func
-            )
-
-        def apply_gain(dst, src, gain):
-            width = src.shape[1] // PACK
+        def apply_gain(dst, act, s0, s1, gain):
+            pairs = (s1 - s0) // 2
             nc.vector.tensor_tensor(
-                dst.rearrange("p (s t) -> p s t", t=PACK),
-                src.rearrange("p (s t) -> p s t", t=PACK),
-                gain.to_broadcast([P, width, PACK]),
+                dst.rearrange("p (c i t) -> p c t i", i=2, t=PACK),
+                act[:, :, s0:s1].rearrange("p t (c i) -> p c t i", i=2),
+                gain.unsqueeze(3).to_broadcast([P, pairs, PACK, 2]),
                 MULT,
             )
 
-        def sweep_unit(a, q):
-            bank = bank_tile("sweep%d%d" % (a, q), NQ * a + q + RING - 1)
-            cols = slice(SQ * q, SQ * (q + 1))
-            for t in range(PACK):
-                chan = slice(P * t, P * (t + 1))
-                nc.tensor.matmul_mx(
-                    out=bank[:, t, :],
-                    lhsT=w2_codes[a][:, chan].bitcast(FP8X4), lhsT_scale=w2_plane[a][:, chan],
-                    rhs=v2_codes[:, cols].bitcast(FP4X4), rhs_scale=v2_plane[:, cols],
-                    start=True, stop=True,
-                )
-            activate(h2_act[a][:, PASS * q : PASS * (q + 1)], bank, ACT.Silu)
-
-        def pool_apply_gain(dst, a, q):
-            cols = slice(PASS * q, PASS * (q + 1))
+        def pool_apply_gain(dst, a, s0):
             nc.gpsimd.tensor_tensor(
-                dst[:, cols].rearrange("p (s t) -> p s t", t=PACK),
-                h2_act[a][:, cols].rearrange("p (s t) -> p s t", t=PACK),
+                dst.rearrange("p (s t) -> p s t", t=PACK),
+                h2_act[a][:, :, s0 : s0 + SQ].rearrange("p t s -> p s t"),
                 pool_gain[:, a : a + 1, :].to_broadcast([P, SQ, PACK]),
                 MULT,
             )
 
-        def first_gain(q0, q1):
-            cols = slice(PASS * q0, PASS * q1)
-            apply_gain(h2_first[:, cols], h2_act[0][:, cols], sweep_gains[:, 0:1, :])
+        def sweep_unit(a, unit):
+            half, u = divmod(unit, 2)
+            bank = bank_tile("sweep%d%d" % (a, unit), 4 * a + unit + RING - 1, [P, 2, HALF])
+            cols = slice(HALF * half, HALF * (half + 1))
+            for v in range(2):
+                chan = slice(P * (2 * u + v), P * (2 * u + v + 1))
+                nc.tensor.matmul_mx(
+                    out=bank[:, v, :],
+                    lhsT=w2_codes[a][:, chan].bitcast(FP8X4), lhsT_scale=w2_plane[a][:, chan],
+                    rhs=v2_codes[:, cols].bitcast(FP4X4), rhs_scale=v2_plane[:, cols],
+                    start=True, stop=True,
+                )
+            nc.scalar.activation(h2_act[a][:, 2 * u : 2 * u + 2, cols], bank[:], ACT.Silu)
 
-        for q in range(NQ):
-            sweep_unit(0, q)
+        for unit in range(4):
+            sweep_unit(0, unit)
         for m0 in (0, 32):
             round_w2(1, w2_fourth, 64, m0, m0 + 32, pool_round)
         history_gains = held.tile([P, 2, P], F32, name="history_gains")
         for b in range(2):
             nc.tensor.transpose(history_gains[:, b, :], gh_rows[:, P * b : P * (b + 1)], identity[:])
-        first_gain(0, 1)
-        first_gain(1, 2)
+        apply_gain(h2_first[:, 0 : 2 * PASS], h2_act[0], 0, HALF, sweep_gains[:, 0:1, :])
         quantize_w2(1)
-        first_gain(2, 3)
-        pool_apply_gain(h2_first, 0, 3)
-        for q in range(NQ):
-            sweep_unit(1, q)
-        v1_codes = [over([P, S], U32, "v1_codes0", 11 * T + 3072), sb([P, S], U32, "v1_codes1")]
+        apply_gain(h2_first[:, 2 * PASS : 3 * PASS], h2_act[0], HALF, 3 * SQ, sweep_gains[:, 0:1, :])
+        pool_apply_gain(h2_first[:, 3 * PASS : 4 * PASS], 0, 3 * SQ)
+        for unit in range(4):
+            sweep_unit(1, unit)
+        v1_codes = [over([P, S], U32, "v1_codes0", 11 * T + 3072)]
         w1_codes = over([P, 2 * 2 * H], U8, "w1_codes", 11 * T + 7168)
         w1_plane = over([P, 2 * H], U8, "w1_plane", 11 * T + 5120)
         nc.vector.tensor_copy(v1_codes[0][:], t1_words[0][:].indirect(list1[:]))
@@ -251,119 +243,96 @@ def tile_list_parking_occupancy_kernel(
             w1_plane[:].bitcast(I32).rearrange("p (x t g w) -> p x g t w", t=PACK, g=16, w=2),
             w1_raw_plane[:].bitcast(I32).rearrange("p a (b g t w) -> p (a b) g t w", t=PACK, g=16, w=2),
         )
-        h2_codes[0] = sb([P, S], U32, "h2_codes0", "w1_raw")
+        v1_codes.append(sb([P, S], U32, "v1_codes1", "w1_raw"))
+        nc.vector.tensor_copy(v1_codes[1][:], t1_words[1][:].indirect(list1[:]))
+        for s0 in (HALF, HALF + SQ):
+            words = slice(PACK * (s0 - HALF), PACK * (s0 - HALF + SQ))
+            pool_apply_gain(h2_second[1][:, words], 1, s0)
+        apply_gain(h2_second[0][:], h2_act[1], 0, HALF, sweep_gains[:, 1:2, :])
         quantize(h2_codes[0][:], h2_plane[0][:], h2_first[:])
-        stage = over([P, 5 * PASS], BF16, "stage", 8 * T)
-        w3_bf = [stage[:, 0 : 4 * PASS].rearrange("p (n t) -> p n t", t=PACK), sb([P, N, PACK], BF16, "w3_bf1")]
-        apply_gain(stage[:, 0 : 2 * PASS], h2_act[1][:, 0 : 2 * PASS], sweep_gains[:, 1:2, :])
-        for q in (2, 3):
-            pool_apply_gain(stage, 1, q)
         for u in range(2):
-            nc.vector.tensor_copy(
-                v1_codes[1][:, 256 * u : 256 * (u + 1)], t1_words[1][:].indirect(list1[:, 16 * u : 16 * (u + 1)])
-            )
-        quantize(h2_codes[1][:], h2_plane[1][:], stage[:, 0 : 4 * PASS])
+            cols = slice(HALF * u, HALF * (u + 1))
+            quantize(h2_codes[1][:, cols], h2_plane[1][:, cols], h2_second[u][:])
 
-        h_act = [sb([P, 2, PASS], F32, "h_act%d" % q) for q in range(NQ)]
-        h_bf = [stage[:, 3 * PASS : 5 * PASS].rearrange("p (b s) -> p b s", b=2)]
-        h_bf.extend(sb([P, 2, PASS], BF16, "h_bf%d" % q) for q in (1, 2))
-        h_codes = [sb([P, 2, SQ], U32, "h_codes%d" % q) for q in range(NQ)]
-        h_plane = [sb([P, 2, SQ], U8, "h_plane%d" % q) for q in range(NQ)]
-        sums = []
+        h_act = [sb([P, PACK, S], F32, "h_act%d" % b) for b in range(2)]
+        h_codes = [sb([P, S], U32, "h_codes%d" % b) for b in range(2)]
+        h_plane = [sb([P, S], U8, "h_plane%d" % b) for b in range(2)]
         banks = {}
 
-        def history_pass(unit, a):
-            q, b = divmod(unit, 2)
-            if a == 0:
-                banks[unit] = bank_tile("history%d" % unit, unit + 1)
-            cols = slice(SQ * q, SQ * (q + 1))
-            for t in range(PACK):
-                c0 = H * a + PASS * b + P * t
-                nc.tensor.matmul_mx(
-                    out=banks[unit][:, t, :],
-                    lhsT=w1_codes[:, 2 * c0 : 2 * (c0 + P)].bitcast(FP4X4),
-                    lhsT_scale=w1_plane[:, c0 : c0 + P],
-                    rhs=v1_codes[a][:, cols].bitcast(FP8X4), rhs_scale=v1_plane[a][:, cols],
-                    start=(a == 0 and t == 0), stop=(a == 1 and t == PACK - 1),
-                )
-            if a == 1:
-                activate(h_act[q][:, b, :], banks[unit], ACT.Gelu_apprx_tanh)
-
-        def history_gain(q):
-            nc.vector.tensor_tensor(
-                h_bf[q][:].rearrange("p b (s t) -> p b s t", t=PACK),
-                h_act[q][:].rearrange("p b (s t) -> p b s t", t=PACK),
-                history_gains[:, :, 0:PACK].unsqueeze(2).to_broadcast([P, 2, SQ, PACK]),
-                MULT,
+        def history_pass(unit, a, first):
+            b, t = divmod(unit, PACK)
+            if first:
+                banks[unit] = bank_tile("history%d" % unit, unit + 1, [P, S])
+            c0 = H * a + PASS * b + P * t
+            nc.tensor.matmul_mx(
+                out=banks[unit][:],
+                lhsT=w1_codes[:, 2 * c0 : 2 * (c0 + P)].bitcast(FP4X4),
+                lhsT_scale=w1_plane[:, c0 : c0 + P],
+                rhs=v1_codes[a][:].bitcast(FP8X4), rhs_scale=v1_plane[a][:],
+                start=first, stop=not first,
             )
+            if not first:
+                nc.scalar.activation(h_act[b][:, t, :], banks[unit][:], ACT.Gelu_apprx_tanh)
 
-        def history_quantize(q):
-            quantize(
-                h_codes[q][:].rearrange("p b s -> p (b s)"),
-                h_plane[q][:].rearrange("p b s -> p (b s)"),
-                h_bf[q][:].rearrange("p b s -> p (b s)"),
-            )
+        for unit in range(AHEAD):
+            history_pass(unit, 0, True)
+        for unit in range(2 * PACK):
+            history_pass(unit, 1, unit >= AHEAD)
+            if unit >= AHEAD:
+                history_pass(unit, 0, False)
 
-        def sweep_sum(q, a):
-            if a == 0:
-                sums.append(bank_tile("sums%d" % q, q + 3))
-            cols = slice(SQ * q, SQ * (q + 1))
-            for i in range(N // P):
-                slots = slice(P * i, P * (i + 1))
+        parts = [(0, HALF, 0, 2), (0, HALF, 2, 2), (HALF, SQ, 0, 4), (HALF + SQ, SQ, 0, 4)]
+        sums = [bank_tile("sums%d" % k, k + 3, [P, part[3], part[1]]) for k, part in enumerate(parts)]
+
+        def add_passes(k, weights, weight_plane, codes, plane, first, final):
+            s0, width, i0, tiles = parts[k]
+            for i in range(tiles):
+                slots = slice(P * (i0 + i), P * (i0 + i + 1))
                 nc.tensor.matmul_mx(
-                    out=sums[q][:, i, :],
-                    lhsT=w4_codes[:, a, slots].bitcast(FP8X4), lhsT_scale=w4_plane[:, a, slots],
-                    rhs=h2_codes[a][:, cols].bitcast(FP8X4), rhs_scale=h2_plane[a][:, cols],
-                    start=(a == 0 and i == 0), stop=False,
+                    out=sums[k][:, i, :],
+                    lhsT=weights[:, slots].bitcast(FP8X4), lhsT_scale=weight_plane[:, slots],
+                    rhs=codes[:, s0 : s0 + width].bitcast(FP8X4), rhs_scale=plane[:, s0 : s0 + width],
+                    start=(first and i == 0), stop=(final and i == tiles - 1),
                 )
 
-        def history_sum(q, b):
-            for i in range(N // P):
-                slots = slice(P * i, P * (i + 1))
-                nc.tensor.matmul_mx(
-                    out=sums[q][:, i, :],
-                    lhsT=w3_codes[b][:, slots].bitcast(FP8X4), lhsT_scale=w3_plane[b][:, slots],
-                    rhs=h_codes[q][:, b, :].bitcast(FP8X4), rhs_scale=h_plane[q][:, b, :],
-                    start=False, stop=(b == 1 and i == N // P - 1),
-                )
+        for k in range(len(parts)):
+            for a in range(2):
+                add_passes(k, w4_codes[:, a, :], w4_plane[:, a, :], h2_codes[a], h2_plane[a], a == 0, False)
+
+        w3_bf = [over([P, N, PACK], BF16, "w3_bf0", 3 * T - 64), sb([P, N, PACK], BF16, "w3_bf1")]
+        for n0 in range(0, N, 128):
+            round_w3(0, n0, n0 + 128, pool_round)
+        round_w3(1, 0, 128, pool_round)
+        round_w3(1, 128, N, nc.scalar.copy)
+
+        def history_gain(dst, b, s0, s1):
+            apply_gain(dst, h_act[b], s0, s1, history_gains[:, b : b + 1, 0:PACK])
+
+        def history_quantize(b, s0, s1, values):
+            quantize(h_codes[b][:, s0:s1], h_plane[b][:, s0:s1], values)
+
+        h_first = sb([P, S * PACK], BF16, "h_first")
+        history_gain(h_first[:, 0 : 2 * PASS], 0, 0, HALF)
+        history_gain(h_first[:, 2 * PASS : 4 * PASS], 0, HALF, S)
+        history_quantize(0, 0, S, h_first[:])
+        h_half = sb([P, HALF * PACK], BF16, "h_half")
+        history_gain(h_half[:], 1, 0, HALF)
+        quantize_w3(0)
+        history_quantize(1, 0, HALF, h_half[:])
+        quantize_w3(1)
+        h_last = sb([P, HALF * PACK], BF16, "h_last", "w3_bf1")
+        history_gain(h_last[:, 0:PASS], 1, HALF, HALF + SQ)
+        history_gain(h_last[:, PASS : 2 * PASS], 1, HALF + SQ, S)
+        history_quantize(1, HALF, HALF + SQ, h_last[:, 0:PASS])
+        history_quantize(1, HALF + SQ, S, h_last[:, PASS : 2 * PASS])
 
         out_rows = out.rearrange("(i p) s -> p i s", p=P)
-
-        def finish(q):
-            prob = sb([P, N // P, SQ], F32, "prob%d" % q)
-            parts = ((0, 2, nc.sync), (2, 4, nc.scalar)) if q == NQ - 1 else ((0, 4, nc.sync),)
-            for i0, i1, queue in parts:
-                nc.scalar.activation(prob[:, i0:i1, :], sums[q][:, i0:i1, :], ACT.Sigmoid)
-                queue.dma_start(out=out_rows[:, i0:i1, SQ * q : SQ * (q + 1)], in_=prob[:, i0:i1, :])
-
-        last = NQ - 1
-        for unit in range(AHEAD):
-            history_pass(unit, 0)
-        for unit in range(2 * NQ):
-            if unit >= AHEAD:
-                history_pass(unit, 0)
-            history_pass(unit, 1)
-        for q in range(NQ):
-            for a in range(2):
-                sweep_sum(q, a)
-        history_gain(0)
-        for n0 in range(0, 384, 128):
-            round_w3(0, n0, n0 + 128, pool_round)
-        round_w3(1, 0, N, nc.scalar.copy)
-        history_gain(1)
-        history_quantize(0)
-        round_w3(0, 384, N, pool_round)
-        history_gain(2)
-        history_quantize(1)
-        quantize_w3(0)
-        quantize_w3(1)
-        h_bf.append(sb([P, 2, PASS], BF16, "h_bf3", "w3_bf1"))
-        apply_gain(h_bf[last][:, 0, :], h_act[last][:, 0, :], history_gains[:, 0:1, 0:PACK])
-        apply_gain(h_bf[last][:, 1, :], h_act[last][:, 1, :], history_gains[:, 1:2, 0:PACK])
-        history_quantize(2)
-        quantize(h_codes[last][:, 0, :], h_plane[last][:, 0, :], h_bf[last][:, 0, :])
-        quantize(h_codes[last][:, 1, :], h_plane[last][:, 1, :], h_bf[last][:, 1, :])
-        for q in range(NQ):
-            for b in range(2):
-                history_sum(q, b)
-            finish(q)
+        for k in range(len(parts)):
+            add_passes(k, w3_codes[0], w3_plane[0], h_codes[0], h_plane[0], False, False)
+        for k, (s0, width, i0, tiles) in enumerate(parts):
+            add_passes(k, w3_codes[1], w3_plane[1], h_codes[1], h_plane[1], False, True)
+            prob = sb([P, tiles, width], F32, "prob%d" % k)
+            pieces = ((0, 2, nc.sync), (2, 4, nc.scalar)) if k == len(parts) - 1 else ((0, tiles, nc.sync),)
+            for j0, j1, queue in pieces:
+                nc.scalar.activation(prob[:, j0:j1, :], sums[k][:, j0:j1, :], ACT.Sigmoid)
+                queue.dma_start(out=out_rows[:, i0 + j0 : i0 + j1, s0 : s0 + width], in_=prob[:, j0:j1, :])

@@ -76,7 +76,6 @@ def tile_list_parking_occupancy_kernel(
         v1_plane = [sb([P, S], U8, "v1_plane%d" % a) for a in range(2)]
         v1_rows = sb([P, S], U8, "v1_rows")
         identity = sb([P, P], F32, "identity")
-        warm = sb([P, 8], F32, "warm")
 
         nc.gpsimd.memset(t2_plane[:].bitcast(I32), 0)
         nc.vector.memset(gs_rows[:], 0.0)
@@ -85,9 +84,9 @@ def tile_list_parking_occupancy_kernel(
         nc.vector.memset(w4_plane[:].bitcast(I32), 0)
         for a in range(2):
             nc.vector.memset(v1_plane[a][:].bitcast(I32), 0)
-        nc.gpsimd.memset(warm[:], 0.0)
-        nc.scalar.activation(warm[:, 4:5], warm[:, 0:1], ACT.Silu)
-        nc.vector.memset(gh_rows[:], 0.0)
+        zero = sb([P, 1], F32, "zero")
+        nc.gpsimd.memset(zero[:], 0.0)
+        nc.scalar.activation(gh_rows[:], zero[:].to_broadcast([P, 2 * P]), ACT.Silu)
         make_identity(nc, identity[:])
 
         w2_rows = w2.rearrange("(p j) c -> p j c", j=PACK)

@@ -21,12 +21,14 @@ ADD = mybir.AluOpType.add
 P = 128
 PACK = 4
 PASS = P * PACK
-QUADS = 4
 SQ = 128
 HALF = S // 2
 RUN = 8
 RING = 6
-AHEAD = 3
+AHEAD = 4
+W2_SCALAR = 44
+W3_SCALAR = 352
+KIB = 1024
 
 
 def tile_list_parking_occupancy_kernel(
@@ -39,38 +41,35 @@ def tile_list_parking_occupancy_kernel(
         reuse = ctx.enter_context(tc.tile_pool(name="reuse", bufs=1))
         held = ctx.enter_context(tc.psum_pool(name="held", bufs=1))
 
-        def sb(shape, dtype, name, tag=None):
-            return keep.tile(shape, dtype, name=name, tag=tag or name, align_bytes=64)
+        def sb(shape, dtype, name):
+            return keep.tile(shape, dtype, name=name, align_bytes=64)
 
-        def over(shape, dtype, name, offset):
-            return reuse.tile(shape, dtype, name=name, align_bytes=64, offset=offset)
+        def over(shape, dtype, name, kib):
+            return reuse.tile(shape, dtype, name=name, align_bytes=64, offset=kib * KIB)
 
-        def load_scales(plane, scales):
+        def load_scale_row(plane, scales, r, first):
             rows = scales.bitcast(I32).rearrange("a (q r) c -> r q a c", r=4)
-            for r in range(4):
-                nc.sync.dma_start(out=plane[:].bitcast(I32)[r:P:32], in_=rows[r])
+            nc.sync.dma_start(out=plane[:].bitcast(I32)[first + r : P : 32], in_=rows[r])
 
         def place_scales(a):
             for r in range(4):
                 nc.sync.dma_start(
                     out=v1_plane[a][:].bitcast(I32)[r:P:32],
-                    in_=v1_rows[:].bitcast(I32)[8 * r + 4 * a : P : 32],
+                    in_=v1_rows[:].bitcast(I32)[64 * a + 4 * r : 64 * (a + 1) : 16],
                 )
 
         list1 = keep.tile([P, S // 16], U16, name="list1")
         list2 = keep.tile([P, S // 16], U16, name="list2")
         t2_words = sb([P, T2], U16, "t2_words")
         t2_plane = sb([P, 1, T2], U8, "t2_plane")
-        t1_words = [over([P, T], U32, "t1_words%d" % a, 4 * T * a) for a in range(2)]
-        t1_plane = over([P, T], U8, "t1_plane", 8 * T)
-        w1_raw = sb([P, 2, H // 2], I32, "w1_raw")
+        t1_words = [sb([P, T], U32, "t1_words%d" % a) for a in range(2)]
+        t1_plane = sb([P, T], U8, "t1_plane")
+        w1_raw = [over([P, H // 2], I32, "w1_raw0", 32), over([P, H // 2], I32, "w1_raw1", 1)]
         w1_raw_plane = sb([P, 2, H], U8, "w1_raw_plane")
-        w4_codes = sb([P, 2, N], U32, "w4_codes")
+        w4_codes = [sb([P, N], U32, "w4_codes%d" % a) for a in range(2)]
         w4_plane = sb([P, 2, N], U8, "w4_plane")
-        w2_first = sb([P, PACK, PASS], F32, "w2_first")
-        w2_third = over([P, PACK, PASS // 2], F32, "w2_third", 17 * T)
-        w2_fourth = sb([P, PACK, PASS // 2], F32, "w2_fourth")
-        w3_raw = [sb([P, PACK, N], F32, "w3_raw%d" % a) for a in range(2)]
+        w2_raw = [sb([P, PACK, PASS], F32, "w2_raw%d" % a) for a in range(2)]
+        w3_raw = [sb([P, PACK, N], F32, "w3_raw0"), over([P, PACK, N], F32, "w3_raw1", 16)]
         gs_rows = sb([P, PASS], F32, "gs_rows")
         gh_rows = sb([P, 2 * P], F32, "gh_rows")
         v1_plane = [sb([P, S], U8, "v1_plane%d" % a) for a in range(2)]
@@ -79,54 +78,57 @@ def tile_list_parking_occupancy_kernel(
 
         nc.gpsimd.memset(t2_plane[:].bitcast(I32), 0)
         nc.vector.memset(gs_rows[:], 0.0)
-        nc.vector.memset(w1_raw_plane[:].bitcast(I32), 0)
         nc.vector.memset(t1_plane[:].bitcast(I32), 0)
-        nc.vector.memset(w4_plane[:].bitcast(I32), 0)
+        nc.vector.memset(w1_raw_plane[:].bitcast(I32), 0)
         for a in range(2):
             nc.vector.memset(v1_plane[a][:].bitcast(I32), 0)
+        nc.vector.memset(w4_plane[:].bitcast(I32), 0)
         zero = sb([P, 1], F32, "zero")
         nc.gpsimd.memset(zero[:], 0.0)
         nc.scalar.activation(gh_rows[:], zero[:].to_broadcast([P, 2 * P]), ACT.Silu)
         make_identity(nc, identity[:])
 
         w2_rows = w2.rearrange("(p j) c -> p j c", j=PACK)
-
-        def load_w2(raw, c0):
-            nc.sync.dma_start(out=raw[:], in_=w2_rows[:, :, c0 : c0 + raw.shape[2]])
-
-        def load_t1(a):
-            nc.sync.dma_start(
-                out=t1_words[a][:].bitcast(I32),
-                in_=tab_words[a].rearrange("p t i -> p (t i)").bitcast(I32),
-            )
-
         w3_rows = w3.rearrange("(b g t e) n -> b t g e n", b=2, t=PACK, e=RUN)
+
+        def load_w2(a):
+            nc.sync.dma_start(out=w2_raw[a][:], in_=w2_rows[:, :, PASS * a : PASS * (a + 1)])
+
+        def load_words(tile, words):
+            nc.sync.dma_start(out=tile[:].bitcast(I32), in_=words.rearrange("p c i -> p (c i)").bitcast(I32))
+
+        def load_w1(a):
+            nc.sync.dma_start(out=w1_raw[a][:], in_=w1_words[a].bitcast(I32))
+
+        def load_w3(b, t):
+            nc.sync.dma_start(out=w3_raw[b][:, t, :], in_=w3_rows[b, t])
 
         nc.sync.dma_start(out=t2_words[:].bitcast(I32), in_=tab2_words[0].bitcast(I32))
         nc.sync.dma_start(list2[:], offs2)
-        load_scales(t2_plane, tab2_scales)
+        for r in range(4):
+            load_scale_row(t2_plane, tab2_scales, r, 0)
         nc.sync.dma_start(out=gs_rows[0:2], in_=gs.rearrange("(a c) -> a c", a=2))
-        load_w2(w2_first, 0)
+        load_w2(0)
         nc.sync.dma_start(list1[:], offs)
-        for a in range(2):
-            nc.sync.dma_start(out=t1_plane[:].bitcast(I32)[4 * a : P : 8], in_=tab_scales[a].bitcast(I32))
-        load_w2(w2_third, PASS)
-        load_w2(w2_fourth, PASS + PASS // 2)
+        nc.sync.dma_start(
+            out=t1_plane[:].bitcast(I32)[0:P:4], in_=tab_scales.bitcast(I32).rearrange("a q c -> (a q) c")
+        )
+        load_w2(1)
         nc.sync.dma_start(
             out=gh_rows[0:PACK].rearrange("t (x e) -> t x e", e=RUN),
             in_=gh.rearrange("(x t e) -> t x e", t=PACK, e=RUN),
         )
-        load_t1(0)
-        load_scales(w1_raw_plane, w1_scales)
-        nc.sync.dma_start(out=w1_raw[:], in_=w1_words.bitcast(I32).rearrange("a p c -> p a c"))
+        for r in range(4):
+            load_scale_row(w1_raw_plane, w1_scales, r, 0)
+        load_words(t1_words[0], tab_words[0])
 
         v2_codes = sb([P, S], U16, "v2_codes")
         v2_plane = sb([P, S], U8, "v2_plane")
         nc.vector.tensor_copy(v2_codes[:], t2_words[:].indirect(list2[:]))
         nc.vector.tensor_copy(v2_plane[:], t2_plane[:, 0, :].indirect(list2[:]))
 
-        w2_bf = [over([P, PACK, P, PACK], BF16, "w2_bf%d" % a, 11 * T + 4096 * a) for a in range(2)]
-        w2_codes = [sb([P, PASS], U32, "w2_codes%d" % a) for a in range(2)]
+        w2_bf = [sb([P, PACK, P, PACK], BF16, "w2_bf%d" % a) for a in range(2)]
+        w2_codes = [over([P, PASS], U32, "w2_codes0", 24), sb([P, PASS], U32, "w2_codes1")]
         w2_plane = [sb([P, PASS], U8, "w2_plane%d" % a) for a in range(2)]
         w3_codes = [sb([P, N], U32, "w3_codes%d" % b) for b in range(2)]
         w3_plane = [sb([P, N], U8, "w3_plane%d" % b) for b in range(2)]
@@ -134,10 +136,10 @@ def tile_list_parking_occupancy_kernel(
         def pool_round(dst, src):
             nc.gpsimd.tensor_scalar(dst, src, 1.0, 0.0, MULT, ADD)
 
-        def round_w2(a, raw, base, m0, m1, rounder):
-            rounder(
-                w2_bf[a][:, :, base + m0 : base + m1, :].rearrange("p t m j -> p m t j"),
-                raw[:, :, PACK * m0 : PACK * m1].rearrange("p j (m t) -> p m t j", t=PACK),
+        def w2_views(a):
+            return (
+                w2_bf[a][:].rearrange("p (u e) m j -> p m u j e", e=2),
+                w2_raw[a][:].rearrange("p j (m u e) -> p m u j e", u=2, e=2),
             )
 
         def quantize(codes, plane, values):
@@ -147,7 +149,10 @@ def tile_list_parking_occupancy_kernel(
             quantize(w2_codes[a][:], w2_plane[a][:], w2_bf[a][:].rearrange("p t m j -> p (t m j)"))
 
         def round_w3(b, n0, n1, rounder):
-            rounder(w3_bf[b][:, n0:n1, :], w3_raw[b][:, :, n0:n1].rearrange("p t n -> p n t"))
+            rounder(
+                w3_bf[b][:, n0:n1, :].rearrange("p (c i) t -> p c t i", i=2),
+                w3_raw[b][:, :, n0:n1].rearrange("p t (c i) -> p c t i", i=2),
+            )
 
         def quantize_w3(b):
             quantize(w3_codes[b][:], w3_plane[b][:], w3_bf[b][:].rearrange("p n t -> p (n t)"))
@@ -155,57 +160,62 @@ def tile_list_parking_occupancy_kernel(
         sweep_gains = held.tile([P, P, PACK], F32, name="sweep_gains")
         for t in range(PACK):
             nc.tensor.transpose(sweep_gains[:, :, t], gs_rows[:, t:PASS:PACK], identity[:])
-        round_w2(0, w2_first, 0, 0, 44, nc.scalar.copy)
-        round_w2(0, w2_first, 0, 44, P, nc.vector.tensor_copy)
+        dst, src = w2_views(0)
+        nc.scalar.copy(dst[:, 0:W2_SCALAR], src[:, 0:W2_SCALAR])
+        nc.vector.tensor_copy(dst[:, W2_SCALAR:P], src[:, W2_SCALAR:P])
         quantize_w2(0)
         nc.vector.tensor_copy(v1_rows[:], t1_plane[:].indirect(list1[:]))
         place_scales(0)
-        load_t1(1)
+        load_w1(0)
+        load_words(t1_words[1], tab_words[1])
         place_scales(1)
-        nc.sync.dma_start(
-            out=w4_codes[:].bitcast(I32),
-            in_=w4_words.rearrange("a p c i -> p a (c i)").bitcast(I32),
-        )
-        w4_rows = w4_scales.bitcast(I32).rearrange("a (q r) c -> r q a c", r=4)
-        for piece in range(2 * PACK):
-            b, t = divmod(piece, PACK)
-            nc.sync.dma_start(out=w3_raw[b][:, t, :], in_=w3_rows[b, t])
-            if 1 <= piece <= 4:
-                nc.sync.dma_start(out=w4_plane[:].bitcast(I32)[piece - 1 : P : 32], in_=w4_rows[piece - 1])
+        load_w1(1)
+        for t in range(PACK):
+            load_w3(0, t)
+        load_words(w4_codes[0], w4_words[0])
+        for r in range(2):
+            load_scale_row(w4_plane, w4_scales, r, 4)
+        load_w3(1, 0)
+        for r in range(2, 4):
+            load_scale_row(w4_plane, w4_scales, r, 4)
+        for t in range(1, PACK):
+            load_w3(1, t)
+        load_words(w4_codes[1], w4_words[1])
 
-        round_w2(1, w2_third, 0, 0, 64, nc.scalar.copy)
-        h2_act = [over([P, PACK, S], F32, "h2_act0", 17 * T), sb([P, PACK, S], F32, "h2_act1")]
-        h2_first = over([P, S * PACK], BF16, "h2_first", 8 * T)
-        h2_second = [over([P, HALF * PACK], BF16, "h2_second%d" % u, 4 * T + 4 * T * u) for u in range(1)]
-        h2_second.append(over([P, HALF * PACK], BF16, "h2_second1", 2 * T))
-        pool_gain = sb([P, 2, PACK], F32, "pool_gain")
-        nc.scalar.copy(pool_gain[:], sweep_gains[:, 0:2, :])
-        h2_codes = [over([P, S], U32, "h2_codes%d" % a, (6 + a) * T) for a in range(2)]
+        pool_gain = sb([P, PACK], F32, "pool_gain")
+        nc.scalar.copy(pool_gain[:], sweep_gains[:, 1, :])
+        for m0 in (0, 32, 64):
+            pool_round(
+                w2_bf[1][:, :, m0 : m0 + 32, :].rearrange("p t m j -> p m t j"),
+                w2_raw[1][:, :, PACK * m0 : PACK * (m0 + 32)].rearrange("p j (m t) -> p m t j", t=PACK),
+            )
+
+        h2_act = [[sb([P, PACK, HALF], F32, "h2_act%d%d" % (a, u)) for u in range(2)] for a in range(2)]
+        h2_codes = [over([P, S], U32, "h2_codes0", 32), over([P, S], U32, "h2_codes1", 0)]
         h2_plane = [sb([P, S], U8, "h2_plane%d" % a) for a in range(2)]
 
         def bank_tile(name, index, shape):
             return held.tile(shape, F32, name=name, tag="bank%d" % (index % RING))
 
-        def apply_gain(dst, act, s0, s1, gain):
-            pairs = (s1 - s0) // 2
+        def apply_gain(dst, act, gain):
             nc.vector.tensor_tensor(
                 dst.rearrange("p (c i t) -> p c t i", i=2, t=PACK),
-                act[:, :, s0:s1].rearrange("p t (c i) -> p c t i", i=2),
-                gain.unsqueeze(3).to_broadcast([P, pairs, PACK, 2]),
+                act.rearrange("p t (c i) -> p c t i", i=2),
+                gain.unsqueeze(1).unsqueeze(3).to_broadcast([P, act.shape[2] // 2, PACK, 2]),
                 MULT,
             )
 
-        def pool_apply_gain(dst, a, s0):
+        def pool_apply_gain(dst, act):
             nc.gpsimd.tensor_tensor(
                 dst.rearrange("p (s t) -> p s t", t=PACK),
-                h2_act[a][:, :, s0 : s0 + SQ].rearrange("p t s -> p s t"),
-                pool_gain[:, a : a + 1, :].to_broadcast([P, SQ, PACK]),
+                act.rearrange("p t s -> p s t"),
+                pool_gain[:].unsqueeze(1).to_broadcast([P, SQ, PACK]),
                 MULT,
             )
 
         def sweep_unit(a, unit):
             half, u = divmod(unit, 2)
-            bank = bank_tile("sweep%d%d" % (a, unit), 4 * a + unit + RING - 1, [P, 2, HALF])
+            bank = bank_tile("sweep%d%d" % (a, unit), 4 * a + unit, [P, 2, HALF])
             cols = slice(HALF * half, HALF * (half + 1))
             for v in range(2):
                 chan = slice(P * (2 * u + v), P * (2 * u + v + 1))
@@ -215,73 +225,81 @@ def tile_list_parking_occupancy_kernel(
                     rhs=v2_codes[:, cols].bitcast(FP4X4), rhs_scale=v2_plane[:, cols],
                     start=True, stop=True,
                 )
-            nc.scalar.activation(h2_act[a][:, 2 * u : 2 * u + 2, cols], bank[:], ACT.Silu)
+            nc.scalar.activation(h2_act[a][half][:, 2 * u : 2 * u + 2, :], bank[:], ACT.Silu)
 
         for unit in range(4):
             sweep_unit(0, unit)
-        for m0 in (0, 32):
-            round_w2(1, w2_fourth, 64, m0, m0 + 32, pool_round)
+        dst, src = w2_views(1)
+        nc.scalar.copy(dst[:, 96:P], src[:, 96:P])
+        w1_plane = over([P, 2 * H], U8, "w1_plane", 24)
+        nc.scalar.copy(
+            w1_plane[:].bitcast(U32).rearrange("p (x t g w) -> p x g t w", t=PACK, g=16, w=2),
+            w1_raw_plane[:].bitcast(U32).rearrange("p a (b g t w) -> p (a b) g t w", t=PACK, g=16, w=2),
+        )
         history_gains = held.tile([P, 2, P], F32, name="history_gains")
         for b in range(2):
             nc.tensor.transpose(history_gains[:, b, :], gh_rows[:, P * b : P * (b + 1)], identity[:])
-        apply_gain(h2_first[:, 0 : 2 * PASS], h2_act[0], 0, HALF, sweep_gains[:, 0:1, :])
+        h2_first = over([P, S * PACK], BF16, "h2_first", 28)
+        for half in range(2):
+            apply_gain(h2_first[:, 2 * PASS * half : 2 * PASS * (half + 1)], h2_act[0][half][:], sweep_gains[:, 0, :])
         quantize_w2(1)
-        apply_gain(h2_first[:, 2 * PASS : 3 * PASS], h2_act[0], HALF, 3 * SQ, sweep_gains[:, 0:1, :])
-        pool_apply_gain(h2_first[:, 3 * PASS : 4 * PASS], 0, 3 * SQ)
         for unit in range(4):
             sweep_unit(1, unit)
-        v1_codes = [over([P, S], U32, "v1_codes0", 11 * T + 3072)]
-        w1_codes = over([P, 2 * 2 * H], U8, "w1_codes", 11 * T + 7168)
-        w1_plane = over([P, 2 * H], U8, "w1_plane", 11 * T + 5120)
-        nc.vector.tensor_copy(v1_codes[0][:], t1_words[0][:].indirect(list1[:]))
-        nc.vector.tensor_copy(
-            w1_codes[:].bitcast(I32).rearrange("p (x t g w) -> p x g t w", t=PACK, g=16, w=4),
-            w1_raw[:].rearrange("p a (b g t w) -> p (a b) g t w", t=PACK, g=16, w=4),
-        )
-        nc.vector.tensor_copy(
-            w1_plane[:].bitcast(I32).rearrange("p (x t g w) -> p x g t w", t=PACK, g=16, w=2),
-            w1_raw_plane[:].bitcast(I32).rearrange("p a (b g t w) -> p (a b) g t w", t=PACK, g=16, w=2),
-        )
-        v1_codes.append(sb([P, S], U32, "v1_codes1", "w1_raw"))
-        nc.vector.tensor_copy(v1_codes[1][:], t1_words[1][:].indirect(list1[:]))
-        for s0 in (HALF, HALF + SQ):
-            words = slice(PACK * (s0 - HALF), PACK * (s0 - HALF + SQ))
-            pool_apply_gain(h2_second[1][:, words], 1, s0)
-        apply_gain(h2_second[0][:], h2_act[1], 0, HALF, sweep_gains[:, 1:2, :])
-        quantize(h2_codes[0][:], h2_plane[0][:], h2_first[:])
-        for u in range(2):
-            cols = slice(HALF * u, HALF * (u + 1))
-            quantize(h2_codes[1][:, cols], h2_plane[1][:, cols], h2_second[u][:])
 
-        h_act = [sb([P, PACK, S], F32, "h_act%d" % b) for b in range(2)]
+        v1_codes = [sb([P, S], U32, "v1_codes0"), over([P, S], U32, "v1_codes1", 8)]
+        w1_codes = [sb([P, 2 * H], U8, "w1_codes%d" % a) for a in range(2)]
+
+        def order_w1(a):
+            nc.vector.tensor_copy(
+                w1_codes[a][:].bitcast(I32).rearrange("p (b t g w) -> p b g t w", t=PACK, g=16, w=4),
+                w1_raw[a][:].rearrange("p (b g t w) -> p b g t w", t=PACK, g=16, w=4),
+            )
+
+        nc.vector.tensor_copy(v1_codes[0][:], t1_words[0][:].indirect(list1[:]))
+        order_w1(0)
+        quantize(h2_codes[0][:], h2_plane[0][:], h2_first[:])
+        h2_quarter = over([P, SQ * PACK], BF16, "h2_quarter", 28)
+        pool_apply_gain(h2_quarter[:], h2_act[1][0][:, :, 0:SQ])
+        nc.vector.tensor_copy(v1_codes[1][:], t1_words[1][:].indirect(list1[:]))
+        order_w1(1)
+        h2_rest = over([P, 3 * SQ * PACK], BF16, "h2_rest", 2)
+        pool_apply_gain(h2_rest[:, 0:PASS], h2_act[1][0][:, :, SQ:HALF])
+        apply_gain(h2_rest[:, PASS : 3 * PASS], h2_act[1][1][:], sweep_gains[:, 1, :])
+        quantize(h2_codes[1][:, 0:SQ], h2_plane[1][:, 0:SQ], h2_quarter[:])
+        quantize(h2_codes[1][:, SQ:S], h2_plane[1][:, SQ:S], h2_rest[:])
+
+        h_act = [[sb([P, PACK, HALF], F32, "h_act%d%d" % (b, u)) for u in range(2)] for b in range(2)]
         h_codes = [sb([P, S], U32, "h_codes%d" % b) for b in range(2)]
         h_plane = [sb([P, S], U8, "h_plane%d" % b) for b in range(2)]
         banks = {}
 
-        def history_pass(unit, a, first):
-            b, t = divmod(unit, PACK)
-            if first:
-                banks[unit] = bank_tile("history%d" % unit, unit + 1, [P, S])
-            c0 = H * a + PASS * b + P * t
-            nc.tensor.matmul_mx(
-                out=banks[unit][:],
-                lhsT=w1_codes[:, 2 * c0 : 2 * (c0 + P)].bitcast(FP4X4),
-                lhsT_scale=w1_plane[:, c0 : c0 + P],
-                rhs=v1_codes[a][:].bitcast(FP8X4), rhs_scale=v1_plane[a][:],
-                start=first, stop=not first,
-            )
-            if not first:
-                nc.scalar.activation(h_act[b][:, t, :], banks[unit][:], ACT.Gelu_apprx_tanh)
+        def history_passes(unit, a):
+            b, rest = divmod(unit, PACK)
+            half, u = divmod(rest, 2)
+            if a == 0:
+                banks[unit] = bank_tile("history%d" % unit, 8 + unit, [P, 2, HALF])
+            cols = slice(HALF * half, HALF * (half + 1))
+            for v in range(2):
+                c0 = PASS * b + P * (2 * u + v)
+                nc.tensor.matmul_mx(
+                    out=banks[unit][:, v, :],
+                    lhsT=w1_codes[a][:, 2 * c0 : 2 * (c0 + P)].bitcast(FP4X4),
+                    lhsT_scale=w1_plane[:, H * a + c0 : H * a + c0 + P],
+                    rhs=v1_codes[a][:, cols].bitcast(FP8X4), rhs_scale=v1_plane[a][:, cols],
+                    start=(a == 0 and v == 0), stop=(a == 1 and v == 1),
+                )
+            if a == 1:
+                nc.scalar.activation(h_act[b][half][:, 2 * u : 2 * u + 2, :], banks[unit][:], ACT.Gelu_apprx_tanh)
 
         for unit in range(AHEAD):
-            history_pass(unit, 0, True)
+            history_passes(unit, 0)
         for unit in range(2 * PACK):
-            history_pass(unit, 1, unit >= AHEAD)
             if unit >= AHEAD:
-                history_pass(unit, 0, False)
+                history_passes(unit, 0)
+            history_passes(unit, 1)
 
         parts = [(0, HALF, 0, 2), (0, HALF, 2, 2), (HALF, SQ, 0, 4), (HALF + SQ, SQ, 0, 4)]
-        sums = [bank_tile("sums%d" % k, k + 3, [P, part[3], part[1]]) for k, part in enumerate(parts)]
+        sums = [bank_tile("sums%d" % k, 16 + k, [P, part[3], part[1]]) for k, part in enumerate(parts)]
 
         def add_passes(k, weights, weight_plane, codes, plane, first, final):
             s0, width, i0, tiles = parts[k]
@@ -294,36 +312,36 @@ def tile_list_parking_occupancy_kernel(
                     start=(first and i == 0), stop=(final and i == tiles - 1),
                 )
 
-        for k in range(len(parts)):
-            for a in range(2):
-                add_passes(k, w4_codes[:, a, :], w4_plane[:, a, :], h2_codes[a], h2_plane[a], a == 0, False)
+        for a in range(2):
+            for k in range(len(parts)):
+                add_passes(k, w4_codes[a], w4_plane[4:P, a, :], h2_codes[a], h2_plane[a], a == 0, False)
 
-        w3_bf = [over([P, N, PACK], BF16, "w3_bf0", 3 * T - 64), sb([P, N, PACK], BF16, "w3_bf1")]
+        w3_bf = [sb([P, N, PACK], BF16, "w3_bf0"), over([P, N, PACK], BF16, "w3_bf1", 8)]
         for n0 in range(0, N, 128):
-            round_w3(0, n0, n0 + 128, pool_round)
-        round_w3(1, 0, 128, pool_round)
-        round_w3(1, 128, N, nc.scalar.copy)
+            pool_round(w3_bf[0][:, n0 : n0 + 128, :], w3_raw[0][:, :, n0 : n0 + 128].rearrange("p t n -> p n t"))
+        round_w3(1, 0, W3_SCALAR, nc.scalar.copy)
 
-        def history_gain(dst, b, s0, s1):
-            apply_gain(dst, h_act[b], s0, s1, history_gains[:, b : b + 1, 0:PACK])
+        def history_gain(dst, b, half, s0, s1):
+            apply_gain(dst, h_act[b][half][:, :, s0:s1], history_gains[:, b, 0:PACK])
 
         def history_quantize(b, s0, s1, values):
             quantize(h_codes[b][:, s0:s1], h_plane[b][:, s0:s1], values)
 
         h_first = sb([P, S * PACK], BF16, "h_first")
-        history_gain(h_first[:, 0 : 2 * PASS], 0, 0, HALF)
-        history_gain(h_first[:, 2 * PASS : 4 * PASS], 0, HALF, S)
-        history_quantize(0, 0, S, h_first[:])
+        for half in range(2):
+            history_gain(h_first[:, 2 * PASS * half : 2 * PASS * (half + 1)], 0, half, 0, HALF)
         h_half = sb([P, HALF * PACK], BF16, "h_half")
-        history_gain(h_half[:], 1, 0, HALF)
+        history_gain(h_half[:], 1, 0, 0, HALF)
+        history_quantize(0, 0, S, h_first[:])
         quantize_w3(0)
+        round_w3(1, W3_SCALAR, N, nc.vector.tensor_copy)
         history_quantize(1, 0, HALF, h_half[:])
         quantize_w3(1)
-        h_last = sb([P, HALF * PACK], BF16, "h_last", "w3_bf1")
-        history_gain(h_last[:, 0:PASS], 1, HALF, HALF + SQ)
-        history_gain(h_last[:, PASS : 2 * PASS], 1, HALF + SQ, S)
-        history_quantize(1, HALF, HALF + SQ, h_last[:, 0:PASS])
-        history_quantize(1, HALF + SQ, S, h_last[:, PASS : 2 * PASS])
+        h_last = over([P, HALF * PACK], BF16, "h_last", 16)
+        for q in range(2):
+            history_gain(h_last[:, PASS * q : PASS * (q + 1)], 1, 1, SQ * q, SQ * (q + 1))
+        for q in range(2):
+            history_quantize(1, HALF + SQ * q, HALF + SQ * (q + 1), h_last[:, PASS * q : PASS * (q + 1)])
 
         out_rows = out.rearrange("(i p) s -> p i s", p=P)
         for k in range(len(parts)):

@@ -27,7 +27,7 @@ RUN = 8
 RING = 6
 AHEAD = 4
 W2_SCALAR = 44
-W3_SCALAR = 352
+W3_SCALAR = 384
 KIB = 1024
 
 
@@ -62,9 +62,9 @@ def tile_list_parking_occupancy_kernel(
         list2 = keep.tile([P, S // 16], U16, name="list2")
         t2_words = sb([P, T2], U16, "t2_words")
         t2_plane = sb([P, 1, T2], U8, "t2_plane")
-        t1_words = [sb([P, T], U32, "t1_words%d" % a) for a in range(2)]
+        t1_words = [over([P, T], U32, "t1_words0", 32), sb([P, T], U32, "t1_words1")]
         t1_plane = sb([P, T], U8, "t1_plane")
-        w1_raw = [over([P, H // 2], I32, "w1_raw0", 32), over([P, H // 2], I32, "w1_raw1", 1)]
+        w1_raw = [sb([P, H // 2], I32, "w1_raw0"), over([P, H // 2], I32, "w1_raw1", 1)]
         w1_raw_plane = sb([P, 2, H], U8, "w1_raw_plane")
         w4_codes = [sb([P, N], U32, "w4_codes%d" % a) for a in range(2)]
         w4_plane = sb([P, 2, N], U8, "w4_plane")
@@ -120,6 +120,7 @@ def tile_list_parking_occupancy_kernel(
         )
         for r in range(4):
             load_scale_row(w1_raw_plane, w1_scales, r, 0)
+        load_w1(0)
         load_words(t1_words[0], tab_words[0])
 
         v2_codes = sb([P, S], U16, "v2_codes")
@@ -127,10 +128,9 @@ def tile_list_parking_occupancy_kernel(
         nc.vector.tensor_copy(v2_codes[:], t2_words[:].indirect(list2[:]))
         nc.vector.tensor_copy(v2_plane[:], t2_plane[:, 0, :].indirect(list2[:]))
 
-        w2_bf = [sb([P, PACK, P, PACK], BF16, "w2_bf%d" % a) for a in range(2)]
+        w2_bf = [sb([P, PACK, P, PACK], BF16, "w2_bf0"), over([P, PACK, P, PACK], BF16, "w2_bf1", 28)]
         w2_codes = [over([P, PASS], U32, "w2_codes0", 24), sb([P, PASS], U32, "w2_codes1")]
-        w2_plane = [sb([P, PASS], U8, "w2_plane%d" % a) for a in range(2)]
-        w3_codes = [sb([P, N], U32, "w3_codes%d" % b) for b in range(2)]
+        w2_plane = [over([P, PASS], U8, "w2_plane0", 26), sb([P, PASS], U8, "w2_plane1")]
         w3_plane = [sb([P, N], U8, "w3_plane%d" % b) for b in range(2)]
 
         def pool_round(dst, src):
@@ -148,14 +148,14 @@ def tile_list_parking_occupancy_kernel(
         def quantize_w2(a):
             quantize(w2_codes[a][:], w2_plane[a][:], w2_bf[a][:].rearrange("p t m j -> p (t m j)"))
 
-        def round_w3(b, n0, n1, rounder):
+        def round_w3(dst, n0, n1, rounder):
             rounder(
-                w3_bf[b][:, n0:n1, :].rearrange("p (c i) t -> p c t i", i=2),
-                w3_raw[b][:, :, n0:n1].rearrange("p t (c i) -> p c t i", i=2),
+                dst[:].rearrange("p (c i) t -> p c t i", i=2),
+                w3_raw[1][:, :, n0:n1].rearrange("p t (c i) -> p c t i", i=2),
             )
 
-        def quantize_w3(b):
-            quantize(w3_codes[b][:], w3_plane[b][:], w3_bf[b][:].rearrange("p n t -> p (n t)"))
+        def quantize_w3(b, n0, n1, values):
+            quantize(w3_codes[b][:, n0:n1], w3_plane[b][:, n0:n1], values[:].rearrange("p n t -> p (n t)"))
 
         sweep_gains = held.tile([P, P, PACK], F32, name="sweep_gains")
         for t in range(PACK):
@@ -166,7 +166,6 @@ def tile_list_parking_occupancy_kernel(
         quantize_w2(0)
         nc.vector.tensor_copy(v1_rows[:], t1_plane[:].indirect(list1[:]))
         place_scales(0)
-        load_w1(0)
         load_words(t1_words[1], tab_words[1])
         place_scales(1)
         load_w1(1)
@@ -184,7 +183,7 @@ def tile_list_parking_occupancy_kernel(
 
         pool_gain = sb([P, PACK], F32, "pool_gain")
         nc.scalar.copy(pool_gain[:], sweep_gains[:, 1, :])
-        for m0 in (0, 32, 64):
+        for m0 in (0, 32):
             pool_round(
                 w2_bf[1][:, :, m0 : m0 + 32, :].rearrange("p t m j -> p m t j"),
                 w2_raw[1][:, :, PACK * m0 : PACK * (m0 + 32)].rearrange("p j (m t) -> p m t j", t=PACK),
@@ -227,55 +226,76 @@ def tile_list_parking_occupancy_kernel(
                 )
             nc.scalar.activation(h2_act[a][half][:, 2 * u : 2 * u + 2, :], bank[:], ACT.Silu)
 
-        for unit in range(4):
+        for q in range(2):
+            bank = bank_tile("sweep0%d" % q, q, [P, PACK, SQ])
+            cols = slice(SQ * q, SQ * (q + 1))
+            for t in range(PACK):
+                chan = slice(P * t, P * (t + 1))
+                nc.tensor.matmul_mx(
+                    out=bank[:, t, :],
+                    lhsT=w2_codes[0][:, chan].bitcast(FP8X4), lhsT_scale=w2_plane[0][:, chan],
+                    rhs=v2_codes[:, cols].bitcast(FP4X4), rhs_scale=v2_plane[:, cols],
+                    start=True, stop=True,
+                )
+            nc.scalar.activation(h2_act[0][0][:, :, cols], bank[:], ACT.Silu)
+        for unit in range(2, 4):
             sweep_unit(0, unit)
-        dst, src = w2_views(1)
-        nc.scalar.copy(dst[:, 96:P], src[:, 96:P])
         w1_plane = over([P, 2 * H], U8, "w1_plane", 24)
         nc.scalar.copy(
             w1_plane[:].bitcast(U32).rearrange("p (x t g w) -> p x g t w", t=PACK, g=16, w=2),
             w1_raw_plane[:].bitcast(U32).rearrange("p a (b g t w) -> p (a b) g t w", t=PACK, g=16, w=2),
         )
+        w1_codes = [over([P, 2 * H], U8, "w1_codes0", 26), sb([P, 2 * H], U8, "w1_codes1")]
+
+        def order_w1(a, mover):
+            mover(
+                w1_codes[a][:].bitcast(U32).rearrange("p (b t g w) -> p b g t w", t=PACK, g=16, w=4),
+                w1_raw[a][:].bitcast(U32).rearrange("p (b g t w) -> p b g t w", t=PACK, g=16, w=4),
+            )
+
+        order_w1(0, nc.scalar.copy)
         history_gains = held.tile([P, 2, P], F32, name="history_gains")
         for b in range(2):
             nc.tensor.transpose(history_gains[:, b, :], gh_rows[:, P * b : P * (b + 1)], identity[:])
-        h2_first = over([P, S * PACK], BF16, "h2_first", 28)
-        for half in range(2):
-            apply_gain(h2_first[:, 2 * PASS * half : 2 * PASS * (half + 1)], h2_act[0][half][:], sweep_gains[:, 0, :])
+        h2_first = [sb([P, HALF * PACK], BF16, "h2_first0"), over([P, HALF * PACK], BF16, "h2_first1", 28)]
+        for q in range(2):
+            apply_gain(h2_first[0][:, PASS * q : PASS * (q + 1)], h2_act[0][0][:, :, SQ * q : SQ * (q + 1)], sweep_gains[:, 0, :])
+        dst, src = w2_views(1)
+        nc.vector.tensor_copy(dst[:, P // 2 : P], src[:, P // 2 : P])
         quantize_w2(1)
+        apply_gain(h2_first[1][:], h2_act[0][1][:], sweep_gains[:, 0, :])
         for unit in range(4):
             sweep_unit(1, unit)
 
         v1_codes = [sb([P, S], U32, "v1_codes0"), over([P, S], U32, "v1_codes1", 8)]
-        w1_codes = [sb([P, 2 * H], U8, "w1_codes%d" % a) for a in range(2)]
-
-        def order_w1(a):
-            nc.vector.tensor_copy(
-                w1_codes[a][:].bitcast(I32).rearrange("p (b t g w) -> p b g t w", t=PACK, g=16, w=4),
-                w1_raw[a][:].rearrange("p (b g t w) -> p b g t w", t=PACK, g=16, w=4),
-            )
-
         nc.vector.tensor_copy(v1_codes[0][:], t1_words[0][:].indirect(list1[:]))
-        order_w1(0)
-        quantize(h2_codes[0][:], h2_plane[0][:], h2_first[:])
+        for u in range(2):
+            cols = slice(HALF * u, HALF * (u + 1))
+            quantize(h2_codes[0][:, cols], h2_plane[0][:, cols], h2_first[u][:])
         h2_quarter = over([P, SQ * PACK], BF16, "h2_quarter", 28)
         pool_apply_gain(h2_quarter[:], h2_act[1][0][:, :, 0:SQ])
         nc.vector.tensor_copy(v1_codes[1][:], t1_words[1][:].indirect(list1[:]))
-        order_w1(1)
+        nc.vector.tensor_copy(
+            w1_codes[1][:].bitcast(I32).rearrange("p (b t g w) -> p b g t w", t=PACK, g=16, w=4),
+            w1_raw[1][:].rearrange("p (b g t w) -> p b g t w", t=PACK, g=16, w=4),
+        )
         h2_rest = over([P, 3 * SQ * PACK], BF16, "h2_rest", 2)
         pool_apply_gain(h2_rest[:, 0:PASS], h2_act[1][0][:, :, SQ:HALF])
         apply_gain(h2_rest[:, PASS : 3 * PASS], h2_act[1][1][:], sweep_gains[:, 1, :])
         quantize(h2_codes[1][:, 0:SQ], h2_plane[1][:, 0:SQ], h2_quarter[:])
         quantize(h2_codes[1][:, SQ:S], h2_plane[1][:, SQ:S], h2_rest[:])
 
-        h_act = [[sb([P, PACK, HALF], F32, "h_act%d%d" % (b, u)) for u in range(2)] for b in range(2)]
-        h_codes = [sb([P, S], U32, "h_codes%d" % b) for b in range(2)]
-        h_plane = [sb([P, S], U8, "h_plane%d" % b) for b in range(2)]
+        h_act = [
+            [sb([P, PACK, HALF], F32, "h_act00"), over([P, PACK, HALF], F32, "h_act01", 40)],
+            [sb([P, PACK, HALF], F32, "h_act10"), sb([P, PACK, HALF], F32, "h_act11")],
+        ]
+        h_codes = [sb([P, 2 * HALF], U32, "h_codes%d" % u) for u in range(2)]
+        h_plane = [sb([P, 2 * HALF], U8, "h_plane%d" % u) for u in range(2)]
         banks = {}
 
         def history_passes(unit, a):
-            b, rest = divmod(unit, PACK)
-            half, u = divmod(rest, 2)
+            half, rest = divmod(unit, PACK)
+            b, u = divmod(rest, 2)
             if a == 0:
                 banks[unit] = bank_tile("history%d" % unit, 8 + unit, [P, 2, HALF])
             cols = slice(HALF * half, HALF * (half + 1))
@@ -301,8 +321,8 @@ def tile_list_parking_occupancy_kernel(
         parts = [(0, HALF, 0, 2), (0, HALF, 2, 2), (HALF, SQ, 0, 4), (HALF + SQ, SQ, 0, 4)]
         sums = [bank_tile("sums%d" % k, 16 + k, [P, part[3], part[1]]) for k, part in enumerate(parts)]
 
-        def add_passes(k, weights, weight_plane, codes, plane, first, final):
-            s0, width, i0, tiles = parts[k]
+        def add_passes(k, weights, weight_plane, codes, plane, s0, first, final):
+            width, i0, tiles = parts[k][1:]
             for i in range(tiles):
                 slots = slice(P * (i0 + i), P * (i0 + i + 1))
                 nc.tensor.matmul_mx(
@@ -314,40 +334,46 @@ def tile_list_parking_occupancy_kernel(
 
         for a in range(2):
             for k in range(len(parts)):
-                add_passes(k, w4_codes[a], w4_plane[4:P, a, :], h2_codes[a], h2_plane[a], a == 0, False)
+                add_passes(k, w4_codes[a], w4_plane[4:P, a, :], h2_codes[a], h2_plane[a], parts[k][0], a == 0, False)
 
-        w3_bf = [sb([P, N, PACK], BF16, "w3_bf0"), over([P, N, PACK], BF16, "w3_bf1", 8)]
+        w3_first = sb([P, N, PACK], BF16, "w3_first")
+        w3_most = over([P, W3_SCALAR, PACK], BF16, "w3_most", 8)
         for n0 in range(0, N, 128):
-            pool_round(w3_bf[0][:, n0 : n0 + 128, :], w3_raw[0][:, :, n0 : n0 + 128].rearrange("p t n -> p n t"))
-        round_w3(1, 0, W3_SCALAR, nc.scalar.copy)
+            pool_round(w3_first[:, n0 : n0 + 128, :], w3_raw[0][:, :, n0 : n0 + 128].rearrange("p t n -> p n t"))
+        round_w3(w3_most, 0, W3_SCALAR, nc.scalar.copy)
 
         def history_gain(dst, b, half, s0, s1):
             apply_gain(dst, h_act[b][half][:, :, s0:s1], history_gains[:, b, 0:PACK])
 
-        def history_quantize(b, s0, s1, values):
-            quantize(h_codes[b][:, s0:s1], h_plane[b][:, s0:s1], values)
-
-        h_first = sb([P, S * PACK], BF16, "h_first")
-        for half in range(2):
-            history_gain(h_first[:, 2 * PASS * half : 2 * PASS * (half + 1)], 0, half, 0, HALF)
-        h_half = sb([P, HALF * PACK], BF16, "h_half")
-        history_gain(h_half[:], 1, 0, 0, HALF)
-        history_quantize(0, 0, S, h_first[:])
-        quantize_w3(0)
-        round_w3(1, W3_SCALAR, N, nc.vector.tensor_copy)
-        history_quantize(1, 0, HALF, h_half[:])
-        quantize_w3(1)
+        h_first = over([P, S * PACK], BF16, "h_first", 12)
+        for b in range(2):
+            history_gain(h_first[:, 2 * PASS * b : 2 * PASS * (b + 1)], b, 0, 0, HALF)
+        h_third = sb([P, HALF * PACK], BF16, "h_third")
+        history_gain(h_third[:], 0, 1, 0, HALF)
+        quantize(h_codes[0][:], h_plane[0][:], h_first[:])
+        w3_codes = [over([P, N], U32, "w3_codes0", 40), sb([P, N], U32, "w3_codes1")]
+        quantize_w3(0, 0, N, w3_first)
+        w3_rest = over([P, N - W3_SCALAR, PACK], BF16, "w3_rest", 12)
+        round_w3(w3_rest, W3_SCALAR, N, nc.vector.tensor_copy)
+        quantize_w3(1, 0, W3_SCALAR, w3_most)
+        quantize_w3(1, W3_SCALAR, N, w3_rest)
+        quantize(h_codes[1][:, 0:HALF], h_plane[1][:, 0:HALF], h_third[:])
         h_last = over([P, HALF * PACK], BF16, "h_last", 16)
         for q in range(2):
             history_gain(h_last[:, PASS * q : PASS * (q + 1)], 1, 1, SQ * q, SQ * (q + 1))
         for q in range(2):
-            history_quantize(1, HALF + SQ * q, HALF + SQ * (q + 1), h_last[:, PASS * q : PASS * (q + 1)])
+            cols = slice(HALF + SQ * q, HALF + SQ * (q + 1))
+            quantize(h_codes[1][:, cols], h_plane[1][:, cols], h_last[:, PASS * q : PASS * (q + 1)])
+
+        def history_sums(k, b):
+            half, s0 = divmod(parts[k][0], HALF)
+            add_passes(k, w3_codes[b], w3_plane[b], h_codes[half], h_plane[half], HALF * b + s0, False, b == 1)
 
         out_rows = out.rearrange("(i p) s -> p i s", p=P)
         for k in range(len(parts)):
-            add_passes(k, w3_codes[0], w3_plane[0], h_codes[0], h_plane[0], False, False)
+            history_sums(k, 0)
         for k, (s0, width, i0, tiles) in enumerate(parts):
-            add_passes(k, w3_codes[1], w3_plane[1], h_codes[1], h_plane[1], False, True)
+            history_sums(k, 1)
             prob = sb([P, tiles, width], F32, "prob%d" % k)
             pieces = ((0, 2, nc.sync), (2, 4, nc.scalar)) if k == len(parts) - 1 else ((0, tiles, nc.sync),)
             for j0, j1, queue in pieces:

@@ -27,7 +27,7 @@ RUN = 8
 RING = 6
 AHEAD = 4
 W2_SCALAR = 44
-W3_SCALAR = 384
+W3_SCALAR = 224
 KIB = 1024
 
 
@@ -62,16 +62,17 @@ def tile_list_parking_occupancy_kernel(
         list2 = keep.tile([P, S // 16], U16, name="list2")
         t2_words = sb([P, T2], U16, "t2_words")
         t2_plane = sb([P, 1, T2], U8, "t2_plane")
-        t1_words = [over([P, T], U32, "t1_words0", 32), sb([P, T], U32, "t1_words1")]
+        t1_words = [over([P, T], U32, "t1_words0", 32), over([P, T], U32, "t1_words1", 4)]
         t1_plane = sb([P, T], U8, "t1_plane")
-        w1_raw = [sb([P, H // 2], I32, "w1_raw0"), over([P, H // 2], I32, "w1_raw1", 1)]
+        w1_raw = [over([P, 2, PASS // 2], I32, "w1_raw0", 55), over([P, 2, PASS // 2], I32, "w1_raw1", 1)]
         w1_raw_plane = sb([P, 2, H], U8, "w1_raw_plane")
         w4_codes = [sb([P, N], U32, "w4_codes%d" % a) for a in range(2)]
         w4_plane = sb([P, 2, N], U8, "w4_plane")
         w2_raw = [sb([P, PACK, PASS], F32, "w2_raw%d" % a) for a in range(2)]
         w3_raw = [sb([P, PACK, N], F32, "w3_raw0"), over([P, PACK, N], F32, "w3_raw1", 16)]
         gs_rows = sb([P, PASS], F32, "gs_rows")
-        gh_rows = sb([P, 2 * P], F32, "gh_rows")
+        gh_raw = sb([2, PASS], F32, "gh_raw")
+        gh_rows = over([P, PASS], F32, "gh_rows", 48)
         v1_plane = [sb([P, S], U8, "v1_plane%d" % a) for a in range(2)]
         v1_rows = sb([P, S], U8, "v1_rows")
         identity = sb([P, P], F32, "identity")
@@ -85,7 +86,7 @@ def tile_list_parking_occupancy_kernel(
         nc.vector.memset(w4_plane[:].bitcast(I32), 0)
         zero = sb([P, 1], F32, "zero")
         nc.gpsimd.memset(zero[:], 0.0)
-        nc.scalar.activation(gh_rows[:], zero[:].to_broadcast([P, 2 * P]), ACT.Silu)
+        nc.scalar.activation(gh_rows[:], zero[:].to_broadcast([P, PASS]), ACT.Silu)
         make_identity(nc, identity[:])
 
         w2_rows = w2.rearrange("(p j) c -> p j c", j=PACK)
@@ -97,8 +98,9 @@ def tile_list_parking_occupancy_kernel(
         def load_words(tile, words):
             nc.sync.dma_start(out=tile[:].bitcast(I32), in_=words.rearrange("p c i -> p (c i)").bitcast(I32))
 
-        def load_w1(a):
-            nc.sync.dma_start(out=w1_raw[a][:], in_=w1_words[a].bitcast(I32))
+        def load_w1(b):
+            words = w1_words.bitcast(I32).rearrange("a p (b c) -> b p a c", b=2)
+            nc.sync.dma_start(out=w1_raw[b][:], in_=words[b])
 
         def load_w3(b, t):
             nc.sync.dma_start(out=w3_raw[b][:, t, :], in_=w3_rows[b, t])
@@ -107,17 +109,14 @@ def tile_list_parking_occupancy_kernel(
         nc.sync.dma_start(list2[:], offs2)
         for r in range(4):
             load_scale_row(t2_plane, tab2_scales, r, 0)
-        nc.sync.dma_start(out=gs_rows[0:2], in_=gs.rearrange("(a c) -> a c", a=2))
         load_w2(0)
+        nc.sync.dma_start(out=gs_rows[0:2], in_=gs.rearrange("(a c) -> a c", a=2))
         nc.sync.dma_start(list1[:], offs)
         nc.sync.dma_start(
             out=t1_plane[:].bitcast(I32)[0:P:4], in_=tab_scales.bitcast(I32).rearrange("a q c -> (a q) c")
         )
         load_w2(1)
-        nc.sync.dma_start(
-            out=gh_rows[0:PACK].rearrange("t (x e) -> t x e", e=RUN),
-            in_=gh.rearrange("(x t e) -> t x e", t=PACK, e=RUN),
-        )
+        nc.sync.dma_start(out=gh_raw[:], in_=gh.rearrange("(b c) -> b c", b=2))
         for r in range(4):
             load_scale_row(w1_raw_plane, w1_scales, r, 0)
         load_w1(0)
@@ -150,7 +149,7 @@ def tile_list_parking_occupancy_kernel(
 
         def round_w3(dst, n0, n1, rounder):
             rounder(
-                dst[:].rearrange("p (c i) t -> p c t i", i=2),
+                dst.rearrange("p (c i) t -> p c t i", i=2),
                 w3_raw[1][:, :, n0:n1].rearrange("p t (c i) -> p c t i", i=2),
             )
 
@@ -189,7 +188,10 @@ def tile_list_parking_occupancy_kernel(
                 w2_raw[1][:, :, PACK * m0 : PACK * (m0 + 32)].rearrange("p j (m t) -> p m t j", t=PACK),
             )
 
-        h2_act = [[sb([P, PACK, HALF], F32, "h2_act%d%d" % (a, u)) for u in range(2)] for a in range(2)]
+        h2_act = [
+            [sb([P, PACK, HALF], F32, "h2_act00"), sb([P, PACK, HALF], F32, "h2_act01")],
+            [over([P, PACK, HALF], F32, "h2_act10", 52), over([P, PACK, HALF], F32, "h2_act11", 56)],
+        ]
         h2_codes = [over([P, S], U32, "h2_codes0", 32), over([P, S], U32, "h2_codes1", 0)]
         h2_plane = [sb([P, S], U8, "h2_plane%d" % a) for a in range(2)]
 
@@ -247,16 +249,20 @@ def tile_list_parking_occupancy_kernel(
         )
         w1_codes = [over([P, 2 * H], U8, "w1_codes0", 26), sb([P, 2 * H], U8, "w1_codes1")]
 
-        def order_w1(a, mover):
+        def order_w1(b, word, mover):
             mover(
-                w1_codes[a][:].bitcast(U32).rearrange("p (b t g w) -> p b g t w", t=PACK, g=16, w=4),
-                w1_raw[a][:].bitcast(U32).rearrange("p (b g t w) -> p b g t w", t=PACK, g=16, w=4),
+                w1_codes[b][:].bitcast(word).rearrange("p (a t g w) -> p a g t w", t=PACK, g=16, w=4),
+                w1_raw[b][:].bitcast(word).rearrange("p a (g t w) -> p a g t w", t=PACK, w=4),
             )
 
-        order_w1(0, nc.scalar.copy)
-        history_gains = held.tile([P, 2, P], F32, name="history_gains")
-        for b in range(2):
-            nc.tensor.transpose(history_gains[:, b, :], gh_rows[:, P * b : P * (b + 1)], identity[:])
+        order_w1(0, U32, nc.scalar.copy)
+        nc.scalar.copy(
+            gh_rows[0:2].rearrange("b (t g e) -> b g t e", t=PACK, e=RUN),
+            gh_raw[:].rearrange("b (g t e) -> b g t e", t=PACK, e=RUN),
+        )
+        history_gains = held.tile([P, P, PACK], F32, name="history_gains")
+        for t in range(PACK):
+            nc.tensor.transpose(history_gains[:, :, t], gh_rows[:, P * t : P * (t + 1)], identity[:])
         h2_first = [sb([P, HALF * PACK], BF16, "h2_first0"), over([P, HALF * PACK], BF16, "h2_first1", 28)]
         for q in range(2):
             apply_gain(h2_first[0][:, PASS * q : PASS * (q + 1)], h2_act[0][0][:, :, SQ * q : SQ * (q + 1)], sweep_gains[:, 0, :])
@@ -267,44 +273,44 @@ def tile_list_parking_occupancy_kernel(
         for unit in range(4):
             sweep_unit(1, unit)
 
-        v1_codes = [sb([P, S], U32, "v1_codes0"), over([P, S], U32, "v1_codes1", 8)]
+        v1_codes = [sb([P, S], U32, "v1_codes0"), sb([P, S], U32, "v1_codes1")]
         nc.vector.tensor_copy(v1_codes[0][:], t1_words[0][:].indirect(list1[:]))
         for u in range(2):
             cols = slice(HALF * u, HALF * (u + 1))
             quantize(h2_codes[0][:, cols], h2_plane[0][:, cols], h2_first[u][:])
-        h2_quarter = over([P, SQ * PACK], BF16, "h2_quarter", 28)
-        pool_apply_gain(h2_quarter[:], h2_act[1][0][:, :, 0:SQ])
-        nc.vector.tensor_copy(v1_codes[1][:], t1_words[1][:].indirect(list1[:]))
-        nc.vector.tensor_copy(
-            w1_codes[1][:].bitcast(I32).rearrange("p (b t g w) -> p b g t w", t=PACK, g=16, w=4),
-            w1_raw[1][:].rearrange("p (b g t w) -> p b g t w", t=PACK, g=16, w=4),
-        )
-        h2_rest = over([P, 3 * SQ * PACK], BF16, "h2_rest", 2)
-        pool_apply_gain(h2_rest[:, 0:PASS], h2_act[1][0][:, :, SQ:HALF])
-        apply_gain(h2_rest[:, PASS : 3 * PASS], h2_act[1][1][:], sweep_gains[:, 1, :])
-        quantize(h2_codes[1][:, 0:SQ], h2_plane[1][:, 0:SQ], h2_quarter[:])
-        quantize(h2_codes[1][:, SQ:S], h2_plane[1][:, SQ:S], h2_rest[:])
+        h2_most = over([P, 3 * SQ * PACK], BF16, "h2_most", 28)
+        for q in range(2):
+            pool_apply_gain(h2_most[:, PASS * q : PASS * (q + 1)], h2_act[1][0][:, :, SQ * q : SQ * (q + 1)])
+        apply_gain(h2_most[:, 2 * PASS : 3 * PASS], h2_act[1][1][:, :, 0:SQ], sweep_gains[:, 1, :])
+        for u in range(2):
+            nc.vector.tensor_copy(
+                v1_codes[1][:, HALF * u : HALF * (u + 1)], t1_words[1][:].indirect(list1[:, 16 * u : 16 * (u + 1)])
+            )
+        h2_last = over([P, SQ * PACK], BF16, "h2_last", 8)
+        apply_gain(h2_last[:], h2_act[1][1][:, :, SQ:HALF], sweep_gains[:, 1, :])
+        order_w1(1, I32, nc.vector.tensor_copy)
+        quantize(h2_codes[1][:, 0 : 3 * SQ], h2_plane[1][:, 0 : 3 * SQ], h2_most[:])
+        quantize(h2_codes[1][:, 3 * SQ : S], h2_plane[1][:, 3 * SQ : S], h2_last[:])
 
         h_act = [
-            [sb([P, PACK, HALF], F32, "h_act00"), over([P, PACK, HALF], F32, "h_act01", 40)],
-            [sb([P, PACK, HALF], F32, "h_act10"), sb([P, PACK, HALF], F32, "h_act11")],
+            [sb([P, PACK, HALF], F32, "h_act00"), sb([P, PACK, HALF], F32, "h_act01")],
+            [over([P, PACK, HALF], F32, "h_act10", 40), sb([P, PACK, HALF], F32, "h_act11")],
         ]
-        h_codes = [sb([P, 2 * HALF], U32, "h_codes%d" % u) for u in range(2)]
         h_plane = [sb([P, 2 * HALF], U8, "h_plane%d" % u) for u in range(2)]
         banks = {}
 
         def history_passes(unit, a):
-            half, rest = divmod(unit, PACK)
-            b, u = divmod(rest, 2)
+            b, rest = divmod(unit, PACK)
+            half, u = divmod(rest, 2)
             if a == 0:
                 banks[unit] = bank_tile("history%d" % unit, 8 + unit, [P, 2, HALF])
             cols = slice(HALF * half, HALF * (half + 1))
             for v in range(2):
-                c0 = PASS * b + P * (2 * u + v)
+                c0 = P * (2 * u + v)
                 nc.tensor.matmul_mx(
                     out=banks[unit][:, v, :],
-                    lhsT=w1_codes[a][:, 2 * c0 : 2 * (c0 + P)].bitcast(FP4X4),
-                    lhsT_scale=w1_plane[:, H * a + c0 : H * a + c0 + P],
+                    lhsT=w1_codes[b][:, 2 * (PASS * a + c0) : 2 * (PASS * a + c0 + P)].bitcast(FP4X4),
+                    lhsT_scale=w1_plane[:, H * a + PASS * b + c0 : H * a + PASS * b + c0 + P],
                     rhs=v1_codes[a][:, cols].bitcast(FP8X4), rhs_scale=v1_plane[a][:, cols],
                     start=(a == 0 and v == 0), stop=(a == 1 and v == 1),
                 )
@@ -332,31 +338,34 @@ def tile_list_parking_occupancy_kernel(
                     start=(first and i == 0), stop=(final and i == tiles - 1),
                 )
 
+        def sweep_sums(k, a):
+            add_passes(k, w4_codes[a], w4_plane[4:P, a, :], h2_codes[a], h2_plane[a], parts[k][0], a == 0, False)
+
         for a in range(2):
             for k in range(len(parts)):
-                add_passes(k, w4_codes[a], w4_plane[4:P, a, :], h2_codes[a], h2_plane[a], parts[k][0], a == 0, False)
+                sweep_sums(k, a)
 
         w3_first = sb([P, N, PACK], BF16, "w3_first")
-        w3_most = over([P, W3_SCALAR, PACK], BF16, "w3_most", 8)
         for n0 in range(0, N, 128):
             pool_round(w3_first[:, n0 : n0 + 128, :], w3_raw[0][:, :, n0 : n0 + 128].rearrange("p t n -> p n t"))
-        round_w3(w3_most, 0, W3_SCALAR, nc.scalar.copy)
 
         def history_gain(dst, b, half, s0, s1):
-            apply_gain(dst, h_act[b][half][:, :, s0:s1], history_gains[:, b, 0:PACK])
+            apply_gain(dst, h_act[b][half][:, :, s0:s1], history_gains[:, b, :])
 
+        h_codes = [sb([P, 2 * HALF], U32, "h_codes0")]
         h_first = over([P, S * PACK], BF16, "h_first", 12)
-        for b in range(2):
-            history_gain(h_first[:, 2 * PASS * b : 2 * PASS * (b + 1)], b, 0, 0, HALF)
         h_third = sb([P, HALF * PACK], BF16, "h_third")
+        history_gain(h_first[:, 0 : 2 * PASS], 0, 0, 0, HALF)
         history_gain(h_third[:], 0, 1, 0, HALF)
+        history_gain(h_first[:, 2 * PASS : 4 * PASS], 1, 0, 0, HALF)
         quantize(h_codes[0][:], h_plane[0][:], h_first[:])
         w3_codes = [over([P, N], U32, "w3_codes0", 40), sb([P, N], U32, "w3_codes1")]
+        w3_second = over([P, N, PACK], BF16, "w3_second", 12)
+        round_w3(w3_second[:, 0:W3_SCALAR, :], 0, W3_SCALAR, nc.scalar.copy)
+        round_w3(w3_second[:, W3_SCALAR:N, :], W3_SCALAR, N, nc.vector.tensor_copy)
         quantize_w3(0, 0, N, w3_first)
-        w3_rest = over([P, N - W3_SCALAR, PACK], BF16, "w3_rest", 12)
-        round_w3(w3_rest, W3_SCALAR, N, nc.vector.tensor_copy)
-        quantize_w3(1, 0, W3_SCALAR, w3_most)
-        quantize_w3(1, W3_SCALAR, N, w3_rest)
+        quantize_w3(1, 0, N, w3_second)
+        h_codes.append(over([P, 2 * HALF], U32, "h_codes1", 12))
         quantize(h_codes[1][:, 0:HALF], h_plane[1][:, 0:HALF], h_third[:])
         h_last = over([P, HALF * PACK], BF16, "h_last", 16)
         for q in range(2):
@@ -370,9 +379,10 @@ def tile_list_parking_occupancy_kernel(
             add_passes(k, w3_codes[b], w3_plane[b], h_codes[half], h_plane[half], HALF * b + s0, False, b == 1)
 
         out_rows = out.rearrange("(i p) s -> p i s", p=P)
-        for k in range(len(parts)):
-            history_sums(k, 0)
         for k, (s0, width, i0, tiles) in enumerate(parts):
+            if k % 2 == 0:
+                for pair in (k, k + 1):
+                    history_sums(pair, 0)
             history_sums(k, 1)
             prob = sb([P, tiles, width], F32, "prob%d" % k)
             pieces = ((0, 2, nc.sync), (2, 4, nc.scalar)) if k == len(parts) - 1 else ((0, tiles, nc.sync),)

@@ -27,7 +27,7 @@ RUN = 8
 RING = 6
 AHEAD = 4
 W2_SCALAR = 44
-W3_SCALAR = 224
+W3_SCALAR = 256
 KIB = 1024
 
 
@@ -111,12 +111,12 @@ def tile_list_parking_occupancy_kernel(
             load_scale_row(t2_plane, tab2_scales, r, 0)
         load_w2(0)
         nc.sync.dma_start(out=gs_rows[0:2], in_=gs.rearrange("(a c) -> a c", a=2))
+        nc.sync.dma_start(out=gh_raw[:], in_=gh.rearrange("(b c) -> b c", b=2))
         nc.sync.dma_start(list1[:], offs)
         nc.sync.dma_start(
             out=t1_plane[:].bitcast(I32)[0:P:4], in_=tab_scales.bitcast(I32).rearrange("a q c -> (a q) c")
         )
         load_w2(1)
-        nc.sync.dma_start(out=gh_raw[:], in_=gh.rearrange("(b c) -> b c", b=2))
         for r in range(4):
             load_scale_row(w1_raw_plane, w1_scales, r, 0)
         load_w1(0)
@@ -182,6 +182,10 @@ def tile_list_parking_occupancy_kernel(
 
         pool_gain = sb([P, PACK], F32, "pool_gain")
         nc.scalar.copy(pool_gain[:], sweep_gains[:, 1, :])
+        pool_round(
+            gh_rows[0:2].rearrange("b (t g e) -> b t g e", t=PACK, e=RUN),
+            gh_raw[:].rearrange("b (g t e) -> b t g e", t=PACK, e=RUN),
+        )
         for m0 in (0, 32):
             pool_round(
                 w2_bf[1][:, :, m0 : m0 + 32, :].rearrange("p t m j -> p m t j"),
@@ -216,7 +220,10 @@ def tile_list_parking_occupancy_kernel(
 
         def sweep_unit(a, unit):
             half, u = divmod(unit, 2)
-            bank = bank_tile("sweep%d%d" % (a, unit), 4 * a + unit, [P, 2, HALF])
+            if (a, unit) == (0, 3):
+                bank = held.tile([P, 2, HALF], F32, name="sweep03", tag="spare")
+            else:
+                bank = bank_tile("sweep%d%d" % (a, unit), 4 * a + unit, [P, 2, HALF])
             cols = slice(HALF * half, HALF * (half + 1))
             for v in range(2):
                 chan = slice(P * (2 * u + v), P * (2 * u + v + 1))
@@ -256,11 +263,7 @@ def tile_list_parking_occupancy_kernel(
             )
 
         order_w1(0, U32, nc.scalar.copy)
-        nc.scalar.copy(
-            gh_rows[0:2].rearrange("b (t g e) -> b g t e", t=PACK, e=RUN),
-            gh_raw[:].rearrange("b (g t e) -> b g t e", t=PACK, e=RUN),
-        )
-        history_gains = held.tile([P, P, PACK], F32, name="history_gains")
+        history_gains = held.tile([P, P, PACK], F32, name="history_gains", tag="spare")
         for t in range(PACK):
             nc.tensor.transpose(history_gains[:, :, t], gh_rows[:, P * t : P * (t + 1)], identity[:])
         h2_first = [sb([P, HALF * PACK], BF16, "h2_first0"), over([P, HALF * PACK], BF16, "h2_first1", 28)]
@@ -273,7 +276,7 @@ def tile_list_parking_occupancy_kernel(
         for unit in range(4):
             sweep_unit(1, unit)
 
-        v1_codes = [sb([P, S], U32, "v1_codes0"), sb([P, S], U32, "v1_codes1")]
+        v1_codes = [sb([P, S], U32, "v1_codes0"), over([P, S], U32, "v1_codes1", 64)]
         nc.vector.tensor_copy(v1_codes[0][:], t1_words[0][:].indirect(list1[:]))
         for u in range(2):
             cols = slice(HALF * u, HALF * (u + 1))
@@ -324,7 +327,7 @@ def tile_list_parking_occupancy_kernel(
                 history_passes(unit, 0)
             history_passes(unit, 1)
 
-        parts = [(0, HALF, 0, 2), (0, HALF, 2, 2), (HALF, SQ, 0, 4), (HALF + SQ, SQ, 0, 4)]
+        parts = [(0, HALF, 0, 2), (0, HALF, 2, 2), (HALF, SQ, 0, 4), (HALF + SQ, SQ, 0, 2), (HALF + SQ, SQ, 2, 2)]
         sums = [bank_tile("sums%d" % k, 16 + k, [P, part[3], part[1]]) for k, part in enumerate(parts)]
 
         def add_passes(k, weights, weight_plane, codes, plane, s0, first, final):
@@ -349,10 +352,13 @@ def tile_list_parking_occupancy_kernel(
         for n0 in range(0, N, 128):
             pool_round(w3_first[:, n0 : n0 + 128, :], w3_raw[0][:, :, n0 : n0 + 128].rearrange("p t n -> p n t"))
 
+        w3_most = over([P, W3_SCALAR, PACK], BF16, "w3_most", 64)
+        round_w3(w3_most[:], 0, W3_SCALAR, nc.scalar.copy)
+
         def history_gain(dst, b, half, s0, s1):
             apply_gain(dst, h_act[b][half][:, :, s0:s1], history_gains[:, b, :])
 
-        h_codes = [sb([P, 2 * HALF], U32, "h_codes0")]
+        h_codes = [sb([P, 2 * HALF], U32, "h_codes%d" % u) for u in range(2)]
         h_first = over([P, S * PACK], BF16, "h_first", 12)
         h_third = sb([P, HALF * PACK], BF16, "h_third")
         history_gain(h_first[:, 0 : 2 * PASS], 0, 0, 0, HALF)
@@ -360,12 +366,11 @@ def tile_list_parking_occupancy_kernel(
         history_gain(h_first[:, 2 * PASS : 4 * PASS], 1, 0, 0, HALF)
         quantize(h_codes[0][:], h_plane[0][:], h_first[:])
         w3_codes = [over([P, N], U32, "w3_codes0", 40), sb([P, N], U32, "w3_codes1")]
-        w3_second = over([P, N, PACK], BF16, "w3_second", 12)
-        round_w3(w3_second[:, 0:W3_SCALAR, :], 0, W3_SCALAR, nc.scalar.copy)
-        round_w3(w3_second[:, W3_SCALAR:N, :], W3_SCALAR, N, nc.vector.tensor_copy)
         quantize_w3(0, 0, N, w3_first)
-        quantize_w3(1, 0, N, w3_second)
-        h_codes.append(over([P, 2 * HALF], U32, "h_codes1", 12))
+        w3_rest = over([P, N - W3_SCALAR, PACK], BF16, "w3_rest", 12)
+        round_w3(w3_rest[:], W3_SCALAR, N, nc.vector.tensor_copy)
+        quantize_w3(1, 0, W3_SCALAR, w3_most)
+        quantize_w3(1, W3_SCALAR, N, w3_rest)
         quantize(h_codes[1][:, 0:HALF], h_plane[1][:, 0:HALF], h_third[:])
         h_last = over([P, HALF * PACK], BF16, "h_last", 16)
         for q in range(2):
@@ -380,12 +385,11 @@ def tile_list_parking_occupancy_kernel(
 
         out_rows = out.rearrange("(i p) s -> p i s", p=P)
         for k, (s0, width, i0, tiles) in enumerate(parts):
-            if k % 2 == 0:
-                for pair in (k, k + 1):
-                    history_sums(pair, 0)
+            if k in (0, 2):
+                for later in range(k, 2 if k == 0 else len(parts)):
+                    history_sums(later, 0)
             history_sums(k, 1)
             prob = sb([P, tiles, width], F32, "prob%d" % k)
-            pieces = ((0, 2, nc.sync), (2, 4, nc.scalar)) if k == len(parts) - 1 else ((0, tiles, nc.sync),)
-            for j0, j1, queue in pieces:
-                nc.scalar.activation(prob[:, j0:j1, :], sums[k][:, j0:j1, :], ACT.Sigmoid)
-                queue.dma_start(out=out_rows[:, i0 + j0 : i0 + j1, s0 : s0 + width], in_=prob[:, j0:j1, :])
+            nc.scalar.activation(prob[:], sums[k][:], ACT.Sigmoid)
+            queue = nc.scalar if k == len(parts) - 1 else nc.sync
+            queue.dma_start(out=out_rows[:, i0 : i0 + tiles, s0 : s0 + width], in_=prob[:])

@@ -28,6 +28,7 @@ RING = 6
 AHEAD = 4
 W2_SCALAR = 44
 W3_SCALAR = 256
+POOL_QUERIES = 64
 KIB = 1024
 
 
@@ -210,11 +211,11 @@ def tile_list_parking_occupancy_kernel(
                 MULT,
             )
 
-        def pool_apply_gain(dst, act):
+        def pool_apply_gain(dst, act, gain):
             nc.gpsimd.tensor_tensor(
                 dst.rearrange("p (s t) -> p s t", t=PACK),
                 act.rearrange("p t s -> p s t"),
-                pool_gain[:].unsqueeze(1).to_broadcast([P, SQ, PACK]),
+                gain.unsqueeze(1).to_broadcast([P, act.shape[2], PACK]),
                 MULT,
             )
 
@@ -283,12 +284,14 @@ def tile_list_parking_occupancy_kernel(
             quantize(h2_codes[0][:, cols], h2_plane[0][:, cols], h2_first[u][:])
         h2_most = over([P, 3 * SQ * PACK], BF16, "h2_most", 28)
         for q in range(2):
-            pool_apply_gain(h2_most[:, PASS * q : PASS * (q + 1)], h2_act[1][0][:, :, SQ * q : SQ * (q + 1)])
+            pool_apply_gain(h2_most[:, PASS * q : PASS * (q + 1)], h2_act[1][0][:, :, SQ * q : SQ * (q + 1)], pool_gain[:])
         apply_gain(h2_most[:, 2 * PASS : 3 * PASS], h2_act[1][1][:, :, 0:SQ], sweep_gains[:, 1, :])
         for u in range(2):
             nc.vector.tensor_copy(
                 v1_codes[1][:, HALF * u : HALF * (u + 1)], t1_words[1][:].indirect(list1[:, 16 * u : 16 * (u + 1)])
             )
+        pool_history = over([P, PACK], F32, "pool_history", 10)
+        nc.vector.tensor_copy(pool_history[:], history_gains[:, 1, :])
         h2_last = over([P, SQ * PACK], BF16, "h2_last", 8)
         apply_gain(h2_last[:], h2_act[1][1][:, :, SQ:HALF], sweep_gains[:, 1, :])
         order_w1(1, I32, nc.vector.tensor_copy)
@@ -372,12 +375,14 @@ def tile_list_parking_occupancy_kernel(
         quantize_w3(1, 0, W3_SCALAR, w3_most)
         quantize_w3(1, W3_SCALAR, N, w3_rest)
         quantize(h_codes[1][:, 0:HALF], h_plane[1][:, 0:HALF], h_third[:])
-        h_last = over([P, HALF * PACK], BF16, "h_last", 16)
-        for q in range(2):
-            history_gain(h_last[:, PASS * q : PASS * (q + 1)], 1, 1, SQ * q, SQ * (q + 1))
+        h_last = [over([P, PASS], BF16, "h_last0", 16), over([P, PASS], BF16, "h_last1", 64)]
+        own = SQ - POOL_QUERIES
+        history_gain(h_last[0][:], 1, 1, 0, SQ)
+        history_gain(h_last[1][:, 0 : PACK * own], 1, 1, SQ, SQ + own)
+        pool_apply_gain(h_last[1][:, PACK * own : PASS], h_act[1][1][:, :, SQ + own : HALF], pool_history[:])
         for q in range(2):
             cols = slice(HALF + SQ * q, HALF + SQ * (q + 1))
-            quantize(h_codes[1][:, cols], h_plane[1][:, cols], h_last[:, PASS * q : PASS * (q + 1)])
+            quantize(h_codes[1][:, cols], h_plane[1][:, cols], h_last[q][:])
 
         def history_sums(k, b):
             half, s0 = divmod(parts[k][0], HALF)

@@ -183,7 +183,7 @@ def tile_list_parking_occupancy_kernel(
 
         pool_gain = sb([P, PACK], F32, "pool_gain")
         nc.scalar.copy(pool_gain[:], sweep_gains[:, 1, :])
-        pool_round(
+        nc.scalar.copy(
             gh_rows[0:2].rearrange("b (t g e) -> b t g e", t=PACK, e=RUN),
             gh_raw[:].rearrange("b (g t e) -> b t g e", t=PACK, e=RUN),
         )

@@ -146,7 +146,9 @@ def tile_list_parking_occupancy_kernel(
             nc.vector.quantize_mx(out=codes.bitcast(FP8X4), scales=plane, in_=values)
 
         def quantize_w2(a):
-            quantize(w2_codes[a][:], w2_plane[a][:], w2_bf[a][:].rearrange("p t m j -> p (t m j)"))
+            for u in range(2):
+                chan = slice(2 * P * u, 2 * P * (u + 1))
+                quantize(w2_codes[a][:, chan], w2_plane[a][:, chan], w2_bf[a][:, 2 * u : 2 * u + 2].rearrange("p t m j -> p (t m j)"))
 
         def round_w3(dst, n0, n1, rounder):
             rounder(
@@ -155,14 +157,15 @@ def tile_list_parking_occupancy_kernel(
             )
 
         def quantize_w3(b, n0, n1, values):
-            quantize(w3_codes[b][:, n0:n1], w3_plane[b][:, n0:n1], values[:].rearrange("p n t -> p (n t)"))
+            quantize(w3_codes[b][:, n0:n1], w3_plane[b][:, n0:n1], values.rearrange("p n t -> p (n t)"))
 
         sweep_gains = held.tile([P, P, PACK], F32, name="sweep_gains")
         for t in range(PACK):
             nc.tensor.transpose(sweep_gains[:, :, t], gs_rows[:, t:PASS:PACK], identity[:])
         dst, src = w2_views(0)
-        nc.scalar.copy(dst[:, 0:W2_SCALAR], src[:, 0:W2_SCALAR])
-        nc.vector.tensor_copy(dst[:, W2_SCALAR:P], src[:, W2_SCALAR:P])
+        for u in range(2):
+            nc.scalar.copy(dst[:, 0:W2_SCALAR, u], src[:, 0:W2_SCALAR, u])
+            nc.vector.tensor_copy(dst[:, W2_SCALAR:P, u], src[:, W2_SCALAR:P, u])
         quantize_w2(0)
         nc.vector.tensor_copy(v1_rows[:], t1_plane[:].indirect(list1[:]))
         place_scales(0)
@@ -271,7 +274,8 @@ def tile_list_parking_occupancy_kernel(
         for q in range(2):
             apply_gain(h2_first[0][:, PASS * q : PASS * (q + 1)], h2_act[0][0][:, :, SQ * q : SQ * (q + 1)], sweep_gains[:, 0, :])
         dst, src = w2_views(1)
-        nc.vector.tensor_copy(dst[:, P // 2 : P], src[:, P // 2 : P])
+        for u in range(2):
+            nc.vector.tensor_copy(dst[:, P // 2 : P, u], src[:, P // 2 : P, u])
         quantize_w2(1)
         apply_gain(h2_first[1][:], h2_act[0][1][:], sweep_gains[:, 0, :])
         for unit in range(4):
@@ -369,11 +373,13 @@ def tile_list_parking_occupancy_kernel(
         history_gain(h_first[:, 2 * PASS : 4 * PASS], 1, 0, 0, HALF)
         quantize(h_codes[0][:], h_plane[0][:], h_first[:])
         w3_codes = [over([P, N], U32, "w3_codes0", 40), sb([P, N], U32, "w3_codes1")]
-        quantize_w3(0, 0, N, w3_first)
+        quantize_w3(0, 0, N, w3_first[:])
         w3_rest = over([P, N - W3_SCALAR, PACK], BF16, "w3_rest", 12)
-        round_w3(w3_rest[:], W3_SCALAR, N, nc.vector.tensor_copy)
-        quantize_w3(1, 0, W3_SCALAR, w3_most)
-        quantize_w3(1, W3_SCALAR, N, w3_rest)
+        for n0 in range(W3_SCALAR, N, P):
+            round_w3(w3_rest[:, n0 - W3_SCALAR : n0 - W3_SCALAR + P], n0, n0 + P, nc.vector.tensor_copy)
+        quantize_w3(1, 0, W3_SCALAR, w3_most[:])
+        for n0 in range(W3_SCALAR, N, P):
+            quantize_w3(1, n0, n0 + P, w3_rest[:, n0 - W3_SCALAR : n0 - W3_SCALAR + P])
         quantize(h_codes[1][:, 0:HALF], h_plane[1][:, 0:HALF], h_third[:])
         h_last = [over([P, PASS], BF16, "h_last0", 16), over([P, PASS], BF16, "h_last1", 64)]
         own = SQ - POOL_QUERIES

from contextlib import ExitStack

import concourse.mybir as mybir
from concourse.masks import make_identity

K, K2, T, T2, S, H, N = 1024, 512, 2048, 1024, 512, 1024, 512
FLOPS = 2 * S * (K * H + K2 * H + 2 * H * N)

F32 = mybir.dt.float32
BF16 = mybir.dt.bfloat16
I32 = mybir.dt.int32
U32 = mybir.dt.uint32
U16 = mybir.dt.uint16
U8 = mybir.dt.uint8
FP8X4 = mybir.dt.float8_e4m3fn_x4
FP4X4 = mybir.dt.float4_e2m1fn_x4
ACT = mybir.ActivationFunctionType
MULT = mybir.AluOpType.mult
ADD = mybir.AluOpType.add

P = 128
PACK = 4
PASS = P * PACK
SQ = 128
HALF = S // 2
RUN = 8
RING = 6
AHEAD = 4
W2_SCALAR = 44
W3_SCALAR = 256
POOL_QUERIES = 64
KIB = 1024


def tile_list_parking_occupancy_kernel(
    tc, tab_words, tab_scales, tab2_words, tab2_scales, offs, offs2,
    w1_words, w1_scales, w2, gh, gs, w3, w4_words, w4_scales, out,
):
    nc = tc.nc
    with ExitStack() as ctx:
        keep = ctx.enter_context(tc.tile_pool(name="keep", bufs=1))
        reuse = ctx.enter_context(tc.tile_pool(name="reuse", bufs=1))
        held = ctx.enter_context(tc.psum_pool(name="held", bufs=1))

        def sb(shape, dtype, name):
            return keep.tile(shape, dtype, name=name, align_bytes=64)

        def over(shape, dtype, name, kib):
            return reuse.tile(shape, dtype, name=name, align_bytes=64, offset=kib * KIB)

        def load_scale_row(plane, scales, r, first):
            rows = scales.bitcast(I32).rearrange("a (q r) c -> r q a c", r=4)
            nc.sync.dma_start(out=plane[:].bitcast(I32)[first + r : P : 32], in_=rows[r])

        def place_scales(a):
            for r in range(4):
                nc.sync.dma_start(
                    out=v1_plane[a][:].bitcast(I32)[r:P:32],
                    in_=v1_rows[:].bitcast(I32)[64 * a + 4 * r : 64 * (a + 1) : 16],
                )

        list1 = keep.tile([P, S // 16], U16, name="list1")
        list2 = keep.tile([P, S // 16], U16, name="list2")
        t2_words = sb([P, T2], U16, "t2_words")
        t2_plane = sb([P, 1, T2], U8, "t2_plane")
        t1_words = [over([P, T], U32, "t1_words0", 32), over([P, T], U32, "t1_words1", 4)]
        t1_plane = sb([P, T], U8, "t1_plane")
        w1_raw = [over([P, 2, PASS // 2], I32, "w1_raw0", 55), over([P, 2, PASS // 2], I32, "w1_raw1", 1)]
        w1_raw_plane = sb([P, 2, H], U8, "w1_raw_plane")
        w4_codes = [sb([P, N], U32, "w4_codes%d" % a) for a in range(2)]
        w4_plane = sb([P, 2, N], U8, "w4_plane")
        w2_raw = [sb([P, PACK, PASS], F32, "w2_raw%d" % a) for a in range(2)]
        w3_raw = [sb([P, PACK, N], F32, "w3_raw0"), over([P, PACK, N], F32, "w3_raw1", 16)]
        gs_rows = sb([P, PASS], F32, "gs_rows")
        gh_raw = sb([2, PASS], F32, "gh_raw")
        gh_rows = over([P, PASS], F32, "gh_rows", 48)
        v1_plane = [sb([P, S], U8, "v1_plane%d" % a) for a in range(2)]
        v1_rows = sb([P, S], U8, "v1_rows")
        identity = sb([P, P], F32, "identity")

        nc.gpsimd.memset(t2_plane[:].bitcast(I32), 0)
        nc.vector.memset(gs_rows[:], 0.0)
        nc.vector.memset(t1_plane[:].bitcast(I32), 0)
        nc.vector.memset(w1_raw_plane[:].bitcast(I32), 0)
        for a in range(2):
            nc.vector.memset(v1_plane[a][:].bitcast(I32), 0)
        nc.vector.memset(w4_plane[:].bitcast(I32), 0)
        zero = sb([P, 1], F32, "zero")
        nc.gpsimd.memset(zero[:], 0.0)
        nc.scalar.activation(gh_rows[:], zero[:].to_broadcast([P, PASS]), ACT.Silu)
        make_identity(nc, identity[:])

        w2_rows = w2.rearrange("(p j) c -> p j c", j=PACK)
        w3_rows = w3.rearrange("(b g t e) n -> b t g e n", b=2, t=PACK, e=RUN)

        def load_w2(a):
            nc.sync.dma_start(out=w2_raw[a][:], in_=w2_rows[:, :, PASS * a : PASS * (a + 1)])

        def load_words(tile, words):
            nc.sync.dma_start(out=tile[:].bitcast(I32), in_=words.rearrange("p c i -> p (c i)").bitcast(I32))

        def load_w1(b):
            words = w1_words.bitcast(I32).rearrange("a p (b c) -> b p a c", b=2)
            nc.sync.dma_start(out=w1_raw[b][:], in_=words[b])

        def load_w3(b, t):
            nc.sync.dma_start(out=w3_raw[b][:, t, :], in_=w3_rows[b, t])

        nc.sync.dma_start(out=t2_words[:].bitcast(I32), in_=tab2_words[0].bitcast(I32))
        nc.sync.dma_start(list2[:], offs2)
        for r in range(4):
            load_scale_row(t2_plane, tab2_scales, r, 0)
        load_w2(0)
        nc.sync.dma_start(out=gs_rows[0:2], in_=gs.rearrange("(a c) -> a c", a=2))
        nc.sync.dma_start(out=gh_raw[:], in_=gh.rearrange("(b c) -> b c", b=2))
        nc.sync.dma_start(list1[:], offs)
        nc.sync.dma_start(
            out=t1_plane[:].bitcast(I32)[0:P:4], in_=tab_scales.bitcast(I32).rearrange("a q c -> (a q) c")
        )
        load_w2(1)
        for r in range(4):
            load_scale_row(w1_raw_plane, w1_scales, r, 0)
        load_w1(0)
        load_words(t1_words[0], tab_words[0])

        v2_codes = sb([P, S], U16, "v2_codes")
        v2_plane = sb([P, S], U8, "v2_plane")
        nc.vector.tensor_copy(v2_codes[:], t2_words[:].indirect(list2[:]))
        nc.vector.tensor_copy(v2_plane[:], t2_plane[:, 0, :].indirect(list2[:]))

        w2_bf = [sb([P, PACK, P, PACK], BF16, "w2_bf0"), over([P, PACK, P, PACK], BF16, "w2_bf1", 28)]
        w2_codes = [over([P, PASS], U32, "w2_codes0", 24), sb([P, PASS], U32, "w2_codes1")]
        w2_plane = [over([P, PASS], U8, "w2_plane0", 26), sb([P, PASS], U8, "w2_plane1")]
        w3_plane = [sb([P, N], U8, "w3_plane%d" % b) for b in range(2)]

        def pool_round(dst, src):
            nc.gpsimd.tensor_scalar(dst, src, 1.0, 0.0, MULT, ADD)

        def w2_views(a):
            return (
                w2_bf[a][:].rearrange("p (u e) m j -> p m u j e", e=2),
                w2_raw[a][:].rearrange("p j (m u e) -> p m u j e", u=2, e=2),
            )

        def quantize(codes, plane, values):
            nc.vector.quantize_mx(out=codes.bitcast(FP8X4), scales=plane, in_=values)

        def quantize_w2(a):
            for u in range(2):
                chan = slice(2 * P * u, 2 * P * (u + 1))
                quantize(w2_codes[a][:, chan], w2_plane[a][:, chan], w2_bf[a][:, 2 * u : 2 * u + 2].rearrange("p t m j -> p (t m j)"))

        def round_w3(dst, n0, n1, rounder):
            rounder(
                dst.rearrange("p (c i) t -> p c t i", i=2),
                w3_raw[1][:, :, n0:n1].rearrange("p t (c i) -> p c t i", i=2),
            )

        def quantize_w3(b, n0, n1, values):
            quantize(w3_codes[b][:, n0:n1], w3_plane[b][:, n0:n1], values.rearrange("p n t -> p (n t)"))

        sweep_gains = held.tile([P, P, PACK], F32, name="sweep_gains")
        for t in range(PACK):
            nc.tensor.transpose(sweep_gains[:, :, t], gs_rows[:, t:PASS:PACK], identity[:])
        dst, src = w2_views(0)
        for u in range(2):
            nc.scalar.copy(dst[:, 0:W2_SCALAR, u], src[:, 0:W2_SCALAR, u])
            nc.vector.tensor_copy(dst[:, W2_SCALAR:P, u], src[:, W2_SCALAR:P, u])
        quantize_w2(0)
        nc.vector.tensor_copy(v1_rows[:], t1_plane[:].indirect(list1[:]))
        place_scales(0)
        load_words(t1_words[1], tab_words[1])
        place_scales(1)
        load_w1(1)
        for t in range(PACK):
            load_w3(0, t)
        load_words(w4_codes[0], w4_words[0])
        for r in range(2):
            load_scale_row(w4_plane, w4_scales, r, 4)
        load_w3(1, 0)
        for r in range(2, 4):
            load_scale_row(w4_plane, w4_scales, r, 4)
        for t in range(1, PACK):
            load_w3(1, t)
        load_words(w4_codes[1], w4_words[1])

        pool_gain = sb([P, PACK], F32, "pool_gain")
        nc.scalar.copy(pool_gain[:], sweep_gains[:, 1, :])
        nc.scalar.copy(
            gh_rows[0:2].rearrange("b (t g e) -> b t g e", t=PACK, e=RUN),
            gh_raw[:].rearrange("b (g t e) -> b t g e", t=PACK, e=RUN),
        )
        for m0 in (0, 32):
            pool_round(
                w2_bf[1][:, :, m0 : m0 + 32, :].rearrange("p t m j -> p m t j"),
                w2_raw[1][:, :, PACK * m0 : PACK * (m0 + 32)].rearrange("p j (m t) -> p m t j", t=PACK),
            )

        h2_act = [
            [sb([P, PACK, HALF], F32, "h2_act00"), sb([P, PACK, HALF], F32, "h2_act01")],
            [over([P, PACK, HALF], F32, "h2_act10", 52), over([P, PACK, HALF], F32, "h2_act11", 56)],
        ]
        h2_codes = [over([P, S], U32, "h2_codes0", 32), over([P, S], U32, "h2_codes1", 0)]
        h2_plane = [sb([P, S], U8, "h2_plane%d" % a) for a in range(2)]

        def bank_tile(name, index, shape):
            return held.tile(shape, F32, name=name, tag="bank%d" % (index % RING))

        def apply_gain(dst, act, gain):
            nc.vector.tensor_tensor(
                dst.rearrange("p (c i t) -> p c t i", i=2, t=PACK),
                act.rearrange("p t (c i) -> p c t i", i=2),
                gain.unsqueeze(1).unsqueeze(3).to_broadcast([P, act.shape[2] // 2, PACK, 2]),
                MULT,
            )

        def pool_apply_gain(dst, act, gain):
            nc.gpsimd.tensor_tensor(
                dst.rearrange("p (s t) -> p s t", t=PACK),
                act.rearrange("p t s -> p s t"),
                gain.unsqueeze(1).to_broadcast([P, act.shape[2], PACK]),
                MULT,
            )

        def sweep_unit(a, unit):
            half, u = divmod(unit, 2)
            if (a, unit) == (0, 3):
                bank = held.tile([P, 2, HALF], F32, name="sweep03", tag="spare")
            else:
                bank = bank_tile("sweep%d%d" % (a, unit), 4 * a + unit, [P, 2, HALF])
            cols = slice(HALF * half, HALF * (half + 1))
            for v in range(2):
                chan = slice(P * (2 * u + v), P * (2 * u + v + 1))
                nc.tensor.matmul_mx(
                    out=bank[:, v, :],
                    lhsT=w2_codes[a][:, chan].bitcast(FP8X4), lhsT_scale=w2_plane[a][:, chan],
                    rhs=v2_codes[:, cols].bitcast(FP4X4), rhs_scale=v2_plane[:, cols],
                    start=True, stop=True,
                )
            nc.scalar.activation(h2_act[a][half][:, 2 * u : 2 * u + 2, :], bank[:], ACT.Silu)

        for q in range(2):
            bank = bank_tile("sweep0%d" % q, q, [P, PACK, SQ])
            cols = slice(SQ * q, SQ * (q + 1))
            for t in range(PACK):
                chan = slice(P * t, P * (t + 1))
                nc.tensor.matmul_mx(
                    out=bank[:, t, :],
                    lhsT=w2_codes[0][:, chan].bitcast(FP8X4), lhsT_scale=w2_plane[0][:, chan],
                    rhs=v2_codes[:, cols].bitcast(FP4X4), rhs_scale=v2_plane[:, cols],
                    start=True, stop=True,
                )
            nc.scalar.activation(h2_act[0][0][:, :, cols], bank[:], ACT.Silu)
        for unit in range(2, 4):
            sweep_unit(0, unit)
        w1_plane = over([P, 2 * H], U8, "w1_plane", 24)
        nc.scalar.copy(
            w1_plane[:].bitcast(U32).rearrange("p (x t g w) -> p x g t w", t=PACK, g=16, w=2),
            w1_raw_plane[:].bitcast(U32).rearrange("p a (b g t w) -> p (a b) g t w", t=PACK, g=16, w=2),
        )
        w1_codes = [over([P, 2 * H], U8, "w1_codes0", 26), sb([P, 2 * H], U8, "w1_codes1")]

        def order_w1(b, word, mover):
            mover(
                w1_codes[b][:].bitcast(word).rearrange("p (a t g w) -> p a g t w", t=PACK, g=16, w=4),
                w1_raw[b][:].bitcast(word).rearrange("p a (g t w) -> p a g t w", t=PACK, w=4),
            )

        order_w1(0, U32, nc.scalar.copy)
        history_gains = held.tile([P, P, PACK], F32, name="history_gains", tag="spare")
        for t in range(PACK):
            nc.tensor.transpose(history_gains[:, :, t], gh_rows[:, P * t : P * (t + 1)], identity[:])
        h2_first = [sb([P, HALF * PACK], BF16, "h2_first0"), over([P, HALF * PACK], BF16, "h2_first1", 28)]
        for q in range(2):
            apply_gain(h2_first[0][:, PASS * q : PASS * (q + 1)], h2_act[0][0][:, :, SQ * q : SQ * (q + 1)], sweep_gains[:, 0, :])
        dst, src = w2_views(1)
        for u in range(2):
            nc.vector.tensor_copy(dst[:, P // 2 : P, u], src[:, P // 2 : P, u])
        quantize_w2(1)
        apply_gain(h2_first[1][:], h2_act[0][1][:], sweep_gains[:, 0, :])
        for unit in range(4):
            sweep_unit(1, unit)

        v1_codes = [sb([P, S], U32, "v1_codes0"), over([P, S], U32, "v1_codes1", 64)]
        nc.vector.tensor_copy(v1_codes[0][:], t1_words[0][:].indirect(list1[:]))
        for u in range(2):
            cols = slice(HALF * u, HALF * (u + 1))
            quantize(h2_codes[0][:, cols], h2_plane[0][:, cols], h2_first[u][:])
        h2_most = over([P, 3 * SQ * PACK], BF16, "h2_most", 28)
        for q in range(2):
            pool_apply_gain(h2_most[:, PASS * q : PASS * (q + 1)], h2_act[1][0][:, :, SQ * q : SQ * (q + 1)], pool_gain[:])
        apply_gain(h2_most[:, 2 * PASS : 3 * PASS], h2_act[1][1][:, :, 0:SQ], sweep_gains[:, 1, :])
        for u in range(2):
            nc.vector.tensor_copy(
                v1_codes[1][:, HALF * u : HALF * (u + 1)], t1_words[1][:].indirect(list1[:, 16 * u : 16 * (u + 1)])
            )
        pool_history = over([P, PACK], F32, "pool_history", 10)
        nc.vector.tensor_copy(pool_history[:], history_gains[:, 1, :])
        h2_last = over([P, SQ * PACK], BF16, "h2_last", 8)
        apply_gain(h2_last[:], h2_act[1][1][:, :, SQ:HALF], sweep_gains[:, 1, :])
        order_w1(1, I32, nc.vector.tensor_copy)
        quantize(h2_codes[1][:, 0 : 3 * SQ], h2_plane[1][:, 0 : 3 * SQ], h2_most[:])
        quantize(h2_codes[1][:, 3 * SQ : S], h2_plane[1][:, 3 * SQ : S], h2_last[:])

        h_act = [
            [sb([P, PACK, HALF], F32, "h_act00"), sb([P, PACK, HALF], F32, "h_act01")],
            [over([P, PACK, HALF], F32, "h_act10", 40), sb([P, PACK, HALF], F32, "h_act11")],
        ]
        h_plane = [sb([P, 2 * HALF], U8, "h_plane%d" % u) for u in range(2)]
        banks = {}

        def history_passes(unit, a):
            b, rest = divmod(unit, PACK)
            half, u = divmod(rest, 2)
            if a == 0:
                banks[unit] = bank_tile("history%d" % unit, 8 + unit, [P, 2, HALF])
            cols = slice(HALF * half, HALF * (half + 1))
            for v in range(2):
                c0 = P * (2 * u + v)
                nc.tensor.matmul_mx(
                    out=banks[unit][:, v, :],
                    lhsT=w1_codes[b][:, 2 * (PASS * a + c0) : 2 * (PASS * a + c0 + P)].bitcast(FP4X4),
                    lhsT_scale=w1_plane[:, H * a + PASS * b + c0 : H * a + PASS * b + c0 + P],
                    rhs=v1_codes[a][:, cols].bitcast(FP8X4), rhs_scale=v1_plane[a][:, cols],
                    start=(a == 0 and v == 0), stop=(a == 1 and v == 1),
                )
            if a == 1:
                nc.scalar.activation(h_act[b][half][:, 2 * u : 2 * u + 2, :], banks[unit][:], ACT.Gelu_apprx_tanh)

        for unit in range(AHEAD):
            history_passes(unit, 0)
        for unit in range(2 * PACK):
            if unit >= AHEAD:
                history_passes(unit, 0)
            history_passes(unit, 1)

        parts = [(0, HALF, 0, 2), (0, HALF, 2, 2), (HALF, SQ, 0, 4), (HALF + SQ, SQ, 0, 2), (HALF + SQ, SQ, 2, 2)]
        sums = [bank_tile("sums%d" % k, 16 + k, [P, part[3], part[1]]) for k, part in enumerate(parts)]

        def add_passes(k, weights, weight_plane, codes, plane, s0, first, final):
            width, i0, tiles = parts[k][1:]
            for i in range(tiles):
                slots = slice(P * (i0 + i), P * (i0 + i + 1))
                nc.tensor.matmul_mx(
                    out=sums[k][:, i, :],
                    lhsT=weights[:, slots].bitcast(FP8X4), lhsT_scale=weight_plane[:, slots],
                    rhs=codes[:, s0 : s0 + width].bitcast(FP8X4), rhs_scale=plane[:, s0 : s0 + width],
                    start=(first and i == 0), stop=(final and i == tiles - 1),
                )

        def sweep_sums(k, a):
            add_passes(k, w4_codes[a], w4_plane[4:P, a, :], h2_codes[a], h2_plane[a], parts[k][0], a == 0, False)

        for a in range(2):
            for k in range(len(parts)):
                sweep_sums(k, a)

        w3_first = sb([P, N, PACK], BF16, "w3_first")
        for n0 in range(0, N, 128):
            pool_round(w3_first[:, n0 : n0 + 128, :], w3_raw[0][:, :, n0 : n0 + 128].rearrange("p t n -> p n t"))

        w3_most = over([P, W3_SCALAR, PACK], BF16, "w3_most", 64)
        round_w3(w3_most[:], 0, W3_SCALAR, nc.scalar.copy)

        def history_gain(dst, b, half, s0, s1):
            apply_gain(dst, h_act[b][half][:, :, s0:s1], history_gains[:, b, :])

        h_codes = [sb([P, 2 * HALF], U32, "h_codes%d" % u) for u in range(2)]
        h_first = over([P, S * PACK], BF16, "h_first", 12)
        h_third = sb([P, HALF * PACK], BF16, "h_third")
        history_gain(h_first[:, 0 : 2 * PASS], 0, 0, 0, HALF)
        history_gain(h_third[:], 0, 1, 0, HALF)
        history_gain(h_first[:, 2 * PASS : 4 * PASS], 1, 0, 0, HALF)
        quantize(h_codes[0][:], h_plane[0][:], h_first[:])
        w3_codes = [over([P, N], U32, "w3_codes0", 40), sb([P, N], U32, "w3_codes1")]
        quantize_w3(0, 0, N, w3_first[:])
        w3_rest = over([P, N - W3_SCALAR, PACK], BF16, "w3_rest", 12)
        for n0 in range(W3_SCALAR, N, P):
            round_w3(w3_rest[:, n0 - W3_SCALAR : n0 - W3_SCALAR + P], n0, n0 + P, nc.vector.tensor_copy)
        quantize_w3(1, 0, W3_SCALAR, w3_most[:])
        for n0 in range(W3_SCALAR, N, P):
            quantize_w3(1, n0, n0 + P, w3_rest[:, n0 - W3_SCALAR : n0 - W3_SCALAR + P])
        quantize(h_codes[1][:, 0:HALF], h_plane[1][:, 0:HALF], h_third[:])
        h_last = [over([P, PASS], BF16, "h_last0", 16), over([P, PASS], BF16, "h_last1", 64)]
        own = SQ - POOL_QUERIES
        history_gain(h_last[0][:], 1, 1, 0, SQ)
        history_gain(h_last[1][:, 0 : PACK * own], 1, 1, SQ, SQ + own)
        pool_apply_gain(h_last[1][:, PACK * own : PASS], h_act[1][1][:, :, SQ + own : HALF], pool_history[:])
        for q in range(2):
            cols = slice(HALF + SQ * q, HALF + SQ * (q + 1))
            quantize(h_codes[1][:, cols], h_plane[1][:, cols], h_last[q][:])

        def history_sums(k, b):
            half, s0 = divmod(parts[k][0], HALF)
            add_passes(k, w3_codes[b], w3_plane[b], h_codes[half], h_plane[half], HALF * b + s0, False, b == 1)

        out_rows = out.rearrange("(i p) s -> p i s", p=P)
        for k, (s0, width, i0, tiles) in enumerate(parts):
            if k in (0, 2):
                for later in range(k, 2 if k == 0 else len(parts)):
                    history_sums(later, 0)
            history_sums(k, 1)
            prob = sb([P, tiles, width], F32, "prob%d" % k)
            nc.scalar.activation(prob[:], sums[k][:], ACT.Sigmoid)
            queue = nc.scalar if k == len(parts) - 1 else nc.sync
            queue.dma_start(out=out_rows[:, i0 : i0 + tiles, s0 : s0 + width], in_=prob[:])
